import numpy as np
import ml_dtypes


def mxq(x, axis, fmt="e4m3"):
    dtype, down = {"e4m3": (ml_dtypes.float8_e4m3fn, 7), "e5m2": (ml_dtypes.float8_e5m2, 14)}[fmt]
    v = np.moveaxis(np.asarray(x, np.float32).astype(ml_dtypes.bfloat16).astype(np.float64), axis, -1)
    blocks = v.reshape(v.shape[:-1] + (-1, 32))
    amax = np.abs(blocks).max(-1, keepdims=True)
    byte = np.maximum(np.where(amax > 0, np.frexp(amax)[1] - 1 + 127, 0) - down, 1)
    scale = np.exp2(byte - 127.0)
    codes = (blocks / scale).astype(np.float32).astype(dtype).astype(np.float64)
    return np.moveaxis((codes * scale).reshape(v.shape), -1, axis)


WIDE = False


def mx_kscale(k):
    if not WIDE:
        return np.ones(k)
    levels = np.array([30, -30])
    if k % 512:
        return np.exp2(np.random.permutation(np.resize(levels, k // 32))).repeat(32)
    a = np.empty((k // 512, 16))
    for p in range(k // 512):
        a[p, :8] = np.random.permutation(np.resize(levels, 8))
        for g in range(8):
            far = levels[np.abs(levels - a[p, g]) >= 10]
            a[p, g + 8] = far[np.random.randint(len(far))]
    return np.exp2(a.ravel()).repeat(32)


def f64(x):
    return np.asarray(x).astype(np.float64)


def striped(idx):
    return np.tile(idx.reshape(-1, 16).T, (8, 1)).astype(np.uint16)


def unstriped(offs):
    return offs[:16].T.reshape(-1).astype(np.int64)


E2M1 = np.array([0.0, 0.5, 1.0, 1.5, 2.0, 3.0, 4.0, 6.0, -0.0, -0.5, -1.0, -1.5, -2.0, -3.0, -4.0, -6.0])


def pack_weight(w, fmt):
    k, n = w.shape
    w = f64(np.asarray(w, np.float32).astype(ml_dtypes.bfloat16)).reshape(k // 32, 32, n)
    amax = np.abs(w).max(1)
    if fmt == "e4m3":
        byte = np.frexp(amax)[1] - 1 + 127 - 7
    else:
        mant, ex = np.frexp(amax / 6.0)
        byte = np.where(mant > 0.5, ex, ex - 1) + 127
    byte = np.clip(np.where(amax > 0, byte, 1), 1, 254)
    scaled = (w * np.exp2(127.0 - byte)[:, None, :]).reshape(k, n).astype(np.float32)
    by_word = np.ascontiguousarray(scaled.reshape(k // 512, 128, 4, n).transpose(0, 1, 3, 2))
    if fmt == "e4m3":
        words = by_word.astype(ml_dtypes.float8_e4m3fn).view(np.uint8)
    else:
        c = by_word.astype(ml_dtypes.float4_e2m1fn).view(np.uint8) & 0xF
        words = (c[..., 0::2] | (c[..., 1::2] << 4)).reshape(k // 512, 128, 2 * n)
    return np.ascontiguousarray(words), np.ascontiguousarray(byte.astype(np.uint8).reshape(k // 512, 16, n))


def unpack_weight(words, scales, fmt):
    g, _, n = scales.shape
    words = np.ascontiguousarray(words).reshape(g, 128, n, -1)
    if fmt == "e4m3":
        vals = words.view(ml_dtypes.float8_e4m3fn).astype(np.float64)
    else:
        nib = np.empty((g, 128, n, 4), np.uint8)
        nib[..., 0::2] = words & 0xF
        nib[..., 1::2] = words >> 4
        vals = E2M1[nib]
    vals = vals * np.repeat(np.exp2(scales.astype(np.float64) - 127.0), 8, axis=1)[..., None]
    return vals.transpose(0, 1, 3, 2).reshape(g * 512, n)


def planes(y):
    n, m = y.shape
    v = y.astype(np.float32).astype(ml_dtypes.bfloat16).astype(np.float64).reshape(n // 32, 32, m)
    top = np.abs(v).max(1)
    byte = np.clip(np.where(top > 0, np.frexp(top)[1] - 1 + 127 - 7, 1), 1, 254)
    codes = (v * np.exp2(127.0 - byte)[:, None, :]).reshape(n, m).astype(np.float32).astype(ml_dtypes.float8_e4m3fn).view(np.uint8)
    words = codes.reshape(n // 512, 128, 4, m).transpose(0, 1, 3, 2)
    return np.ascontiguousarray(words), np.ascontiguousarray(byte.astype(np.uint8).reshape(n // 512, 16, m))


K, N, T, J = 1024, 512, 2048, 1024


def setup_inputs():
    n = np.random.standard_normal
    s = mx_kscale(K)[:, None]
    m = np.exp(0.5 * n((1, J)))
    p_w4 = pack_weight(n((K, N)) / np.sqrt(K) / s, "e2m1")
    return {
        "dy": (m * n((K, J)) * s).astype(np.float32),
        "w4_words": p_w4[0],
        "w4_scales": p_w4[1],
        "wd": (0.4 * (n((K, N)) / np.sqrt(K) / s)).astype(np.float32),
        "d": (0.5 + 0.3 * n((N, J))).astype(np.float32),
        "wgo": np.tile(np.random.uniform(0.5, 2.0, J), (128, 1)).astype(np.float32),
        "offs": striped(np.random.permutation(T)[:J]),
    }


def reference(dy, w4_words, w4_scales, wd, d, wgo, offs):
    idx = unstriped(offs)
    dy_ = mxq(f64(dy), 0, "e5m2")
    w4_ = unpack_weight(w4_words, w4_scales, "e2m1")
    wd_ = mxq(f64(wd), 0, "e4m3")
    dx = w4_.T @ dy_ + wd_.T @ dy_
    out = np.zeros((N, T))
    out[:, idx] = f64(wgo)[0] * (dx * f64(d))
    return (out,) + planes(out)

@@ -1,0 +1,259 @@
+from contextlib import ExitStack
+
+import concourse.mybir as mybir
+from concourse.masks import make_identity
+
+K, N, T, J = 1024, 512, 2048, 1024
+FLOPS = 2 * 2 * K * N * J
+
+F32 = mybir.dt.float32
+BF16 = mybir.dt.bfloat16
+I32 = mybir.dt.int32
+U32 = mybir.dt.uint32
+U16 = mybir.dt.uint16
+U8 = mybir.dt.uint8
+E4M3 = mybir.dt.float8_e4m3fn_x4
+E5M2 = mybir.dt.float8_e5m2_x4
+E2M1 = mybir.dt.float4_e2m1fn_x4
+MULT = mybir.AluOpType.mult
+COPY = mybir.ActivationFunctionType.Copy
+
+P = 128
+PACK = 4
+K_PASS = P * PACK
+PASSES = K // K_PASS
+CHUNK = 256
+CHUNKS = J // CHUNK
+BLOCKS = CHUNK // P
+OUT_CHUNK = 512
+OUT_CHUNKS = T // OUT_CHUNK
+QUADS = 4
+QUAD = 32
+
+
+def interleave(copy, grouped, rows):
+    copy(
+        out=grouped.rearrange("p (c f) i -> p c i f", f=4),
+        in_=rows.rearrange("p i (c f) -> p c i f", f=4),
+    )
+
+
+def flat(grouped):
+    return grouped.rearrange("p c i -> p (c i)")
+
+
+def tile_list_embg_dl_mulP_kernel(tc, dy, w4_words, w4_scales, wd, d, wgo, offs, out_0, out_1, out_2):
+    nc = tc.nc
+    on_vector = nc.vector.tensor_copy
+    on_scalar = nc.scalar.copy
+    with ExitStack() as ctx:
+        keep = ctx.enter_context(tc.tile_pool(name="keep", bufs=1))
+        psum = ctx.enter_context(tc.psum_pool(name="psum", bufs=1))
+
+        offsets = keep.tile([P, J // 16], U16, name="offsets")
+        w4_codes = keep.tile([P, PASSES, 2 * N], U8, name="w4_codes", align_bytes=64)
+        w4_plane = keep.tile([P, PASSES, N], U8, name="w4_plane", align_bytes=64)
+        wgo_rows = keep.tile([P, P], F32, name="wgo_rows")
+        wgo_cols = keep.tile([P, J // P], F32, name="wgo_cols")
+        ident = keep.tile([P, P], F32, name="ident")
+        wd_raw = [keep.tile([P, PACK, N], F32, name=f"wd_raw{a}") for a in range(PASSES)]
+        wd_grouped = [keep.tile([P, N, PACK], BF16, name=f"wd_grouped{a}", align_bytes=64) for a in range(PASSES)]
+        wd_codes = [keep.tile([P, N], U32, name=f"wd_codes{a}", align_bytes=64) for a in range(PASSES)]
+        wd_plane = [keep.tile([P, N], U8, name=f"wd_plane{a}", align_bytes=64) for a in range(PASSES)]
+        dy_raw = [[keep.tile([P, PACK, CHUNK], F32, name=f"dy_raw{c}_{a}") for a in range(PASSES)] for c in range(CHUNKS)]
+        dy_grouped = [[keep.tile([P, CHUNK, PACK], BF16, name=f"dy_grouped{c}_{a}", align_bytes=64) for a in range(PASSES)] for c in range(CHUNKS)]
+        dy_codes = [[keep.tile([P, CHUNK], U32, name=f"dy_codes{c}_{a}", align_bytes=64) for a in range(PASSES)] for c in range(CHUNKS)]
+        dy_plane = [[keep.tile([P, CHUNK], U8, name=f"dy_plane{c}_{a}", align_bytes=64) for a in range(PASSES)] for c in range(CHUNKS)]
+        d_early = [keep.tile([P, PACK, CHUNK], F32, name=f"d_early{c}") for c in range(2)]
+        d_late = keep.tile([P, PACK, 2 * CHUNK], F32, name="d_late")
+        by_token = [keep.tile([P, PACK, P], F32, name=f"by_token{b}") for b in range(J // P)]
+        by_row = [keep.tile([P, J], F32, name=f"by_row{t}") for t in range(PACK)]
+        window = [keep.tile([P, T], F32, name=f"window{t}") for t in range(PACK)]
+        rounded = [keep.tile([P, PACK, OUT_CHUNK], BF16, name=f"rounded{c}") for c in range(OUT_CHUNKS)]
+        out_grouped = [keep.tile([P, OUT_CHUNK, PACK], BF16, name=f"out_grouped{c}", align_bytes=64) for c in range(OUT_CHUNKS)]
+        out_codes = [keep.tile([P, OUT_CHUNK], U32, name=f"out_codes{c}", align_bytes=64) for c in range(OUT_CHUNKS)]
+        out_plane = keep.tile([P, OUT_CHUNK], U8, name="out_plane", align_bytes=64)
+
+        dy_rows = dy.rearrange("(a p i) j -> a p i j", a=PASSES, i=PACK)
+        wd_rows = wd.rearrange("(a p i) n -> a p i n", a=PASSES, i=PACK)
+        d_rows = d.rearrange("(p t) j -> p t j", t=PACK)
+        out_rows = out_0.rearrange("(p t) c -> p t c", t=PACK)
+
+        def cols(c, width=CHUNK):
+            return slice(c * width, (c + 1) * width)
+
+        def load_dy(c, a):
+            nc.sync.dma_start(out=dy_raw[c][a][:], in_=dy_rows[a][:, :, cols(c)])
+
+        nc.vector.memset(w4_plane[:].rearrange("p a n -> p (a n)").bitcast(I32), 0)
+        nc.gpsimd.memset(wgo_rows[:], 0.0)
+        make_identity(nc, ident[:])
+        for t in range(PACK):
+            nc.vector.memset(window[t][:].bitcast(I32), 0)
+
+        nc.sync.dma_start(out=wd_raw[0][:], in_=wd_rows[0])
+        for q in range(QUADS):
+            nc.sync.dma_start(
+                out=w4_plane[QUAD * q : QUAD * q + 4].bitcast(I32),
+                in_=w4_scales[:, 4 * q : 4 * q + 4, :].rearrange("a r n -> r a n").bitcast(I32),
+            )
+        nc.sync.dma_start(out=wgo_rows[0 : J // P, :], in_=wgo[0:1, :].rearrange("o (b m) -> (o b) m", m=P))
+        load_dy(0, 0)
+        nc.sync.dma_start(out=w4_codes[:].bitcast(I32), in_=w4_words.rearrange("a p c -> p a c").bitcast(I32))
+        nc.sync.dma_start(out=wd_raw[1][:], in_=wd_rows[1])
+        load_dy(0, 1)
+        load_dy(1, 0)
+        load_dy(1, 1)
+        nc.sync.dma_start(offsets[:], offs)
+        nc.sync.dma_start(out=d_early[0][:], in_=d_rows[:, :, cols(0)])
+        load_dy(2, 0)
+        load_dy(2, 1)
+        nc.sync.dma_start(out=d_early[1][:], in_=d_rows[:, :, cols(1)])
+        load_dy(3, 0)
+        load_dy(3, 1)
+        nc.sync.dma_start(out=d_late[:], in_=d_rows[:, :, cols(1, 2 * CHUNK)])
+
+        def group_wd(a, split):
+            interleave(on_scalar, wd_grouped[a][:, :split, :], wd_raw[a][:, :, :split])
+            interleave(on_vector, wd_grouped[a][:, split:, :], wd_raw[a][:, :, split:])
+
+        def quantize_wd(a):
+            nc.vector.quantize_mx(out=wd_codes[a][:].bitcast(E4M3), scales=wd_plane[a][:], in_=flat(wd_grouped[a][:]))
+
+        def group_dy(copy, c, a, part=slice(0, CHUNK)):
+            interleave(copy, dy_grouped[c][a][:, part, :], dy_raw[c][a][:, :, part])
+
+        def quantize_dy(c, a, part=slice(0, CHUNK)):
+            nc.vector.quantize_mx(
+                out=dy_codes[c][a][:, part].bitcast(E5M2), scales=dy_plane[c][a][:, part], in_=flat(dy_grouped[c][a][:, part, :])
+            )
+
+        def passes(bank, c, b, a):
+            tokens = cols(b, P)
+            lhs = dict(lhsT=dy_codes[c][a][:, tokens].bitcast(E5M2), lhsT_scale=dy_plane[c][a][:, tokens])
+            nc.tensor.matmul_mx(
+                out=bank[:], rhs=w4_codes[:, a, :].bitcast(E2M1), rhs_scale=w4_plane[:, a, :], start=(a == 0), stop=False, **lhs
+            )
+            nc.tensor.matmul_mx(
+                out=bank[:], rhs=wd_codes[a][:].bitcast(E4M3), rhs_scale=wd_plane[a][:], start=False, stop=(a == PASSES - 1), **lhs
+            )
+
+        def multiply(c):
+            banks = [psum.tile([P, N], F32, name=f"sums{c}_{b}", tag=f"bank{(4 * c + 1 - b) % 8}") for b in range(BLOCKS)]
+            for a in range(PASSES):
+                for b in range(BLOCKS):
+                    passes(banks[b], c, b, a)
+            return banks
+
+        def weigh(c, banks, vector_blocks=()):
+            for b in range(BLOCKS):
+                block = BLOCKS * c + b
+                dealt = banks[b][:].rearrange("j (m t) -> j t m", t=PACK)
+                weight = wgo_cols[:, block : block + 1]
+                if b in vector_blocks:
+                    nc.vector.tensor_scalar(out=by_token[block][:], in0=dealt, scalar1=weight, scalar2=None, op0=MULT)
+                else:
+                    nc.scalar.activation(out=by_token[block][:], in_=dealt, func=COPY, scale=weight)
+
+        def turn(c, t):
+            bank = psum.tile([P, CHUNK], F32, name=f"turned{c}_{t}", tag=f"bank{(4 * c + 2 + t) % 8}")
+            for b in range(BLOCKS):
+                nc.tensor.transpose(bank[:, cols(b, P)], by_token[BLOCKS * c + b][:, t, :], ident[:])
+            nc.scalar.copy(out=by_row[t][:, cols(c)], in_=bank[:])
+
+        def scatter(t, first, count, d_part):
+            lo, hi = first * CHUNK, (first + count) * CHUNK
+            nc.vector.tensor_tensor(window[t][:].indirect(offsets[:, lo // 16 : hi // 16]), by_row[t][:, lo:hi], d_part, MULT)
+
+        def round_plane(copy, t, c):
+            copy(out=rounded[c][:, t, :], in_=window[t][:, cols(c, OUT_CHUNK)])
+
+        def finish(t):
+            nc.sync.dma_start(out=out_rows[:, t, :], in_=window[t][:])
+            if t < PACK - 1:
+                for c in range(OUT_CHUNKS):
+                    round_plane(on_scalar, t, c)
+
+        wgo_bank = psum.tile([P, P], F32, name="wgo_bank", tag="bank7")
+
+        nc.tensor.transpose(wgo_bank[:], wgo_rows[:], ident[:])
+        nc.scalar.copy(out=wgo_cols[:], in_=wgo_bank[:, 0 : J // P])
+        group_wd(0, 256)
+        quantize_wd(0)
+        group_dy(on_scalar, 0, 0)
+        quantize_dy(0, 0)
+        group_wd(1, 176)
+        quantize_wd(1)
+        group_dy(on_vector, 0, 1, cols(0, P))
+        group_dy(on_scalar, 0, 1, cols(1, P))
+        quantize_dy(0, 1, cols(0, P))
+        quantize_dy(0, 1, cols(1, P))
+        banks = multiply(0)
+        group_dy(on_vector, 1, 0)
+        quantize_dy(1, 0)
+        weigh(0, banks, vector_blocks=(1,))
+        group_dy(on_vector, 1, 1)
+        quantize_dy(1, 1)
+        for t in range(PACK):
+            turn(0, t)
+        banks = multiply(1)
+        for t in range(PACK):
+            scatter(t, 0, 1, d_early[0][:, t, :])
+        for a in range(PASSES):
+            group_dy(on_scalar, 2, a)
+        weigh(1, banks)
+        for t in range(PACK):
+            turn(1, t)
+        for a in range(PASSES):
+            quantize_dy(2, a)
+        banks = multiply(2)
+        for a in range(PASSES):
+            group_dy(on_scalar, 3, a)
+        for t in range(2):
+            scatter(t, 1, 1, d_early[1][:, t, :])
+        for a in range(PASSES):
+            quantize_dy(3, a)
+        for t in range(2, PACK):
+            scatter(t, 1, 1, d_early[1][:, t, :])
+        weigh(2, banks)
+        for t in range(PACK):
+            turn(2, t)
+        banks = multiply(3)
+        weigh(3, banks)
+        for t in range(PACK):
+            turn(3, t)
+        for t in range(PACK - 1):
+            scatter(t, 2, 1, d_late[:, t, cols(0)])
+        for t in range(PACK - 1):
+            scatter(t, 3, 1, d_late[:, t, cols(1)])
+            finish(t)
+        scatter(PACK - 1, 2, 2, d_late[:, PACK - 1, :])
+        finish(PACK - 1)
+
+        def group_out(copy, c):
+            interleave(copy, out_grouped[c][:], rounded[c][:])
+
+        def quantize_out(c):
+            nc.vector.quantize_mx(out=out_codes[c][:].bitcast(E4M3), scales=out_plane[4 * c :, :], in_=flat(out_grouped[c][:]))
+            nc.sync.dma_start(
+                out=out_1[0][:, cols(c, OUT_CHUNK), :].rearrange("p c i -> p (c i)").bitcast(I32), in_=out_codes[c][:].bitcast(I32)
+            )
+
+        last = PACK - 1
+        round_plane(on_scalar, last, 1)
+        round_plane(on_vector, last, 0)
+        round_plane(on_vector, last, 3)
+        group_out(on_scalar, 1)
+        group_out(on_vector, 0)
+        round_plane(on_vector, last, 2)
+        group_out(on_scalar, 3)
+        quantize_out(0)
+        group_out(on_vector, 2)
+        quantize_out(1)
+        quantize_out(2)
+        quantize_out(3)
+        for q in range(QUADS):
+            nc.scalar.dma_start(
+                out=out_2[0][4 * q : 4 * q + 4, :].rearrange("r (c n) -> c r n", c=OUT_CHUNKS).bitcast(I32),
+                in_=out_plane[QUAD * q : QUAD * q + 4 * OUT_CHUNKS, :].bitcast(I32),
+            )

@@ -27,6 +27,7 @@ CHUNKS = J // CHUNK
 BLOCKS = CHUNK // P
 OUT_CHUNK = 512
 OUT_CHUNKS = T // OUT_CHUNK
+HALF = N // 2
 QUADS = 4
 QUAD = 32
 
@@ -56,19 +57,21 @@ def tile_list_embg_dl_mulP_kernel(tc, dy, w4_words, w4_scales, wd, d, wgo, offs,
         wgo_rows = keep.tile([P, P], F32, name="wgo_rows")
         wgo_cols = keep.tile([P, J // P], F32, name="wgo_cols")
         ident = keep.tile([P, P], F32, name="ident")
-        wd_raw = [keep.tile([P, PACK, N], F32, name=f"wd_raw{a}") for a in range(PASSES)]
+        wd_first = keep.tile([P, PACK, N], F32, name="wd_first")
+        wd_second = [keep.tile([P, PACK, HALF], F32, name=f"wd_second{h}") for h in range(2)]
         wd_grouped = [keep.tile([P, N, PACK], BF16, name=f"wd_grouped{a}", align_bytes=64) for a in range(PASSES)]
         wd_codes = [keep.tile([P, N], U32, name=f"wd_codes{a}", align_bytes=64) for a in range(PASSES)]
         wd_plane = [keep.tile([P, N], U8, name=f"wd_plane{a}", align_bytes=64) for a in range(PASSES)]
         dy_raw = [[keep.tile([P, PACK, CHUNK], F32, name=f"dy_raw{c}_{a}") for a in range(PASSES)] for c in range(CHUNKS)]
         dy_grouped = [[keep.tile([P, CHUNK, PACK], BF16, name=f"dy_grouped{c}_{a}", align_bytes=64) for a in range(PASSES)] for c in range(CHUNKS)]
+        last_half = [keep.tile([P, P, PACK], BF16, name=f"last_half{b}", tag=f"window{2 + b}", align_bytes=64) for b in range(BLOCKS)]
         dy_codes = [[keep.tile([P, CHUNK], U32, name=f"dy_codes{c}_{a}", align_bytes=64) for a in range(PASSES)] for c in range(CHUNKS)]
         dy_plane = [[keep.tile([P, CHUNK], U8, name=f"dy_plane{c}_{a}", align_bytes=64) for a in range(PASSES)] for c in range(CHUNKS)]
         d_early = [keep.tile([P, PACK, CHUNK], F32, name=f"d_early{c}") for c in range(2)]
         d_late = keep.tile([P, PACK, 2 * CHUNK], F32, name="d_late")
         by_token = [keep.tile([P, PACK, P], F32, name=f"by_token{b}") for b in range(J // P)]
         by_row = [keep.tile([P, J], F32, name=f"by_row{t}") for t in range(PACK)]
-        window = [keep.tile([P, T], F32, name=f"window{t}") for t in range(PACK)]
+        window = [keep.tile([P, T], F32, name=f"window{t}") for t in range(2)]
         rounded = [keep.tile([P, PACK, OUT_CHUNK], BF16, name=f"rounded{c}") for c in range(OUT_CHUNKS)]
         out_grouped = [keep.tile([P, OUT_CHUNK, PACK], BF16, name=f"out_grouped{c}", align_bytes=64) for c in range(OUT_CHUNKS)]
         out_codes = [keep.tile([P, OUT_CHUNK], U32, name=f"out_codes{c}", align_bytes=64) for c in range(OUT_CHUNKS)]
@@ -85,24 +88,25 @@ def tile_list_embg_dl_mulP_kernel(tc, dy, w4_words, w4_scales, wd, d, wgo, offs,
         def load_dy(c, a):
             nc.sync.dma_start(out=dy_raw[c][a][:], in_=dy_rows[a][:, :, cols(c)])
 
-        nc.vector.memset(w4_plane[:].rearrange("p a n -> p (a n)").bitcast(I32), 0)
+        nc.gpsimd.memset(w4_plane[:].rearrange("p a n -> p (a n)").bitcast(I32), 0)
         nc.gpsimd.memset(wgo_rows[:], 0.0)
         make_identity(nc, ident[:])
-        for t in range(PACK):
-            nc.vector.memset(window[t][:].bitcast(I32), 0)
+        for t in range(2):
+            nc.vector.memset(window[t][:], 0.0)
 
-        nc.sync.dma_start(out=wd_raw[0][:], in_=wd_rows[0])
+        nc.sync.dma_start(out=wd_first[:], in_=wd_rows[0])
+        load_dy(0, 0)
+        nc.sync.dma_start(out=w4_codes[:].bitcast(I32), in_=w4_words.rearrange("a p c -> p a c").bitcast(I32))
         for q in range(QUADS):
             nc.sync.dma_start(
                 out=w4_plane[QUAD * q : QUAD * q + 4].bitcast(I32),
                 in_=w4_scales[:, 4 * q : 4 * q + 4, :].rearrange("a r n -> r a n").bitcast(I32),
             )
-        nc.sync.dma_start(out=wgo_rows[0 : J // P, :], in_=wgo[0:1, :].rearrange("o (b m) -> (o b) m", m=P))
-        load_dy(0, 0)
-        nc.sync.dma_start(out=w4_codes[:].bitcast(I32), in_=w4_words.rearrange("a p c -> p a c").bitcast(I32))
-        nc.sync.dma_start(out=wd_raw[1][:], in_=wd_rows[1])
         load_dy(0, 1)
+        for h in range(2):
+            nc.sync.dma_start(out=wd_second[h][:], in_=wd_rows[1][:, :, cols(h, HALF)])
         load_dy(1, 0)
+        nc.sync.dma_start(out=wgo_rows[0 : J // P, :], in_=wgo[0:1, :].rearrange("o (b m) -> (o b) m", m=P))
         load_dy(1, 1)
         nc.sync.dma_start(offsets[:], offs)
         nc.sync.dma_start(out=d_early[0][:], in_=d_rows[:, :, cols(0)])
@@ -113,12 +117,12 @@ def tile_list_embg_dl_mulP_kernel(tc, dy, w4_words, w4_scales, wd, d, wgo, offs,
         load_dy(3, 1)
         nc.sync.dma_start(out=d_late[:], in_=d_rows[:, :, cols(1, 2 * CHUNK)])
 
-        def group_wd(a, split):
-            interleave(on_scalar, wd_grouped[a][:, :split, :], wd_raw[a][:, :, :split])
-            interleave(on_vector, wd_grouped[a][:, split:, :], wd_raw[a][:, :, split:])
+        def group_wd(grouped, raw, split):
+            interleave(on_scalar, grouped[:, :split, :], raw[:, :, :split])
+            interleave(on_vector, grouped[:, split:, :], raw[:, :, split:])
 
-        def quantize_wd(a):
-            nc.vector.quantize_mx(out=wd_codes[a][:].bitcast(E4M3), scales=wd_plane[a][:], in_=flat(wd_grouped[a][:]))
+        def quantize_wd(a, part):
+            nc.vector.quantize_mx(out=wd_codes[a][:, part].bitcast(E4M3), scales=wd_plane[a][:, part], in_=flat(wd_grouped[a][:, part, :]))
 
         def group_dy(copy, c, a, part=slice(0, CHUNK)):
             interleave(copy, dy_grouped[c][a][:, part, :], dy_raw[c][a][:, :, part])
@@ -128,22 +132,26 @@ def tile_list_embg_dl_mulP_kernel(tc, dy, w4_words, w4_scales, wd, d, wgo, offs,
                 out=dy_codes[c][a][:, part].bitcast(E5M2), scales=dy_plane[c][a][:, part], in_=flat(dy_grouped[c][a][:, part, :])
             )
 
-        def passes(bank, c, b, a):
-            tokens = cols(b, P)
-            lhs = dict(lhsT=dy_codes[c][a][:, tokens].bitcast(E5M2), lhsT_scale=dy_plane[c][a][:, tokens])
-            nc.tensor.matmul_mx(
-                out=bank[:], rhs=w4_codes[:, a, :].bitcast(E2M1), rhs_scale=w4_plane[:, a, :], start=(a == 0), stop=False, **lhs
-            )
-            nc.tensor.matmul_mx(
-                out=bank[:], rhs=wd_codes[a][:].bitcast(E4M3), rhs_scale=wd_plane[a][:], start=False, stop=(a == PASSES - 1), **lhs
-            )
-
-        def multiply(c):
+        def multiply(c, order):
             banks = [psum.tile([P, N], F32, name=f"sums{c}_{b}", tag=f"bank{(4 * c + 1 - b) % 8}") for b in range(BLOCKS)]
-            for a in range(PASSES):
+            for step, (codes, plane, a) in enumerate(order):
                 for b in range(BLOCKS):
-                    passes(banks[b], c, b, a)
+                    tokens = cols(b, P)
+                    nc.tensor.matmul_mx(
+                        out=banks[b][:],
+                        lhsT=dy_codes[c][a][:, tokens].bitcast(E5M2),
+                        lhsT_scale=dy_plane[c][a][:, tokens],
+                        rhs=codes,
+                        rhs_scale=plane,
+                        start=(step == 0),
+                        stop=(step == len(order) - 1),
+                    )
             return banks
+
+        w4_pass = [(w4_codes[:, a, :].bitcast(E2M1), w4_plane[:, a, :], a) for a in range(PASSES)]
+        wd_pass = [(wd_codes[a][:].bitcast(E4M3), wd_plane[a][:], a) for a in range(PASSES)]
+        base_first = [wd_pass[0], w4_pass[0], w4_pass[1], wd_pass[1]]
+        pass_by_pass = [w4_pass[0], wd_pass[0], w4_pass[1], wd_pass[1]]
 
         def weigh(c, banks, vector_blocks=()):
             for b in range(BLOCKS):
@@ -176,27 +184,36 @@ def tile_list_embg_dl_mulP_kernel(tc, dy, w4_words, w4_scales, wd, d, wgo, offs,
 
         wgo_bank = psum.tile([P, P], F32, name="wgo_bank", tag="bank7")
 
+        group_wd(wd_grouped[0][:], wd_first[:], 256)
+        quantize_wd(0, slice(0, N))
+        group_dy(on_scalar, 0, 0, cols(1, P))
+        group_dy(on_vector, 0, 0, cols(0, P))
+        group_dy(on_scalar, 0, 1)
+        quantize_dy(0, 0)
+        quantize_dy(0, 1)
+        interleave(on_scalar, wd_grouped[1][:, cols(0, HALF), :], wd_second[0][:])
+        quantize_wd(1, cols(0, HALF))
+        group_wd(wd_grouped[1][:, cols(1, HALF), :], wd_second[1][:], 96)
+        quantize_wd(1, cols(1, HALF))
+        group_dy(on_scalar, 1, 0, cols(1, P))
+        group_dy(on_vector, 1, 0, cols(0, P))
         nc.tensor.transpose(wgo_bank[:], wgo_rows[:], ident[:])
         nc.scalar.copy(out=wgo_cols[:], in_=wgo_bank[:, 0 : J // P])
-        group_wd(0, 256)
-        quantize_wd(0)
-        group_dy(on_scalar, 0, 0)
-        quantize_dy(0, 0)
-        group_wd(1, 176)
-        quantize_wd(1)
-        group_dy(on_vector, 0, 1, cols(0, P))
-        group_dy(on_scalar, 0, 1, cols(1, P))
-        quantize_dy(0, 1, cols(0, P))
-        quantize_dy(0, 1, cols(1, P))
-        banks = multiply(0)
-        group_dy(on_vector, 1, 0)
-        quantize_dy(1, 0)
+        banks = multiply(0, base_first)
         weigh(0, banks, vector_blocks=(1,))
-        group_dy(on_vector, 1, 1)
-        quantize_dy(1, 1)
+        for b, copy in enumerate((on_vector, on_scalar)):
+            interleave(copy, last_half[b][:], dy_raw[1][1][:, :, cols(b, P)])
+        quantize_dy(1, 0)
+        for b in range(BLOCKS):
+            nc.vector.quantize_mx(
+                out=dy_codes[1][1][:, cols(b, P)].bitcast(E5M2), scales=dy_plane[1][1][:, cols(b, P)], in_=flat(last_half[b][:])
+            )
+        for t in range(2, PACK):
+            window.append(keep.tile([P, T], F32, name=f"window{t}", tag=f"window{t}", align_bytes=64))
+            nc.gpsimd.memset(window[t][:], 0.0)
         for t in range(PACK):
             turn(0, t)
-        banks = multiply(1)
+        banks = multiply(1, pass_by_pass)
         for t in range(PACK):
             scatter(t, 0, 1, d_early[0][:, t, :])
         for a in range(PASSES):
@@ -206,7 +223,7 @@ def tile_list_embg_dl_mulP_kernel(tc, dy, w4_words, w4_scales, wd, d, wgo, offs,
             turn(1, t)
         for a in range(PASSES):
             quantize_dy(2, a)
-        banks = multiply(2)
+        banks = multiply(2, pass_by_pass)
         for a in range(PASSES):
             group_dy(on_scalar, 3, a)
         for t in range(2):
@@ -218,7 +235,7 @@ def tile_list_embg_dl_mulP_kernel(tc, dy, w4_words, w4_scales, wd, d, wgo, offs,
         weigh(2, banks)
         for t in range(PACK):
             turn(2, t)
-        banks = multiply(3)
+        banks = multiply(3, pass_by_pass)
         weigh(3, banks)
         for t in range(PACK):
             turn(3, t)
@@ -230,30 +247,37 @@ def tile_list_embg_dl_mulP_kernel(tc, dy, w4_words, w4_scales, wd, d, wgo, offs,
         scatter(PACK - 1, 2, 2, d_late[:, PACK - 1, :])
         finish(PACK - 1)
 
-        def group_out(copy, c):
-            interleave(copy, out_grouped[c][:], rounded[c][:])
+        def group_out(copy, c, part=slice(0, OUT_CHUNK)):
+            interleave(copy, out_grouped[c][:, part, :], rounded[c][:, :, part])
 
-        def quantize_out(c):
-            nc.vector.quantize_mx(out=out_codes[c][:].bitcast(E4M3), scales=out_plane[4 * c :, :], in_=flat(out_grouped[c][:]))
+        def quantize_out(c, part=slice(0, OUT_CHUNK)):
+            nc.vector.quantize_mx(
+                out=out_codes[c][:, part].bitcast(E4M3), scales=out_plane[4 * c :, part], in_=flat(out_grouped[c][:, part, :])
+            )
             nc.sync.dma_start(
-                out=out_1[0][:, cols(c, OUT_CHUNK), :].rearrange("p c i -> p (c i)").bitcast(I32), in_=out_codes[c][:].bitcast(I32)
+                out=out_1[0][:, cols(c, OUT_CHUNK), :][:, part, :].rearrange("p c i -> p (c i)").bitcast(I32),
+                in_=out_codes[c][:, part].bitcast(I32),
             )
 
         last = PACK - 1
+        halves = [cols(h, OUT_CHUNK // 2) for h in range(2)]
         round_plane(on_scalar, last, 1)
         round_plane(on_vector, last, 0)
-        round_plane(on_vector, last, 3)
+        round_plane(on_vector, last, 2)
         group_out(on_scalar, 1)
         group_out(on_vector, 0)
-        round_plane(on_vector, last, 2)
-        group_out(on_scalar, 3)
+        round_plane(on_scalar, last, 3)
+        for part in halves:
+            group_out(on_scalar, 3, part)
         quantize_out(0)
         group_out(on_vector, 2)
         quantize_out(1)
         quantize_out(2)
-        quantize_out(3)
+        for part in halves:
+            quantize_out(3, part)
         for q in range(QUADS):
-            nc.scalar.dma_start(
+            queue = nc.scalar if q % 2 == 0 else nc.sync
+            queue.dma_start(
                 out=out_2[0][4 * q : 4 * q + 4, :].rearrange("r (c n) -> c r n", c=OUT_CHUNKS).bitcast(I32),
                 in_=out_plane[QUAD * q : QUAD * q + 4 * OUT_CHUNKS, :].bitcast(I32),
             )

@@ -25,11 +25,11 @@ PASSES = K // K_PASS
 CHUNK = 256
 CHUNKS = J // CHUNK
 BLOCKS = CHUNK // P
-OUT_CHUNK = 512
-OUT_CHUNKS = T // OUT_CHUNK
+WINDOWS = N // P
 HALF = N // 2
 QUADS = 4
 QUAD = 32
+QUARTER = T // QUADS
 
 
 def interleave(copy, grouped, rows):
@@ -41,6 +41,10 @@ def interleave(copy, grouped, rows):
 
 def flat(grouped):
     return grouped.rearrange("p c i -> p (c i)")
+
+
+def cols(c, width=CHUNK, count=1):
+    return slice(c * width, (c + count) * width)
 
 
 def tile_list_embg_dl_mulP_kernel(tc, dy, w4_words, w4_scales, wd, d, wgo, offs, out_0, out_1, out_2):
@@ -59,31 +63,23 @@ def tile_list_embg_dl_mulP_kernel(tc, dy, w4_words, w4_scales, wd, d, wgo, offs,
         ident = keep.tile([P, P], F32, name="ident")
         wd_first = keep.tile([P, PACK, N], F32, name="wd_first")
         wd_second = [keep.tile([P, PACK, HALF], F32, name=f"wd_second{h}") for h in range(2)]
-        wd_grouped = [keep.tile([P, N, PACK], BF16, name=f"wd_grouped{a}", align_bytes=64) for a in range(PASSES)]
+        wd_grouped = keep.tile([P, N, PACK], BF16, name="wd_grouped", align_bytes=64)
+        wd_halves = [keep.tile([P, HALF, PACK], BF16, name=f"wd_half{h}", tag=f"wd_half{h}", align_bytes=64) for h in range(2)]
         wd_codes = [keep.tile([P, N], U32, name=f"wd_codes{a}", align_bytes=64) for a in range(PASSES)]
         wd_plane = [keep.tile([P, N], U8, name=f"wd_plane{a}", align_bytes=64) for a in range(PASSES)]
-        dy_raw = [[keep.tile([P, PACK, CHUNK], F32, name=f"dy_raw{c}_{a}") for a in range(PASSES)] for c in range(CHUNKS)]
-        dy_grouped = [[keep.tile([P, CHUNK, PACK], BF16, name=f"dy_grouped{c}_{a}", align_bytes=64) for a in range(PASSES)] for c in range(CHUNKS)]
-        last_half = [keep.tile([P, P, PACK], BF16, name=f"last_half{b}", tag=f"window{2 + b}", align_bytes=64) for b in range(BLOCKS)]
-        dy_codes = [[keep.tile([P, CHUNK], U32, name=f"dy_codes{c}_{a}", align_bytes=64) for a in range(PASSES)] for c in range(CHUNKS)]
+        dy_raw = [[keep.tile([P, PACK, CHUNK], F32, name=f"dy_raw{c}_{a}", tag=f"dy_raw{c}_{a}", align_bytes=64) for a in range(PASSES)] for c in range(CHUNKS)]
+        dy_codes = [[keep.tile([P, CHUNK], U32, name=f"dy_codes{c}_{a}", tag=f"dy_codes{c}_{a}", align_bytes=64) for a in range(PASSES)] for c in range(CHUNKS)]
         dy_plane = [[keep.tile([P, CHUNK], U8, name=f"dy_plane{c}_{a}", align_bytes=64) for a in range(PASSES)] for c in range(CHUNKS)]
-        d_early = [keep.tile([P, PACK, CHUNK], F32, name=f"d_early{c}") for c in range(2)]
-        d_late = keep.tile([P, PACK, 2 * CHUNK], F32, name="d_late")
-        by_token = [keep.tile([P, PACK, P], F32, name=f"by_token{b}") for b in range(J // P)]
-        by_row = [keep.tile([P, J], F32, name=f"by_row{t}") for t in range(PACK)]
-        window = [keep.tile([P, T], F32, name=f"window{t}") for t in range(2)]
-        rounded = [keep.tile([P, PACK, OUT_CHUNK], BF16, name=f"rounded{c}") for c in range(OUT_CHUNKS)]
-        out_grouped = [keep.tile([P, OUT_CHUNK, PACK], BF16, name=f"out_grouped{c}", align_bytes=64) for c in range(OUT_CHUNKS)]
-        out_codes = [keep.tile([P, OUT_CHUNK], U32, name=f"out_codes{c}", align_bytes=64) for c in range(OUT_CHUNKS)]
-        out_plane = keep.tile([P, OUT_CHUNK], U8, name="out_plane", align_bytes=64)
+        d_first = keep.tile([P, WINDOWS, CHUNK], F32, name="d_first")
+        d_second = keep.tile([P, WINDOWS, CHUNK], F32, name="d_second")
+        d_third = keep.tile([P, WINDOWS, 2 * CHUNK], F32, name="d_third")
+        window = [keep.tile([P, T], F32, name=f"window{s}") for s in range(2)]
+        out_plane = keep.tile([P, QUARTER], U8, name="out_plane", align_bytes=64)
 
         dy_rows = dy.rearrange("(a p i) j -> a p i j", a=PASSES, i=PACK)
         wd_rows = wd.rearrange("(a p i) n -> a p i n", a=PASSES, i=PACK)
-        d_rows = d.rearrange("(p t) j -> p t j", t=PACK)
-        out_rows = out_0.rearrange("(p t) c -> p t c", t=PACK)
-
-        def cols(c, width=CHUNK):
-            return slice(c * width, (c + 1) * width)
+        d_rows = d.rearrange("(p s) j -> p s j", s=WINDOWS)
+        out_rows = out_0.rearrange("(p s) c -> p s c", s=WINDOWS)
 
         def load_dy(c, a):
             nc.sync.dma_start(out=dy_raw[c][a][:], in_=dy_rows[a][:, :, cols(c)])
@@ -91,8 +87,8 @@ def tile_list_embg_dl_mulP_kernel(tc, dy, w4_words, w4_scales, wd, d, wgo, offs,
         nc.gpsimd.memset(w4_plane[:].rearrange("p a n -> p (a n)").bitcast(I32), 0)
         nc.gpsimd.memset(wgo_rows[:], 0.0)
         make_identity(nc, ident[:])
-        for t in range(2):
-            nc.vector.memset(window[t][:], 0.0)
+        for s in range(2):
+            nc.vector.memset(window[s][:], 0.0)
 
         nc.sync.dma_start(out=wd_first[:], in_=wd_rows[0])
         load_dy(0, 0)
@@ -105,35 +101,32 @@ def tile_list_embg_dl_mulP_kernel(tc, dy, w4_words, w4_scales, wd, d, wgo, offs,
         load_dy(0, 1)
         for h in range(2):
             nc.sync.dma_start(out=wd_second[h][:], in_=wd_rows[1][:, :, cols(h, HALF)])
-        load_dy(1, 0)
         nc.sync.dma_start(out=wgo_rows[0 : J // P, :], in_=wgo[0:1, :].rearrange("o (b m) -> (o b) m", m=P))
-        load_dy(1, 1)
         nc.sync.dma_start(offsets[:], offs)
-        nc.sync.dma_start(out=d_early[0][:], in_=d_rows[:, :, cols(0)])
+        nc.sync.dma_start(out=d_first[:], in_=d_rows[:, :, cols(0)])
+        load_dy(1, 0)
+        load_dy(1, 1)
+        nc.sync.dma_start(out=d_second[:], in_=d_rows[:, :, cols(1)])
         load_dy(2, 0)
         load_dy(2, 1)
-        nc.sync.dma_start(out=d_early[1][:], in_=d_rows[:, :, cols(1)])
         load_dy(3, 0)
         load_dy(3, 1)
-        nc.sync.dma_start(out=d_late[:], in_=d_rows[:, :, cols(1, 2 * CHUNK)])
+        nc.sync.dma_start(out=d_third[:], in_=d_rows[:, :, cols(2, count=2)])
 
         def group_wd(grouped, raw, split):
             interleave(on_scalar, grouped[:, :split, :], raw[:, :, :split])
             interleave(on_vector, grouped[:, split:, :], raw[:, :, split:])
 
-        def quantize_wd(a, part):
-            nc.vector.quantize_mx(out=wd_codes[a][:, part].bitcast(E4M3), scales=wd_plane[a][:, part], in_=flat(wd_grouped[a][:, part, :]))
+        def quantize_wd(a, part, grouped):
+            nc.vector.quantize_mx(out=wd_codes[a][:, part].bitcast(E4M3), scales=wd_plane[a][:, part], in_=flat(grouped))
 
-        def group_dy(copy, c, a, part=slice(0, CHUNK)):
-            interleave(copy, dy_grouped[c][a][:, part, :], dy_raw[c][a][:, :, part])
+        def prepare_dy(c, a, behind=None):
+            grouped = keep.tile([P, CHUNK, PACK], BF16, name=f"dy_grouped{c}_{a}", tag=behind or f"dy_grouped{c}_{a}", align_bytes=64)
+            interleave(on_scalar, grouped[:], dy_raw[c][a][:])
+            nc.vector.quantize_mx(out=dy_codes[c][a][:].bitcast(E5M2), scales=dy_plane[c][a][:], in_=flat(grouped[:]))
 
-        def quantize_dy(c, a, part=slice(0, CHUNK)):
-            nc.vector.quantize_mx(
-                out=dy_codes[c][a][:, part].bitcast(E5M2), scales=dy_plane[c][a][:, part], in_=flat(dy_grouped[c][a][:, part, :])
-            )
-
-        def multiply(c, order):
-            banks = [psum.tile([P, N], F32, name=f"sums{c}_{b}", tag=f"bank{(4 * c + 1 - b) % 8}") for b in range(BLOCKS)]
+        def multiply(c, order, tags):
+            banks = [psum.tile([P, N], F32, name=f"sums{c}_{b}", tag=f"bank{tags[b]}") for b in range(BLOCKS)]
             for step, (codes, plane, a) in enumerate(order):
                 for b in range(BLOCKS):
                     tokens = cols(b, P)
@@ -153,114 +146,119 @@ def tile_list_embg_dl_mulP_kernel(tc, dy, w4_words, w4_scales, wd, d, wgo, offs,
         base_first = [wd_pass[0], w4_pass[0], w4_pass[1], wd_pass[1]]
         pass_by_pass = [w4_pass[0], wd_pass[0], w4_pass[1], wd_pass[1]]
 
-        def weigh(c, banks, vector_blocks=()):
+        by_token = {}
+
+        def weigh(c, banks, first=0, count=WINDOWS, vector_blocks=()):
             for b in range(BLOCKS):
                 block = BLOCKS * c + b
-                dealt = banks[b][:].rearrange("j (m t) -> j t m", t=PACK)
                 weight = wgo_cols[:, block : block + 1]
+                weighed = keep.tile([P, count, P], F32, name=f"by_token{block}_{first}", tag=f"by_token{block}_{first}", align_bytes=64)
+                sums = banks[b][:].rearrange("j (m s) -> j s m", s=WINDOWS)[:, first : first + count, :]
                 if b in vector_blocks:
-                    nc.vector.tensor_scalar(out=by_token[block][:], in0=dealt, scalar1=weight, scalar2=None, op0=MULT)
+                    nc.vector.tensor_scalar(out=weighed[:], in0=sums, scalar1=weight, scalar2=None, op0=MULT)
                 else:
-                    nc.scalar.activation(out=by_token[block][:], in_=dealt, func=COPY, scale=weight)
+                    nc.scalar.activation(out=weighed[:], in_=sums, func=COPY, scale=weight)
+                for s in range(count):
+                    by_token[block, first + s] = weighed[:, s, :]
 
-        def turn(c, t):
-            bank = psum.tile([P, CHUNK], F32, name=f"turned{c}_{t}", tag=f"bank{(4 * c + 2 + t) % 8}")
-            for b in range(BLOCKS):
-                nc.tensor.transpose(bank[:, cols(b, P)], by_token[BLOCKS * c + b][:, t, :], ident[:])
-            nc.scalar.copy(out=by_row[t][:, cols(c)], in_=bank[:])
+        def turn(pieces, tag, rows):
+            bank = psum.tile([P, len(pieces) * CHUNK], F32, name=f"turned{pieces[0][0]}_{pieces[0][1]}", tag=f"bank{tag}")
+            for k, (s, c) in enumerate(pieces):
+                for b in range(BLOCKS):
+                    nc.tensor.transpose(bank[:, cols(BLOCKS * k + b, P)], by_token[BLOCKS * c + b, s], ident[:])
+            nc.scalar.copy(out=rows, in_=bank[:])
 
-        def scatter(t, first, count, d_part):
-            lo, hi = first * CHUNK, (first + count) * CHUNK
-            nc.vector.tensor_tensor(window[t][:].indirect(offsets[:, lo // 16 : hi // 16]), by_row[t][:, lo:hi], d_part, MULT)
+        def scatter(s, first, count, rows, d_part):
+            nc.vector.tensor_tensor(window[s][:].indirect(offsets[:, cols(first, CHUNK // 16, count)]), rows, d_part, MULT)
 
-        def round_plane(copy, t, c):
-            copy(out=rounded[c][:, t, :], in_=window[t][:, cols(c, OUT_CHUNK)])
+        def place(first, count, c, tag, d_part, behind=None):
+            rows = keep.tile([P, count * CHUNK], F32, name=f"by_row{first}_{c}", tag=behind or f"by_row{first}_{c}", align_bytes=64)
+            turn([(first + k, c) for k in range(count)], tag, rows[:])
+            for k in range(count):
+                scatter(first + k, c, 1, rows[:, cols(k)], d_part[:, first + k, :])
 
-        def finish(t):
-            nc.sync.dma_start(out=out_rows[:, t, :], in_=window[t][:])
-            if t < PACK - 1:
-                for c in range(OUT_CHUNKS):
-                    round_plane(on_scalar, t, c)
+        rounded = [keep.tile([P, PACK, QUARTER], BF16, name=f"rounded{c}") for c in range(QUADS)]
+        out_grouped = [keep.tile([P, QUARTER, PACK], BF16, name=f"out_grouped{c}", align_bytes=64) for c in range(QUADS)]
+        out_codes = [keep.tile([P, QUARTER], U32, name=f"out_codes{c}", align_bytes=64) for c in range(QUADS)]
+
+        def round_plane(copy, s, c):
+            copy(out=rounded[c][:, s, :], in_=window[s][:, cols(c, QUARTER)])
+
+        def store_window(s):
+            nc.sync.dma_start(out=out_rows[:, s, :], in_=window[s][:])
+            if s < WINDOWS - 1:
+                for c in range(QUADS):
+                    round_plane(on_scalar, s, c)
 
         wgo_bank = psum.tile([P, P], F32, name="wgo_bank", tag="bank7")
 
-        group_wd(wd_grouped[0][:], wd_first[:], 256)
-        quantize_wd(0, slice(0, N))
-        group_dy(on_scalar, 0, 0, cols(1, P))
-        group_dy(on_vector, 0, 0, cols(0, P))
-        group_dy(on_scalar, 0, 1)
-        quantize_dy(0, 0)
-        quantize_dy(0, 1)
-        interleave(on_scalar, wd_grouped[1][:, cols(0, HALF), :], wd_second[0][:])
-        quantize_wd(1, cols(0, HALF))
-        group_wd(wd_grouped[1][:, cols(1, HALF), :], wd_second[1][:], 96)
-        quantize_wd(1, cols(1, HALF))
-        group_dy(on_scalar, 1, 0, cols(1, P))
-        group_dy(on_vector, 1, 0, cols(0, P))
+        group_wd(wd_grouped[:], wd_first[:], HALF)
+        quantize_wd(0, slice(0, N), wd_grouped[:])
+        prepare_dy(0, 0)
+        prepare_dy(0, 1)
+        interleave(on_vector, wd_halves[0][:], wd_second[0][:])
+        quantize_wd(1, cols(0, HALF), wd_halves[0][:])
+        group_wd(wd_halves[1][:], wd_second[1][:], 96)
+        quantize_wd(1, cols(1, HALF), wd_halves[1][:])
         nc.tensor.transpose(wgo_bank[:], wgo_rows[:], ident[:])
         nc.scalar.copy(out=wgo_cols[:], in_=wgo_bank[:, 0 : J // P])
-        banks = multiply(0, base_first)
-        weigh(0, banks, vector_blocks=(1,))
-        for b, copy in enumerate((on_vector, on_scalar)):
-            interleave(copy, last_half[b][:], dy_raw[1][1][:, :, cols(b, P)])
-        quantize_dy(1, 0)
-        for b in range(BLOCKS):
-            nc.vector.quantize_mx(
-                out=dy_codes[1][1][:, cols(b, P)].bitcast(E5M2), scales=dy_plane[1][1][:, cols(b, P)], in_=flat(last_half[b][:])
-            )
-        for t in range(2, PACK):
-            window.append(keep.tile([P, T], F32, name=f"window{t}", tag=f"window{t}", align_bytes=64))
-            nc.gpsimd.memset(window[t][:], 0.0)
-        for t in range(PACK):
-            turn(0, t)
-        banks = multiply(1, pass_by_pass)
-        for t in range(PACK):
-            scatter(t, 0, 1, d_early[0][:, t, :])
-        for a in range(PASSES):
-            group_dy(on_scalar, 2, a)
-        weigh(1, banks)
-        for t in range(PACK):
-            turn(1, t)
-        for a in range(PASSES):
-            quantize_dy(2, a)
-        banks = multiply(2, pass_by_pass)
-        for a in range(PASSES):
-            group_dy(on_scalar, 3, a)
-        for t in range(2):
-            scatter(t, 1, 1, d_early[1][:, t, :])
-        for a in range(PASSES):
-            quantize_dy(3, a)
-        for t in range(2, PACK):
-            scatter(t, 1, 1, d_early[1][:, t, :])
-        weigh(2, banks)
-        for t in range(PACK):
-            turn(2, t)
-        banks = multiply(3, pass_by_pass)
-        weigh(3, banks)
-        for t in range(PACK):
-            turn(3, t)
-        for t in range(PACK - 1):
-            scatter(t, 2, 1, d_late[:, t, cols(0)])
-        for t in range(PACK - 1):
-            scatter(t, 3, 1, d_late[:, t, cols(1)])
-            finish(t)
-        scatter(PACK - 1, 2, 2, d_late[:, PACK - 1, :])
-        finish(PACK - 1)
+        window.append(keep.tile([P, T], F32, name="window2", tag="wd_half1", align_bytes=64))
+        nc.gpsimd.memset(window[2][:], 0.0)
 
-        def group_out(copy, c, part=slice(0, OUT_CHUNK)):
+        banks = multiply(0, base_first, (0, 1))
+        weigh(0, banks, 0, 1, vector_blocks=(1,))
+        weigh(0, banks, 1, 1, vector_blocks=(1,))
+        weigh(0, banks, 2, 2, vector_blocks=(1,))
+        place(0, 1, 0, 4, d_first)
+        window.append(keep.tile([P, T], F32, name="window3", tag="by_token0_0", align_bytes=64))
+        nc.gpsimd.memset(window[3][:], 0.0)
+        prepare_dy(1, 0, behind="by_token1_1")
+        place(1, 1, 0, 5, d_first, behind="dy_raw1_0")
+        prepare_dy(1, 1, behind="by_token1_1")
+        place(2, 2, 0, 6, d_first, behind="dy_raw1_1")
+
+        banks = multiply(1, pass_by_pass, (2, 3))
+        weigh(1, banks, 0, 1)
+        place(0, 1, 1, 7, d_second)
+        weigh(1, banks, 1, 3)
+        prepare_dy(2, 0)
+        prepare_dy(2, 1, behind="by_token3_0")
+        place(1, 1, 1, 0, d_second, behind="dy_raw2_1")
+        prepare_dy(3, 0, behind="dy_codes1_1")
+        place(2, 1, 1, 1, d_second, behind="dy_raw3_0")
+        prepare_dy(3, 1, behind="dy_codes1_1")
+        place(3, 1, 1, 4, d_second, behind="dy_raw3_1")
+
+        banks = multiply(2, pass_by_pass, (7, 0))
+        weigh(2, banks)
+        for s, tag in enumerate((5, 6, 2)):
+            place(s, 1, 2, tag, d_third[:, :, cols(0)])
+
+        banks = multiply(3, pass_by_pass, (5, 6))
+        weigh(3, banks)
+        for s, tag in enumerate((3, 1, 7)):
+            place(s, 1, 3, tag, d_third[:, :, cols(1)])
+        last_rows = keep.tile([P, 2 * CHUNK], F32, name="last_rows")
+        turn([(3, 2), (3, 3)], 4, last_rows[:])
+        for s in range(WINDOWS - 1):
+            store_window(s)
+        scatter(3, 2, 2, last_rows[:], d_third[:, 3, :])
+        store_window(3)
+
+        def group_out(copy, c, part=slice(0, QUARTER)):
             interleave(copy, out_grouped[c][:, part, :], rounded[c][:, :, part])
 
-        def quantize_out(c, part=slice(0, OUT_CHUNK)):
+        def quantize_out(c, part=slice(0, QUARTER)):
             nc.vector.quantize_mx(
                 out=out_codes[c][:, part].bitcast(E4M3), scales=out_plane[4 * c :, part], in_=flat(out_grouped[c][:, part, :])
             )
             nc.sync.dma_start(
-                out=out_1[0][:, cols(c, OUT_CHUNK), :][:, part, :].rearrange("p c i -> p (c i)").bitcast(I32),
+                out=out_1[0][:, cols(c, QUARTER), :][:, part, :].rearrange("p c i -> p (c i)").bitcast(I32),
                 in_=out_codes[c][:, part].bitcast(I32),
             )
 
         last = PACK - 1
-        halves = [cols(h, OUT_CHUNK // 2) for h in range(2)]
+        halves = [cols(h, QUARTER // 2) for h in range(2)]
         round_plane(on_scalar, last, 1)
         round_plane(on_vector, last, 0)
         round_plane(on_vector, last, 2)
@@ -278,6 +276,6 @@ def tile_list_embg_dl_mulP_kernel(tc, dy, w4_words, w4_scales, wd, d, wgo, offs,
         for q in range(QUADS):
             queue = nc.scalar if q % 2 == 0 else nc.sync
             queue.dma_start(
-                out=out_2[0][4 * q : 4 * q + 4, :].rearrange("r (c n) -> c r n", c=OUT_CHUNKS).bitcast(I32),
-                in_=out_plane[QUAD * q : QUAD * q + 4 * OUT_CHUNKS, :].bitcast(I32),
+                out=out_2[0][4 * q : 4 * q + 4, :].rearrange("r (c n) -> c r n", c=QUADS).bitcast(I32),
+                in_=out_plane[QUAD * q : QUAD * q + 4 * QUADS, :].bitcast(I32),
             )

@@ -61,18 +61,17 @@ def tile_list_embg_dl_mulP_kernel(tc, dy, w4_words, w4_scales, wd, d, wgo, offs,
         wgo_rows = keep.tile([P, P], F32, name="wgo_rows")
         wgo_cols = keep.tile([P, J // P], F32, name="wgo_cols")
         ident = keep.tile([P, P], F32, name="ident")
-        wd_first = keep.tile([P, PACK, N], F32, name="wd_first")
-        wd_second = [keep.tile([P, PACK, HALF], F32, name=f"wd_second{h}") for h in range(2)]
-        wd_grouped = keep.tile([P, N, PACK], BF16, name="wd_grouped", align_bytes=64)
-        wd_halves = [keep.tile([P, HALF, PACK], BF16, name=f"wd_half{h}", tag=f"wd_half{h}", align_bytes=64) for h in range(2)]
+        wd_raw = [keep.tile([P, PACK, N], F32, name=f"wd_raw{a}") for a in range(PASSES)]
+        wd_grouped = [keep.tile([P, N, PACK], BF16, name=f"wd_grouped{a}", align_bytes=64) for a in range(PASSES)]
         wd_codes = [keep.tile([P, N], U32, name=f"wd_codes{a}", align_bytes=64) for a in range(PASSES)]
         wd_plane = [keep.tile([P, N], U8, name=f"wd_plane{a}", align_bytes=64) for a in range(PASSES)]
         dy_raw = [[keep.tile([P, PACK, CHUNK], F32, name=f"dy_raw{c}_{a}", tag=f"dy_raw{c}_{a}", align_bytes=64) for a in range(PASSES)] for c in range(CHUNKS)]
         dy_codes = [[keep.tile([P, CHUNK], U32, name=f"dy_codes{c}_{a}", tag=f"dy_codes{c}_{a}", align_bytes=64) for a in range(PASSES)] for c in range(CHUNKS)]
         dy_plane = [[keep.tile([P, CHUNK], U8, name=f"dy_plane{c}_{a}", align_bytes=64) for a in range(PASSES)] for c in range(CHUNKS)]
         d_first = keep.tile([P, WINDOWS, CHUNK], F32, name="d_first")
-        d_second = keep.tile([P, WINDOWS, CHUNK], F32, name="d_second")
-        d_third = keep.tile([P, WINDOWS, 2 * CHUNK], F32, name="d_third")
+        d_second = keep.tile([P, WINDOWS - 1, CHUNK], F32, name="d_second")
+        d_third = keep.tile([P, WINDOWS - 1, 2 * CHUNK], F32, name="d_third")
+        d_last = keep.tile([P, 3 * CHUNK], F32, name="d_last")
         window = [keep.tile([P, T], F32, name=f"window{s}") for s in range(2)]
         out_plane = keep.tile([P, QUARTER], U8, name="out_plane", align_bytes=64)
 
@@ -90,7 +89,7 @@ def tile_list_embg_dl_mulP_kernel(tc, dy, w4_words, w4_scales, wd, d, wgo, offs,
         for s in range(2):
             nc.vector.memset(window[s][:], 0.0)
 
-        nc.sync.dma_start(out=wd_first[:], in_=wd_rows[0])
+        nc.sync.dma_start(out=wd_raw[0][:], in_=wd_rows[0])
         load_dy(0, 0)
         nc.sync.dma_start(out=w4_codes[:].bitcast(I32), in_=w4_words.rearrange("a p c -> p a c").bitcast(I32))
         for q in range(QUADS):
@@ -98,37 +97,37 @@ def tile_list_embg_dl_mulP_kernel(tc, dy, w4_words, w4_scales, wd, d, wgo, offs,
                 out=w4_plane[QUAD * q : QUAD * q + 4].bitcast(I32),
                 in_=w4_scales[:, 4 * q : 4 * q + 4, :].rearrange("a r n -> r a n").bitcast(I32),
             )
+        nc.sync.dma_start(out=wd_raw[1][:], in_=wd_rows[1])
         load_dy(0, 1)
-        for h in range(2):
-            nc.sync.dma_start(out=wd_second[h][:], in_=wd_rows[1][:, :, cols(h, HALF)])
         nc.sync.dma_start(out=wgo_rows[0 : J // P, :], in_=wgo[0:1, :].rearrange("o (b m) -> (o b) m", m=P))
         nc.sync.dma_start(offsets[:], offs)
-        nc.sync.dma_start(out=d_first[:], in_=d_rows[:, :, cols(0)])
         load_dy(1, 0)
+        nc.sync.dma_start(out=d_first[:], in_=d_rows[:, :, cols(0)])
         load_dy(1, 1)
-        nc.sync.dma_start(out=d_second[:], in_=d_rows[:, :, cols(1)])
+        nc.sync.dma_start(out=d_second[:], in_=d_rows[:, 0 : WINDOWS - 1, cols(1)])
         load_dy(2, 0)
         load_dy(2, 1)
         load_dy(3, 0)
         load_dy(3, 1)
-        nc.sync.dma_start(out=d_third[:], in_=d_rows[:, :, cols(2, count=2)])
+        nc.sync.dma_start(out=d_third[:], in_=d_rows[:, 0 : WINDOWS - 1, cols(2, count=2)])
+        nc.sync.dma_start(out=d_last[:], in_=d_rows[:, WINDOWS - 1, cols(1, count=3)])
 
-        def group_wd(grouped, raw, split):
-            interleave(on_scalar, grouped[:, :split, :], raw[:, :, :split])
-            interleave(on_vector, grouped[:, split:, :], raw[:, :, split:])
+        def prepare_wd(a, split):
+            interleave(on_scalar, wd_grouped[a][:, :split, :], wd_raw[a][:, :, :split])
+            interleave(on_vector, wd_grouped[a][:, split:, :], wd_raw[a][:, :, split:])
+            nc.vector.quantize_mx(out=wd_codes[a][:].bitcast(E4M3), scales=wd_plane[a][:], in_=flat(wd_grouped[a][:]))
 
-        def quantize_wd(a, part, grouped):
-            nc.vector.quantize_mx(out=wd_codes[a][:, part].bitcast(E4M3), scales=wd_plane[a][:, part], in_=flat(grouped))
-
-        def prepare_dy(c, a, behind=None):
-            grouped = keep.tile([P, CHUNK, PACK], BF16, name=f"dy_grouped{c}_{a}", tag=behind or f"dy_grouped{c}_{a}", align_bytes=64)
-            interleave(on_scalar, grouped[:], dy_raw[c][a][:])
-            nc.vector.quantize_mx(out=dy_codes[c][a][:].bitcast(E5M2), scales=dy_plane[c][a][:], in_=flat(grouped[:]))
+        def prepare_dy(c, a, behind=None, part=slice(0, CHUNK)):
+            name = f"dy_grouped{c}_{a}_{part.start}"
+            grouped = keep.tile([P, part.stop - part.start, PACK], BF16, name=name, tag=behind or name, align_bytes=64)
+            interleave(on_scalar, grouped[:], dy_raw[c][a][:, :, part])
+            nc.vector.quantize_mx(out=dy_codes[c][a][:, part].bitcast(E5M2), scales=dy_plane[c][a][:, part], in_=flat(grouped[:]))
 
         def multiply(c, order, tags):
             banks = [psum.tile([P, N], F32, name=f"sums{c}_{b}", tag=f"bank{tags[b]}") for b in range(BLOCKS)]
-            for step, (codes, plane, a) in enumerate(order):
-                for b in range(BLOCKS):
+            steps = [(step, b) for step in range(2) for b in range(BLOCKS)] + [(step, b) for b in range(BLOCKS) for step in range(2, 4)]
+            for step, b in steps:
+                for codes, plane, a in order[step : step + 1]:
                     tokens = cols(b, P)
                     nc.tensor.matmul_mx(
                         out=banks[b][:],
@@ -143,7 +142,7 @@ def tile_list_embg_dl_mulP_kernel(tc, dy, w4_words, w4_scales, wd, d, wgo, offs,
 
         w4_pass = [(w4_codes[:, a, :].bitcast(E2M1), w4_plane[:, a, :], a) for a in range(PASSES)]
         wd_pass = [(wd_codes[a][:].bitcast(E4M3), wd_plane[a][:], a) for a in range(PASSES)]
-        base_first = [wd_pass[0], w4_pass[0], w4_pass[1], wd_pass[1]]
+        base_first = [wd_pass[0], w4_pass[0], wd_pass[1], w4_pass[1]]
         pass_by_pass = [w4_pass[0], wd_pass[0], w4_pass[1], wd_pass[1]]
 
         by_token = {}
@@ -161,92 +160,92 @@ def tile_list_embg_dl_mulP_kernel(tc, dy, w4_words, w4_scales, wd, d, wgo, offs,
                 for s in range(count):
                     by_token[block, first + s] = weighed[:, s, :]
 
-        def turn(pieces, tag, rows):
+        def turn(pieces, tag, rows, copy=on_scalar):
             bank = psum.tile([P, len(pieces) * CHUNK], F32, name=f"turned{pieces[0][0]}_{pieces[0][1]}", tag=f"bank{tag}")
             for k, (s, c) in enumerate(pieces):
                 for b in range(BLOCKS):
                     nc.tensor.transpose(bank[:, cols(BLOCKS * k + b, P)], by_token[BLOCKS * c + b, s], ident[:])
-            nc.scalar.copy(out=rows, in_=bank[:])
+            copy(out=rows, in_=bank[:])
 
         def scatter(s, first, count, rows, d_part):
             nc.vector.tensor_tensor(window[s][:].indirect(offsets[:, cols(first, CHUNK // 16, count)]), rows, d_part, MULT)
 
-        def place(first, count, c, tag, d_part, behind=None):
+        def place(first, count, c, tag, d_part, behind=None, copy=on_scalar):
             rows = keep.tile([P, count * CHUNK], F32, name=f"by_row{first}_{c}", tag=behind or f"by_row{first}_{c}", align_bytes=64)
-            turn([(first + k, c) for k in range(count)], tag, rows[:])
+            turn([(first + k, c) for k in range(count)], tag, rows[:], copy)
             for k in range(count):
                 scatter(first + k, c, 1, rows[:, cols(k)], d_part[:, first + k, :])
 
-        rounded = [keep.tile([P, PACK, QUARTER], BF16, name=f"rounded{c}") for c in range(QUADS)]
+        def store_window(s):
+            nc.sync.dma_start(out=out_rows[:, s, :], in_=window[s][:])
+
+        wgo_bank = psum.tile([P, P], F32, name="wgo_bank", tag="bank7")
+
+        prepare_wd(0, HALF)
+        prepare_dy(0, 0)
+        prepare_wd(1, 192)
+        for b in range(BLOCKS):
+            prepare_dy(0, 1, part=cols(b, P))
+        nc.tensor.transpose(wgo_bank[:], wgo_rows[:], ident[:])
+        nc.scalar.copy(out=wgo_cols[:], in_=wgo_bank[:, 0 : J // P])
+        window.append(keep.tile([P, T], F32, name="window2", tag=f"dy_grouped0_1_{P}", align_bytes=64))
+        nc.gpsimd.memset(window[2][:], 0.0)
+
+        prepare_dy(1, 0)
+
+        banks = multiply(0, base_first, (0, 1))
+        weigh(0, banks, 0, 1, vector_blocks=(0, 1))
+        place(0, 1, 0, 4, d_first, copy=on_vector)
+        window.append(keep.tile([P, T], F32, name="window3", tag="by_token0_0", align_bytes=64))
+        nc.gpsimd.memset(window[3][:], 0.0)
+        weigh(0, banks, 1, 3, vector_blocks=(1,))
+        place(1, 1, 0, 5, d_first)
+        prepare_dy(1, 1)
+        place(2, 2, 0, 6, d_first, behind="dy_raw1_1")
+
+        banks = multiply(1, pass_by_pass, (4, 5))
+        weigh(1, banks, 0, 1)
+        prepare_dy(2, 0)
+        prepare_dy(2, 1)
+        place(0, 1, 1, 7, d_second, behind="dy_raw2_1")
+        weigh(1, banks, 1, 3)
+        place(1, 1, 1, 0, d_second)
+        prepare_dy(3, 0, behind="dy_codes1_1")
+        prepare_dy(3, 1, behind="dy_raw3_0")
+        place(2, 1, 1, 1, d_second, behind="dy_raw3_1")
+
+        banks = multiply(2, pass_by_pass, (7, 0))
+        weigh(2, banks, 0, 1)
+        place(0, 1, 2, 2, d_third[:, :, cols(0)])
+        weigh(2, banks, 1, 3)
+        place(1, 1, 2, 3, d_third[:, :, cols(0)])
+
+        banks = multiply(3, pass_by_pass, (2, 1))
+        weigh(3, banks, 0, 1)
+        place(0, 1, 3, 4, d_third[:, :, cols(1)])
+        store_window(0)
+        weigh(3, banks, 1, 3)
+        place(1, 1, 3, 6, d_third[:, :, cols(1)])
+        store_window(1)
+        late_rows = keep.tile([P, 2 * CHUNK], F32, name="late_rows", tag="late_rows")
+        turn([(2, 2), (2, 3)], 5, late_rows[:])
+        scatter(2, 2, 2, late_rows[:], d_third[:, 2, :])
+        store_window(2)
+        last = WINDOWS - 1
+        last_rows = keep.tile([P, 2 * CHUNK], F32, name="last_rows")
+        turn([(last, 1), (last, 2)], 0, last_rows[:])
+        scatter(last, 1, 2, last_rows[:], d_last[:, cols(0, count=2)])
+
+        pairs = [keep.tile([P, 2, QUARTER, 2], BF16, name=f"pairs{c}") for c in range(QUADS)]
         out_grouped = [keep.tile([P, QUARTER, PACK], BF16, name=f"out_grouped{c}", align_bytes=64) for c in range(QUADS)]
         out_codes = [keep.tile([P, QUARTER], U32, name=f"out_codes{c}", align_bytes=64) for c in range(QUADS)]
 
         def round_plane(copy, s, c):
-            copy(out=rounded[c][:, s, :], in_=window[s][:, cols(c, QUARTER)])
-
-        def store_window(s):
-            nc.sync.dma_start(out=out_rows[:, s, :], in_=window[s][:])
-            if s < WINDOWS - 1:
-                for c in range(QUADS):
-                    round_plane(on_scalar, s, c)
-
-        wgo_bank = psum.tile([P, P], F32, name="wgo_bank", tag="bank7")
-
-        group_wd(wd_grouped[:], wd_first[:], HALF)
-        quantize_wd(0, slice(0, N), wd_grouped[:])
-        prepare_dy(0, 0)
-        prepare_dy(0, 1)
-        interleave(on_vector, wd_halves[0][:], wd_second[0][:])
-        quantize_wd(1, cols(0, HALF), wd_halves[0][:])
-        group_wd(wd_halves[1][:], wd_second[1][:], 96)
-        quantize_wd(1, cols(1, HALF), wd_halves[1][:])
-        nc.tensor.transpose(wgo_bank[:], wgo_rows[:], ident[:])
-        nc.scalar.copy(out=wgo_cols[:], in_=wgo_bank[:, 0 : J // P])
-        window.append(keep.tile([P, T], F32, name="window2", tag="wd_half1", align_bytes=64))
-        nc.gpsimd.memset(window[2][:], 0.0)
-
-        banks = multiply(0, base_first, (0, 1))
-        weigh(0, banks, 0, 1, vector_blocks=(1,))
-        weigh(0, banks, 1, 1, vector_blocks=(1,))
-        weigh(0, banks, 2, 2, vector_blocks=(1,))
-        place(0, 1, 0, 4, d_first)
-        window.append(keep.tile([P, T], F32, name="window3", tag="by_token0_0", align_bytes=64))
-        nc.gpsimd.memset(window[3][:], 0.0)
-        prepare_dy(1, 0, behind="by_token1_1")
-        place(1, 1, 0, 5, d_first, behind="dy_raw1_0")
-        prepare_dy(1, 1, behind="by_token1_1")
-        place(2, 2, 0, 6, d_first, behind="dy_raw1_1")
-
-        banks = multiply(1, pass_by_pass, (2, 3))
-        weigh(1, banks, 0, 1)
-        place(0, 1, 1, 7, d_second)
-        weigh(1, banks, 1, 3)
-        prepare_dy(2, 0)
-        prepare_dy(2, 1, behind="by_token3_0")
-        place(1, 1, 1, 0, d_second, behind="dy_raw2_1")
-        prepare_dy(3, 0, behind="dy_codes1_1")
-        place(2, 1, 1, 1, d_second, behind="dy_raw3_0")
-        prepare_dy(3, 1, behind="dy_codes1_1")
-        place(3, 1, 1, 4, d_second, behind="dy_raw3_1")
-
-        banks = multiply(2, pass_by_pass, (7, 0))
-        weigh(2, banks)
-        for s, tag in enumerate((5, 6, 2)):
-            place(s, 1, 2, tag, d_third[:, :, cols(0)])
-
-        banks = multiply(3, pass_by_pass, (5, 6))
-        weigh(3, banks)
-        for s, tag in enumerate((3, 1, 7)):
-            place(s, 1, 3, tag, d_third[:, :, cols(1)])
-        last_rows = keep.tile([P, 2 * CHUNK], F32, name="last_rows")
-        turn([(3, 2), (3, 3)], 4, last_rows[:])
-        for s in range(WINDOWS - 1):
-            store_window(s)
-        scatter(3, 2, 2, last_rows[:], d_third[:, 3, :])
-        store_window(3)
+            copy(out=pairs[c][:, s // 2, :, s % 2], in_=window[s][:, cols(c, QUARTER)])
 
         def group_out(copy, c, part=slice(0, QUARTER)):
-            interleave(copy, out_grouped[c][:, part, :], rounded[c][:, :, part])
+            words = pairs[c][:].rearrange("p h c e -> p (h c e)").bitcast(F32).rearrange("p (h c) -> p c h", h=2)
+            copy(out=flat(out_grouped[c][:]).bitcast(F32).rearrange("p (c h) -> p c h", h=2)[:, part, :], in_=words[:, part, :])
 
         def quantize_out(c, part=slice(0, QUARTER)):
             nc.vector.quantize_mx(
@@ -257,18 +256,27 @@ def tile_list_embg_dl_mulP_kernel(tc, dy, w4_words, w4_scales, wd, d, wgo, offs,
                 in_=out_codes[c][:, part].bitcast(I32),
             )
 
-        last = PACK - 1
+        for s, quarters in ((0, range(QUADS)), (1, (0, 2)), (2, (0, 2))):
+            for c in quarters:
+                round_plane(on_scalar, s, c)
+        final_rows = keep.tile([P, CHUNK], F32, name="final_rows", tag="late_rows")
+        turn([(last, 3)], 7, final_rows[:])
+        scatter(last, 3, 1, final_rows[:], d_last[:, cols(2)])
+        store_window(last)
+        for s in (1, 2):
+            for c in (1, 3):
+                round_plane(on_scalar, s, c)
         halves = [cols(h, QUARTER // 2) for h in range(2)]
         round_plane(on_scalar, last, 1)
         round_plane(on_vector, last, 0)
         round_plane(on_vector, last, 2)
         group_out(on_scalar, 1)
         group_out(on_vector, 0)
+        group_out(on_vector, 2)
         round_plane(on_scalar, last, 3)
         for part in halves:
             group_out(on_scalar, 3, part)
         quantize_out(0)
-        group_out(on_vector, 2)
         quantize_out(1)
         quantize_out(2)
         for part in halves:

@@ -66,13 +66,13 @@ def tile_list_embg_dl_mulP_kernel(tc, dy, w4_words, w4_scales, wd, d, wgo, offs,
         wd_codes = [keep.tile([P, N], U32, name=f"wd_codes{a}", align_bytes=64) for a in range(PASSES)]
         wd_plane = [keep.tile([P, N], U8, name=f"wd_plane{a}", align_bytes=64) for a in range(PASSES)]
         dy_raw = [[keep.tile([P, PACK, CHUNK], F32, name=f"dy_raw{c}_{a}", tag=f"dy_raw{c}_{a}", align_bytes=64) for a in range(PASSES)] for c in range(CHUNKS)]
-        dy_codes = [[keep.tile([P, CHUNK], U32, name=f"dy_codes{c}_{a}", tag=f"dy_codes{c}_{a}", align_bytes=64) for a in range(PASSES)] for c in range(CHUNKS)]
+        dy_codes = {}
         dy_plane = [[keep.tile([P, CHUNK], U8, name=f"dy_plane{c}_{a}", align_bytes=64) for a in range(PASSES)] for c in range(CHUNKS)]
         d_first = keep.tile([P, WINDOWS, CHUNK], F32, name="d_first")
         d_second = keep.tile([P, WINDOWS - 1, CHUNK], F32, name="d_second")
         d_third = keep.tile([P, WINDOWS - 1, 2 * CHUNK], F32, name="d_third")
         d_last = keep.tile([P, 3 * CHUNK], F32, name="d_last")
-        window = [keep.tile([P, T], F32, name=f"window{s}") for s in range(2)]
+        window = [keep.tile([P, T], F32, name=f"window{s}") for s in range(WINDOWS)]
         out_plane = keep.tile([P, QUARTER], U8, name="out_plane", align_bytes=64)
 
         dy_rows = dy.rearrange("(a p i) j -> a p i j", a=PASSES, i=PACK)
@@ -86,7 +86,7 @@ def tile_list_embg_dl_mulP_kernel(tc, dy, w4_words, w4_scales, wd, d, wgo, offs,
         nc.gpsimd.memset(w4_plane[:].rearrange("p a n -> p (a n)").bitcast(I32), 0)
         nc.gpsimd.memset(wgo_rows[:], 0.0)
         make_identity(nc, ident[:])
-        for s in range(2):
+        for s in range(WINDOWS):
             nc.vector.memset(window[s][:], 0.0)
 
         nc.sync.dma_start(out=wd_raw[0][:], in_=wd_rows[0])
@@ -117,11 +117,20 @@ def tile_list_embg_dl_mulP_kernel(tc, dy, w4_words, w4_scales, wd, d, wgo, offs,
             interleave(on_vector, wd_grouped[a][:, split:, :], wd_raw[a][:, :, split:])
             nc.vector.quantize_mx(out=wd_codes[a][:].bitcast(E4M3), scales=wd_plane[a][:], in_=flat(wd_grouped[a][:]))
 
-        def prepare_dy(c, a, behind=None, part=slice(0, CHUNK)):
+        def group_dy(c, a, behind=None, part=slice(0, CHUNK)):
             name = f"dy_grouped{c}_{a}_{part.start}"
             grouped = keep.tile([P, part.stop - part.start, PACK], BF16, name=name, tag=behind or name, align_bytes=64)
             interleave(on_scalar, grouped[:], dy_raw[c][a][:, :, part])
-            nc.vector.quantize_mx(out=dy_codes[c][a][:, part].bitcast(E5M2), scales=dy_plane[c][a][:, part], in_=flat(grouped[:]))
+            return grouped
+
+        def quantize_dy(c, a, grouped, behind=None, part=slice(0, CHUNK)):
+            if (c, a) not in dy_codes:
+                name = f"dy_codes{c}_{a}"
+                dy_codes[c, a] = keep.tile([P, CHUNK], U32, name=name, tag=behind or name, align_bytes=64)
+            nc.vector.quantize_mx(out=dy_codes[c, a][:, part].bitcast(E5M2), scales=dy_plane[c][a][:, part], in_=flat(grouped[:]))
+
+        def prepare_dy(c, a, behind=None, part=slice(0, CHUNK)):
+            quantize_dy(c, a, group_dy(c, a, behind, part), part=part)
 
         def multiply(c, order, tags):
             banks = [psum.tile([P, N], F32, name=f"sums{c}_{b}", tag=f"bank{tags[b]}") for b in range(BLOCKS)]
@@ -131,7 +140,7 @@ def tile_list_embg_dl_mulP_kernel(tc, dy, w4_words, w4_scales, wd, d, wgo, offs,
                     tokens = cols(b, P)
                     nc.tensor.matmul_mx(
                         out=banks[b][:],
-                        lhsT=dy_codes[c][a][:, tokens].bitcast(E5M2),
+                        lhsT=dy_codes[c, a][:, tokens].bitcast(E5M2),
                         lhsT_scale=dy_plane[c][a][:, tokens],
                         rhs=codes,
                         rhs_scale=plane,
@@ -188,25 +197,22 @@ def tile_list_embg_dl_mulP_kernel(tc, dy, w4_words, w4_scales, wd, d, wgo, offs,
             prepare_dy(0, 1, part=cols(b, P))
         nc.tensor.transpose(wgo_bank[:], wgo_rows[:], ident[:])
         nc.scalar.copy(out=wgo_cols[:], in_=wgo_bank[:, 0 : J // P])
-        window.append(keep.tile([P, T], F32, name="window2", tag=f"dy_grouped0_1_{P}", align_bytes=64))
-        nc.gpsimd.memset(window[2][:], 0.0)
 
-        prepare_dy(1, 0)
+        early = group_dy(1, 0)
 
         banks = multiply(0, base_first, (0, 1))
         weigh(0, banks, 0, 1, vector_blocks=(0, 1))
         place(0, 1, 0, 4, d_first, copy=on_vector)
-        window.append(keep.tile([P, T], F32, name="window3", tag="by_token0_0", align_bytes=64))
-        nc.gpsimd.memset(window[3][:], 0.0)
+        quantize_dy(1, 0, early, behind="by_token1_0")
         weigh(0, banks, 1, 3, vector_blocks=(1,))
         place(1, 1, 0, 5, d_first)
-        prepare_dy(1, 1)
+        prepare_dy(1, 1, behind="by_token0_1")
         place(2, 2, 0, 6, d_first, behind="dy_raw1_1")
 
         banks = multiply(1, pass_by_pass, (4, 5))
         weigh(1, banks, 0, 1)
-        prepare_dy(2, 0)
-        prepare_dy(2, 1)
+        prepare_dy(2, 0, behind="by_token0_1")
+        prepare_dy(2, 1, behind="dy_raw2_0")
         place(0, 1, 1, 7, d_second, behind="dy_raw2_1")
         weigh(1, banks, 1, 3)
         place(1, 1, 1, 0, d_second)

@@ -68,7 +68,8 @@ def tile_list_embg_dl_mulP_kernel(tc, dy, w4_words, w4_scales, wd, d, wgo, offs,
         dy_raw = [[keep.tile([P, PACK, CHUNK], F32, name=f"dy_raw{c}_{a}", tag=f"dy_raw{c}_{a}", align_bytes=64) for a in range(PASSES)] for c in range(CHUNKS)]
         dy_codes = {}
         dy_plane = [[keep.tile([P, CHUNK], U8, name=f"dy_plane{c}_{a}", align_bytes=64) for a in range(PASSES)] for c in range(CHUNKS)]
-        d_first = keep.tile([P, WINDOWS, CHUNK], F32, name="d_first")
+        d_lead = keep.tile([P, 1, CHUNK], F32, name="d_lead")
+        d_first = keep.tile([P, WINDOWS - 1, CHUNK], F32, name="d_first")
         d_second = keep.tile([P, WINDOWS - 1, CHUNK], F32, name="d_second")
         d_third = keep.tile([P, WINDOWS - 1, 2 * CHUNK], F32, name="d_third")
         d_last = keep.tile([P, 3 * CHUNK], F32, name="d_last")
@@ -97,16 +98,17 @@ def tile_list_embg_dl_mulP_kernel(tc, dy, w4_words, w4_scales, wd, d, wgo, offs,
                 out=w4_plane[QUAD * q : QUAD * q + 4].bitcast(I32),
                 in_=w4_scales[:, 4 * q : 4 * q + 4, :].rearrange("a r n -> r a n").bitcast(I32),
             )
+        nc.sync.dma_start(out=wgo_rows[0 : J // P, :], in_=wgo[0:1, :].rearrange("o (b m) -> (o b) m", m=P))
         nc.sync.dma_start(out=wd_raw[1][:], in_=wd_rows[1])
         load_dy(0, 1)
-        nc.sync.dma_start(out=wgo_rows[0 : J // P, :], in_=wgo[0:1, :].rearrange("o (b m) -> (o b) m", m=P))
         nc.sync.dma_start(offsets[:], offs)
+        nc.sync.dma_start(out=d_lead[:], in_=d_rows[:, 0:1, cols(0)])
         load_dy(1, 0)
-        nc.sync.dma_start(out=d_first[:], in_=d_rows[:, :, cols(0)])
+        nc.sync.dma_start(out=d_first[:], in_=d_rows[:, 1:WINDOWS, cols(0)])
         load_dy(1, 1)
-        nc.sync.dma_start(out=d_second[:], in_=d_rows[:, 0 : WINDOWS - 1, cols(1)])
         load_dy(2, 0)
         load_dy(2, 1)
+        nc.sync.dma_start(out=d_second[:], in_=d_rows[:, 0 : WINDOWS - 1, cols(1)])
         load_dy(3, 0)
         load_dy(3, 1)
         nc.sync.dma_start(out=d_third[:], in_=d_rows[:, 0 : WINDOWS - 1, cols(2, count=2)])
@@ -117,10 +119,10 @@ def tile_list_embg_dl_mulP_kernel(tc, dy, w4_words, w4_scales, wd, d, wgo, offs,
             interleave(on_vector, wd_grouped[a][:, split:, :], wd_raw[a][:, :, split:])
             nc.vector.quantize_mx(out=wd_codes[a][:].bitcast(E4M3), scales=wd_plane[a][:], in_=flat(wd_grouped[a][:]))
 
-        def group_dy(c, a, behind=None, part=slice(0, CHUNK)):
+        def group_dy(c, a, behind=None, part=slice(0, CHUNK), copy=on_scalar):
             name = f"dy_grouped{c}_{a}_{part.start}"
             grouped = keep.tile([P, part.stop - part.start, PACK], BF16, name=name, tag=behind or name, align_bytes=64)
-            interleave(on_scalar, grouped[:], dy_raw[c][a][:, :, part])
+            interleave(copy, grouped[:], dy_raw[c][a][:, :, part])
             return grouped
 
         def quantize_dy(c, a, grouped, behind=None, part=slice(0, CHUNK)):
@@ -179,11 +181,11 @@ def tile_list_embg_dl_mulP_kernel(tc, dy, w4_words, w4_scales, wd, d, wgo, offs,
         def scatter(s, first, count, rows, d_part):
             nc.vector.tensor_tensor(window[s][:].indirect(offsets[:, cols(first, CHUNK // 16, count)]), rows, d_part, MULT)
 
-        def place(first, count, c, tag, d_part, behind=None, copy=on_scalar):
+        def place(first, count, c, tag, d_part, behind=None, copy=on_scalar, origin=0):
             rows = keep.tile([P, count * CHUNK], F32, name=f"by_row{first}_{c}", tag=behind or f"by_row{first}_{c}", align_bytes=64)
             turn([(first + k, c) for k in range(count)], tag, rows[:], copy)
             for k in range(count):
-                scatter(first + k, c, 1, rows[:, cols(k)], d_part[:, first + k, :])
+                scatter(first + k, c, 1, rows[:, cols(k)], d_part[:, first + k - origin, :])
 
         def store_window(s):
             nc.sync.dma_start(out=out_rows[:, s, :], in_=window[s][:])
@@ -192,9 +194,10 @@ def tile_list_embg_dl_mulP_kernel(tc, dy, w4_words, w4_scales, wd, d, wgo, offs,
 
         prepare_wd(0, HALF)
         prepare_dy(0, 0)
-        prepare_wd(1, 192)
+        prepare_wd(1, 160)
+        blocks = [group_dy(0, 1, part=cols(b, P), copy=copy) for b, copy in enumerate((on_scalar, on_vector))]
         for b in range(BLOCKS):
-            prepare_dy(0, 1, part=cols(b, P))
+            quantize_dy(0, 1, blocks[b], part=cols(b, P))
         nc.tensor.transpose(wgo_bank[:], wgo_rows[:], ident[:])
         nc.scalar.copy(out=wgo_cols[:], in_=wgo_bank[:, 0 : J // P])
 
@@ -202,12 +205,12 @@ def tile_list_embg_dl_mulP_kernel(tc, dy, w4_words, w4_scales, wd, d, wgo, offs,
 
         banks = multiply(0, base_first, (0, 1))
         weigh(0, banks, 0, 1, vector_blocks=(0, 1))
-        place(0, 1, 0, 4, d_first, copy=on_vector)
+        place(0, 1, 0, 4, d_lead, copy=on_vector)
         quantize_dy(1, 0, early, behind="by_token1_0")
         weigh(0, banks, 1, 3, vector_blocks=(1,))
-        place(1, 1, 0, 5, d_first)
+        place(1, 1, 0, 5, d_first, origin=1)
         prepare_dy(1, 1, behind="by_token0_1")
-        place(2, 2, 0, 6, d_first, behind="dy_raw1_1")
+        place(2, 2, 0, 6, d_first, behind="dy_raw1_1", origin=1)
 
         banks = multiply(1, pass_by_pass, (4, 5))
         weigh(1, banks, 0, 1)

@@ -20,22 +20,26 @@ COPY = mybir.ActivationFunctionType.Copy
 
 P = 128
 PACK = 4
-K_PASS = P * PACK
-PASSES = K // K_PASS
+PASSES = K // (P * PACK)
 CHUNK = 256
 CHUNKS = J // CHUNK
 BLOCKS = CHUNK // P
 WINDOWS = N // P
-HALF = N // 2
-QUADS = 4
-QUAD = 32
-QUARTER = T // QUADS
+LAST = WINDOWS - 1
+LIST_ROWS = 16
+QUADRANTS = 4
+QUADRANT = P // QUADRANTS
+SCALE_ROWS = 4
+QUARTERS = 4
+QUARTER = T // QUARTERS
+RUN = 4
+WD_ON_SCALAR = (256, 160)
 
 
 def interleave(copy, grouped, rows):
     copy(
-        out=grouped.rearrange("p (c f) i -> p c i f", f=4),
-        in_=rows.rearrange("p i (c f) -> p c i f", f=4),
+        out=grouped.rearrange("p (c f) i -> p c i f", f=RUN),
+        in_=rows.rearrange("p i (c f) -> p c i f", f=RUN),
     )
 
 
@@ -43,8 +47,8 @@ def flat(grouped):
     return grouped.rearrange("p c i -> p (c i)")
 
 
-def cols(c, width=CHUNK, count=1):
-    return slice(c * width, (c + count) * width)
+def cols(index, width=CHUNK, count=1):
+    return slice(index * width, (index + count) * width)
 
 
 def tile_list_embg_dl_mulP_kernel(tc, dy, w4_words, w4_scales, wd, d, wgo, offs, out_0, out_1, out_2):
@@ -55,7 +59,7 @@ def tile_list_embg_dl_mulP_kernel(tc, dy, w4_words, w4_scales, wd, d, wgo, offs,
         keep = ctx.enter_context(tc.tile_pool(name="keep", bufs=1))
         psum = ctx.enter_context(tc.psum_pool(name="psum", bufs=1))
 
-        offsets = keep.tile([P, J // 16], U16, name="offsets")
+        offsets = keep.tile([P, J // LIST_ROWS], U16, name="offsets")
         w4_codes = keep.tile([P, PASSES, 2 * N], U8, name="w4_codes", align_bytes=64)
         w4_plane = keep.tile([P, PASSES, N], U8, name="w4_plane", align_bytes=64)
         wgo_rows = keep.tile([P, P], F32, name="wgo_rows")
@@ -65,13 +69,16 @@ def tile_list_embg_dl_mulP_kernel(tc, dy, w4_words, w4_scales, wd, d, wgo, offs,
         wd_grouped = [keep.tile([P, N, PACK], BF16, name=f"wd_grouped{a}", align_bytes=64) for a in range(PASSES)]
         wd_codes = [keep.tile([P, N], U32, name=f"wd_codes{a}", align_bytes=64) for a in range(PASSES)]
         wd_plane = [keep.tile([P, N], U8, name=f"wd_plane{a}", align_bytes=64) for a in range(PASSES)]
-        dy_raw = [[keep.tile([P, PACK, CHUNK], F32, name=f"dy_raw{c}_{a}", tag=f"dy_raw{c}_{a}", align_bytes=64) for a in range(PASSES)] for c in range(CHUNKS)]
+        dy_raw = [
+            [keep.tile([P, PACK, CHUNK], F32, name=f"dy_raw{c}_{a}", tag=f"dy_raw{c}_{a}", align_bytes=64) for a in range(PASSES)]
+            for c in range(CHUNKS)
+        ]
         dy_codes = {}
         dy_plane = [[keep.tile([P, CHUNK], U8, name=f"dy_plane{c}_{a}", align_bytes=64) for a in range(PASSES)] for c in range(CHUNKS)]
         d_lead = keep.tile([P, 1, CHUNK], F32, name="d_lead")
-        d_first = keep.tile([P, WINDOWS - 1, CHUNK], F32, name="d_first")
-        d_second = keep.tile([P, WINDOWS - 1, CHUNK], F32, name="d_second")
-        d_third = keep.tile([P, WINDOWS - 1, 2 * CHUNK], F32, name="d_third")
+        d_first = keep.tile([P, LAST, CHUNK], F32, name="d_first")
+        d_second = keep.tile([P, LAST, CHUNK], F32, name="d_second")
+        d_third = keep.tile([P, LAST, 2 * CHUNK], F32, name="d_third")
         d_last = keep.tile([P, 3 * CHUNK], F32, name="d_last")
         window = [keep.tile([P, T], F32, name=f"window{s}") for s in range(WINDOWS)]
         out_plane = keep.tile([P, QUARTER], U8, name="out_plane", align_bytes=64)
@@ -93,10 +100,10 @@ def tile_list_embg_dl_mulP_kernel(tc, dy, w4_words, w4_scales, wd, d, wgo, offs,
         nc.sync.dma_start(out=wd_raw[0][:], in_=wd_rows[0])
         load_dy(0, 0)
         nc.sync.dma_start(out=w4_codes[:].bitcast(I32), in_=w4_words.rearrange("a p c -> p a c").bitcast(I32))
-        for q in range(QUADS):
+        for q in range(QUADRANTS):
             nc.sync.dma_start(
-                out=w4_plane[QUAD * q : QUAD * q + 4].bitcast(I32),
-                in_=w4_scales[:, 4 * q : 4 * q + 4, :].rearrange("a r n -> r a n").bitcast(I32),
+                out=w4_plane[QUADRANT * q : QUADRANT * q + SCALE_ROWS].bitcast(I32),
+                in_=w4_scales[:, cols(q, SCALE_ROWS), :].rearrange("a r n -> r a n").bitcast(I32),
             )
         nc.sync.dma_start(out=wgo_rows[0 : J // P, :], in_=wgo[0:1, :].rearrange("o (b m) -> (o b) m", m=P))
         nc.sync.dma_start(out=wd_raw[1][:], in_=wd_rows[1])
@@ -108,13 +115,14 @@ def tile_list_embg_dl_mulP_kernel(tc, dy, w4_words, w4_scales, wd, d, wgo, offs,
         load_dy(1, 1)
         load_dy(2, 0)
         load_dy(2, 1)
-        nc.sync.dma_start(out=d_second[:], in_=d_rows[:, 0 : WINDOWS - 1, cols(1)])
+        nc.sync.dma_start(out=d_second[:], in_=d_rows[:, 0:LAST, cols(1)])
         load_dy(3, 0)
         load_dy(3, 1)
-        nc.sync.dma_start(out=d_third[:], in_=d_rows[:, 0 : WINDOWS - 1, cols(2, count=2)])
-        nc.sync.dma_start(out=d_last[:], in_=d_rows[:, WINDOWS - 1, cols(1, count=3)])
+        nc.sync.dma_start(out=d_third[:], in_=d_rows[:, 0:LAST, cols(2, count=2)])
+        nc.sync.dma_start(out=d_last[:], in_=d_rows[:, LAST, cols(1, count=3)])
 
-        def prepare_wd(a, split):
+        def prepare_wd(a):
+            split = WD_ON_SCALAR[a]
             interleave(on_scalar, wd_grouped[a][:, :split, :], wd_raw[a][:, :, :split])
             interleave(on_vector, wd_grouped[a][:, split:, :], wd_raw[a][:, :, split:])
             nc.vector.quantize_mx(out=wd_codes[a][:].bitcast(E4M3), scales=wd_plane[a][:], in_=flat(wd_grouped[a][:]))
@@ -131,168 +139,177 @@ def tile_list_embg_dl_mulP_kernel(tc, dy, w4_words, w4_scales, wd, d, wgo, offs,
                 dy_codes[c, a] = keep.tile([P, CHUNK], U32, name=name, tag=behind or name, align_bytes=64)
             nc.vector.quantize_mx(out=dy_codes[c, a][:, part].bitcast(E5M2), scales=dy_plane[c][a][:, part], in_=flat(grouped[:]))
 
-        def prepare_dy(c, a, behind=None, part=slice(0, CHUNK)):
-            quantize_dy(c, a, group_dy(c, a, behind, part), part=part)
+        def prepare_dy(c, a, behind=None):
+            quantize_dy(c, a, group_dy(c, a, behind))
 
-        def multiply(c, order, tags):
-            banks = [psum.tile([P, N], F32, name=f"sums{c}_{b}", tag=f"bank{tags[b]}") for b in range(BLOCKS)]
-            steps = [(step, b) for step in range(2) for b in range(BLOCKS)] + [(step, b) for b in range(BLOCKS) for step in range(2, 4)]
+        def multiply(c, order, bank_numbers):
+            banks = [psum.tile([P, N], F32, name=f"sums{c}_{b}", tag=f"bank{bank_numbers[b]}") for b in range(BLOCKS)]
+            half = len(order) // 2
+            steps = [(step, b) for step in range(half) for b in range(BLOCKS)]
+            steps = steps + [(step, b) for b in range(BLOCKS) for step in range(half, len(order))]
             for step, b in steps:
-                for codes, plane, a in order[step : step + 1]:
-                    tokens = cols(b, P)
-                    nc.tensor.matmul_mx(
-                        out=banks[b][:],
-                        lhsT=dy_codes[c, a][:, tokens].bitcast(E5M2),
-                        lhsT_scale=dy_plane[c][a][:, tokens],
-                        rhs=codes,
-                        rhs_scale=plane,
-                        start=(step == 0),
-                        stop=(step == len(order) - 1),
-                    )
+                codes, plane, a = order[step]
+                tokens = cols(b, P)
+                nc.tensor.matmul_mx(
+                    out=banks[b][:],
+                    lhsT=dy_codes[c, a][:, tokens].bitcast(E5M2),
+                    lhsT_scale=dy_plane[c][a][:, tokens],
+                    rhs=codes,
+                    rhs_scale=plane,
+                    start=(step == 0),
+                    stop=(step == len(order) - 1),
+                )
             return banks
 
         w4_pass = [(w4_codes[:, a, :].bitcast(E2M1), w4_plane[:, a, :], a) for a in range(PASSES)]
         wd_pass = [(wd_codes[a][:].bitcast(E4M3), wd_plane[a][:], a) for a in range(PASSES)]
-        base_first = [wd_pass[0], w4_pass[0], wd_pass[1], w4_pass[1]]
-        pass_by_pass = [w4_pass[0], wd_pass[0], w4_pass[1], wd_pass[1]]
+        wd_first = [wd_pass[0], w4_pass[0], wd_pass[1], w4_pass[1]]
+        w4_first = [w4_pass[0], wd_pass[0], w4_pass[1], wd_pass[1]]
 
         by_token = {}
 
-        def weigh(c, banks, first=0, count=WINDOWS, vector_blocks=()):
+        def weigh(c, banks, first_window, count, vector_blocks=()):
             for b in range(BLOCKS):
                 block = BLOCKS * c + b
                 weight = wgo_cols[:, block : block + 1]
-                weighed = keep.tile([P, count, P], F32, name=f"by_token{block}_{first}", tag=f"by_token{block}_{first}", align_bytes=64)
-                sums = banks[b][:].rearrange("j (m s) -> j s m", s=WINDOWS)[:, first : first + count, :]
+                name = f"by_token{block}_{first_window}"
+                weighed = keep.tile([P, count, P], F32, name=name, tag=name, align_bytes=64)
+                sums = banks[b][:].rearrange("j (m s) -> j s m", s=WINDOWS)[:, first_window : first_window + count, :]
                 if b in vector_blocks:
                     nc.vector.tensor_scalar(out=weighed[:], in0=sums, scalar1=weight, scalar2=None, op0=MULT)
                 else:
                     nc.scalar.activation(out=weighed[:], in_=sums, func=COPY, scale=weight)
                 for s in range(count):
-                    by_token[block, first + s] = weighed[:, s, :]
+                    by_token[block, first_window + s] = weighed[:, s, :]
 
-        def turn(pieces, tag, rows, copy=on_scalar):
-            bank = psum.tile([P, len(pieces) * CHUNK], F32, name=f"turned{pieces[0][0]}_{pieces[0][1]}", tag=f"bank{tag}")
+        def turn(pieces, bank_number, rows, copy=on_scalar):
+            bank = psum.tile([P, len(pieces) * CHUNK], F32, name=f"turned{pieces[0][0]}_{pieces[0][1]}", tag=f"bank{bank_number}")
             for k, (s, c) in enumerate(pieces):
                 for b in range(BLOCKS):
                     nc.tensor.transpose(bank[:, cols(BLOCKS * k + b, P)], by_token[BLOCKS * c + b, s], ident[:])
             copy(out=rows, in_=bank[:])
 
-        def scatter(s, first, count, rows, d_part):
-            nc.vector.tensor_tensor(window[s][:].indirect(offsets[:, cols(first, CHUNK // 16, count)]), rows, d_part, MULT)
+        def scatter(s, first_chunk, count, rows, d_part):
+            entries = offsets[:, cols(first_chunk, CHUNK // LIST_ROWS, count)]
+            nc.vector.tensor_tensor(window[s][:].indirect(entries), rows, d_part, MULT)
 
-        def place(first, count, c, tag, d_part, behind=None, copy=on_scalar, origin=0):
-            rows = keep.tile([P, count * CHUNK], F32, name=f"by_row{first}_{c}", tag=behind or f"by_row{first}_{c}", align_bytes=64)
-            turn([(first + k, c) for k in range(count)], tag, rows[:], copy)
+        def place(first_window, count, c, bank_number, d_part, behind=None, copy=on_scalar, origin=0):
+            name = f"by_row{first_window}_{c}"
+            rows = keep.tile([P, count * CHUNK], F32, name=name, tag=behind or name, align_bytes=64)
+            turn([(first_window + k, c) for k in range(count)], bank_number, rows[:], copy)
             for k in range(count):
-                scatter(first + k, c, 1, rows[:, cols(k)], d_part[:, first + k - origin, :])
+                scatter(first_window + k, c, 1, rows[:, cols(k)], d_part[:, first_window + k - origin, :])
 
         def store_window(s):
             nc.sync.dma_start(out=out_rows[:, s, :], in_=window[s][:])
 
         wgo_bank = psum.tile([P, P], F32, name="wgo_bank", tag="bank7")
 
-        prepare_wd(0, HALF)
+        prepare_wd(0)
         prepare_dy(0, 0)
-        prepare_wd(1, 160)
-        blocks = [group_dy(0, 1, part=cols(b, P), copy=copy) for b, copy in enumerate((on_scalar, on_vector))]
+        prepare_wd(1)
+        halves_of_chunk = [group_dy(0, 1, part=cols(b, P), copy=copy) for b, copy in enumerate((on_scalar, on_vector))]
         for b in range(BLOCKS):
-            quantize_dy(0, 1, blocks[b], part=cols(b, P))
+            quantize_dy(0, 1, halves_of_chunk[b], part=cols(b, P))
         nc.tensor.transpose(wgo_bank[:], wgo_rows[:], ident[:])
         nc.scalar.copy(out=wgo_cols[:], in_=wgo_bank[:, 0 : J // P])
 
         early = group_dy(1, 0)
 
-        banks = multiply(0, base_first, (0, 1))
+        banks = multiply(0, wd_first, (0, 1))
         weigh(0, banks, 0, 1, vector_blocks=(0, 1))
         place(0, 1, 0, 4, d_lead, copy=on_vector)
         quantize_dy(1, 0, early, behind="by_token1_0")
-        weigh(0, banks, 1, 3, vector_blocks=(1,))
+        weigh(0, banks, 1, LAST, vector_blocks=(1,))
         place(1, 1, 0, 5, d_first, origin=1)
         prepare_dy(1, 1, behind="by_token0_1")
         place(2, 2, 0, 6, d_first, behind="dy_raw1_1", origin=1)
 
-        banks = multiply(1, pass_by_pass, (4, 5))
+        banks = multiply(1, w4_first, (4, 5))
         weigh(1, banks, 0, 1)
         prepare_dy(2, 0, behind="by_token0_1")
         prepare_dy(2, 1, behind="dy_raw2_0")
         place(0, 1, 1, 7, d_second, behind="dy_raw2_1")
-        weigh(1, banks, 1, 3)
+        weigh(1, banks, 1, LAST)
         place(1, 1, 1, 0, d_second)
         prepare_dy(3, 0, behind="dy_codes1_1")
         prepare_dy(3, 1, behind="dy_raw3_0")
         place(2, 1, 1, 1, d_second, behind="dy_raw3_1")
 
-        banks = multiply(2, pass_by_pass, (7, 0))
+        banks = multiply(2, w4_first, (7, 0))
         weigh(2, banks, 0, 1)
         place(0, 1, 2, 2, d_third[:, :, cols(0)])
-        weigh(2, banks, 1, 3)
+        weigh(2, banks, 1, LAST)
         place(1, 1, 2, 3, d_third[:, :, cols(0)])
 
-        banks = multiply(3, pass_by_pass, (2, 1))
+        banks = multiply(3, w4_first, (2, 1))
         weigh(3, banks, 0, 1)
         place(0, 1, 3, 4, d_third[:, :, cols(1)])
         store_window(0)
-        weigh(3, banks, 1, 3)
+        weigh(3, banks, 1, LAST)
         place(1, 1, 3, 6, d_third[:, :, cols(1)])
         store_window(1)
         late_rows = keep.tile([P, 2 * CHUNK], F32, name="late_rows", tag="late_rows")
         turn([(2, 2), (2, 3)], 5, late_rows[:])
         scatter(2, 2, 2, late_rows[:], d_third[:, 2, :])
         store_window(2)
-        last = WINDOWS - 1
-        last_rows = keep.tile([P, 2 * CHUNK], F32, name="last_rows")
-        turn([(last, 1), (last, 2)], 0, last_rows[:])
-        scatter(last, 1, 2, last_rows[:], d_last[:, cols(0, count=2)])
+        last_rows = keep.tile([P, 3 * CHUNK], F32, name="last_rows")
+        turn([(LAST, 1), (LAST, 2)], 0, last_rows[:, cols(0, count=2)])
+        turn([(LAST, 3)], 7, last_rows[:, cols(2)])
+        scatter(LAST, 1, 3, last_rows[:], d_last[:])
+        store_window(LAST)
 
-        pairs = [keep.tile([P, 2, QUARTER, 2], BF16, name=f"pairs{c}") for c in range(QUADS)]
-        out_grouped = [keep.tile([P, QUARTER, PACK], BF16, name=f"out_grouped{c}", align_bytes=64) for c in range(QUADS)]
-        out_codes = [keep.tile([P, QUARTER], U32, name=f"out_codes{c}", align_bytes=64) for c in range(QUADS)]
+        shares = [
+            keep.tile([P, 2, 2, QUARTER, 2], BF16, name=f"pairs{k}", tag=tag, align_bytes=64)
+            for k, tag in enumerate(("by_token7_1", "by_token6_1"))
+        ]
+        out_grouped = [keep.tile([P, QUARTER, PACK], BF16, name=f"out_grouped{c}", align_bytes=64) for c in range(QUARTERS)]
+        out_codes = [keep.tile([P, QUARTER], U32, name=f"out_codes{c}", align_bytes=64) for c in range(QUARTERS)]
 
-        def round_plane(copy, s, c):
-            copy(out=pairs[c][:, s // 2, :, s % 2], in_=window[s][:, cols(c, QUARTER)])
+        def share_of(s, k):
+            return window[s][:, cols(k, T // 2)].rearrange("p (g c) -> p g c", g=2)
 
-        def group_out(copy, c, part=slice(0, QUARTER)):
-            words = pairs[c][:].rearrange("p h c e -> p (h c e)").bitcast(F32).rearrange("p (h c) -> p c h", h=2)
-            copy(out=flat(out_grouped[c][:]).bitcast(F32).rearrange("p (c h) -> p c h", h=2)[:, part, :], in_=words[:, part, :])
+        def round_share(s, k):
+            on_scalar(out=shares[k][:, :, s // 2, :, s % 2], in_=share_of(s, k))
+
+        def round_quarter(copy, s, c):
+            copy(out=shares[c // 2][:, c % 2][:, s // 2, :, s % 2], in_=window[s][:, cols(c, QUARTER)])
+
+        def join(copy, c, part=slice(0, QUARTER)):
+            pairs = shares[c // 2][:, c % 2].rearrange("p h c e -> p (h c e)").bitcast(F32).rearrange("p (h c) -> p c h", h=2)
+            copy(out=flat(out_grouped[c][:]).bitcast(F32).rearrange("p (c h) -> p c h", h=2)[:, part, :], in_=pairs[:, part, :])
 
         def quantize_out(c, part=slice(0, QUARTER)):
             nc.vector.quantize_mx(
-                out=out_codes[c][:, part].bitcast(E4M3), scales=out_plane[4 * c :, part], in_=flat(out_grouped[c][:, part, :])
+                out=out_codes[c][:, part].bitcast(E4M3), scales=out_plane[SCALE_ROWS * c :, part], in_=flat(out_grouped[c][:, part, :])
             )
             nc.sync.dma_start(
                 out=out_1[0][:, cols(c, QUARTER), :][:, part, :].rearrange("p c i -> p (c i)").bitcast(I32),
                 in_=out_codes[c][:, part].bitcast(I32),
             )
 
-        for s, quarters in ((0, range(QUADS)), (1, (0, 2)), (2, (0, 2))):
-            for c in quarters:
-                round_plane(on_scalar, s, c)
-        final_rows = keep.tile([P, CHUNK], F32, name="final_rows", tag="late_rows")
-        turn([(last, 3)], 7, final_rows[:])
-        scatter(last, 3, 1, final_rows[:], d_last[:, cols(2)])
-        store_window(last)
-        for s in (1, 2):
-            for c in (1, 3):
-                round_plane(on_scalar, s, c)
+        for s in (0, 1):
+            for k in range(len(shares)):
+                round_share(s, k)
+        on_scalar(out=shares[0][:, :, 1, :, :], in_=share_of(2, 0).unsqueeze(3).to_broadcast([P, 2, QUARTER, 2]))
+        round_share(2, 1)
         halves = [cols(h, QUARTER // 2) for h in range(2)]
-        round_plane(on_scalar, last, 1)
-        round_plane(on_vector, last, 0)
-        round_plane(on_vector, last, 2)
-        group_out(on_scalar, 1)
-        group_out(on_vector, 0)
-        group_out(on_vector, 2)
-        round_plane(on_scalar, last, 3)
+        for c in (0, 1):
+            round_quarter(on_vector, LAST, c)
+        for c in (0, 1):
+            join(on_vector, c)
+        for c in (2, 3):
+            round_quarter(on_scalar, LAST, c)
+        join(on_scalar, 2)
         for part in halves:
-            group_out(on_scalar, 3, part)
-        quantize_out(0)
-        quantize_out(1)
-        quantize_out(2)
+            join(on_scalar, 3, part)
+        for c in (0, 1, 2):
+            quantize_out(c)
         for part in halves:
             quantize_out(3, part)
-        for q in range(QUADS):
+        for q in range(QUADRANTS):
             queue = nc.scalar if q % 2 == 0 else nc.sync
             queue.dma_start(
-                out=out_2[0][4 * q : 4 * q + 4, :].rearrange("r (c n) -> c r n", c=QUADS).bitcast(I32),
-                in_=out_plane[QUAD * q : QUAD * q + 4 * QUADS, :].bitcast(I32),
+                out=out_2[0][cols(q, SCALE_ROWS), :].rearrange("r (c n) -> c r n", c=QUARTERS).bitcast(I32),
+                in_=out_plane[QUADRANT * q : QUADRANT * q + SCALE_ROWS * QUARTERS, :].bitcast(I32),
             )

@@ -33,13 +33,20 @@ SCALE_ROWS = 4
 QUARTERS = 4
 QUARTER = T // QUARTERS
 RUN = 4
-WD_ON_SCALAR = (256, 160)
+LEAD = 2
 
 
 def interleave(copy, grouped, rows):
     copy(
         out=grouped.rearrange("p (c f) i -> p c i f", f=RUN),
         in_=rows.rearrange("p i (c f) -> p c i f", f=RUN),
+    )
+
+
+def deal(copy, grouped, rows, part):
+    copy(
+        out=grouped.rearrange("p s m i -> p m i s"),
+        in_=rows.rearrange("p i (m s) -> p m i s", s=WINDOWS)[:, :, :, part],
     )
 
 
@@ -62,11 +69,16 @@ def tile_list_embg_dl_mulP_kernel(tc, dy, w4_words, w4_scales, wd, d, wgo, offs,
         offsets = keep.tile([P, J // LIST_ROWS], U16, name="offsets")
         w4_codes = keep.tile([P, PASSES, 2 * N], U8, name="w4_codes", align_bytes=64)
         w4_plane = keep.tile([P, PASSES, N], U8, name="w4_plane", align_bytes=64)
+        w4_codes_raw = keep.tile([P, PASSES, 2 * N], U8, name="w4_codes_raw", align_bytes=64)
+        w4_plane_raw = keep.tile([P, PASSES, N], U8, name="w4_plane_raw", align_bytes=64)
+        wgo_lead = keep.tile([P, CHUNK], F32, name="wgo_lead")
         wgo_rows = keep.tile([P, P], F32, name="wgo_rows")
-        wgo_cols = keep.tile([P, J // P], F32, name="wgo_cols")
         ident = keep.tile([P, P], F32, name="ident")
         wd_raw = [keep.tile([P, PACK, N], F32, name=f"wd_raw{a}") for a in range(PASSES)]
-        wd_grouped = [keep.tile([P, N, PACK], BF16, name=f"wd_grouped{a}", align_bytes=64) for a in range(PASSES)]
+        wd_grouped = [
+            [keep.tile([P, LEAD, P, PACK], BF16, name=f"wd_grouped{a}_{h}", align_bytes=64) for h in range(WINDOWS // LEAD)]
+            for a in range(PASSES)
+        ]
         wd_codes = [keep.tile([P, N], U32, name=f"wd_codes{a}", align_bytes=64) for a in range(PASSES)]
         wd_plane = [keep.tile([P, N], U8, name=f"wd_plane{a}", align_bytes=64) for a in range(PASSES)]
         dy_raw = [
@@ -75,8 +87,8 @@ def tile_list_embg_dl_mulP_kernel(tc, dy, w4_words, w4_scales, wd, d, wgo, offs,
         ]
         dy_codes = {}
         dy_plane = [[keep.tile([P, CHUNK], U8, name=f"dy_plane{c}_{a}", align_bytes=64) for a in range(PASSES)] for c in range(CHUNKS)]
-        d_lead = keep.tile([P, 1, CHUNK], F32, name="d_lead")
-        d_first = keep.tile([P, LAST, CHUNK], F32, name="d_first")
+        d_lead = [keep.tile([P, CHUNK], F32, name=f"d_lead{s}") for s in range(LEAD)]
+        d_first = keep.tile([P, WINDOWS - LEAD, CHUNK], F32, name="d_first")
         d_second = keep.tile([P, LAST, CHUNK], F32, name="d_second")
         d_third = keep.tile([P, LAST, 2 * CHUNK], F32, name="d_third")
         d_last = keep.tile([P, 3 * CHUNK], F32, name="d_last")
@@ -91,28 +103,30 @@ def tile_list_embg_dl_mulP_kernel(tc, dy, w4_words, w4_scales, wd, d, wgo, offs,
         def load_dy(c, a):
             nc.sync.dma_start(out=dy_raw[c][a][:], in_=dy_rows[a][:, :, cols(c)])
 
-        nc.gpsimd.memset(w4_plane[:].rearrange("p a n -> p (a n)").bitcast(I32), 0)
+        nc.gpsimd.memset(w4_plane_raw[:].rearrange("p a n -> p (a n)").bitcast(I32), 0)
         nc.gpsimd.memset(wgo_rows[:], 0.0)
         make_identity(nc, ident[:])
         for s in range(WINDOWS):
             nc.vector.memset(window[s][:], 0.0)
 
+        nc.sync.dma_start(out=w4_codes_raw[:].bitcast(I32), in_=w4_words.rearrange("a p c -> p a c").bitcast(I32))
         nc.sync.dma_start(out=wd_raw[0][:], in_=wd_rows[0])
-        load_dy(0, 0)
-        nc.sync.dma_start(out=w4_codes[:].bitcast(I32), in_=w4_words.rearrange("a p c -> p a c").bitcast(I32))
         for q in range(QUADRANTS):
             nc.sync.dma_start(
-                out=w4_plane[QUADRANT * q : QUADRANT * q + SCALE_ROWS].bitcast(I32),
+                out=w4_plane_raw[QUADRANT * q : QUADRANT * q + SCALE_ROWS].bitcast(I32),
                 in_=w4_scales[:, cols(q, SCALE_ROWS), :].rearrange("a r n -> r a n").bitcast(I32),
             )
+        load_dy(0, 0)
         nc.sync.dma_start(out=wgo_rows[0 : J // P, :], in_=wgo[0:1, :].rearrange("o (b m) -> (o b) m", m=P))
         nc.sync.dma_start(out=wd_raw[1][:], in_=wd_rows[1])
         load_dy(0, 1)
+        nc.sync.dma_start(out=wgo_lead[:], in_=wgo[:, cols(0)])
         nc.sync.dma_start(offsets[:], offs)
-        nc.sync.dma_start(out=d_lead[:], in_=d_rows[:, 0:1, cols(0)])
+        nc.sync.dma_start(out=d_lead[0][:], in_=d_rows[:, 0, cols(0)])
         load_dy(1, 0)
-        nc.sync.dma_start(out=d_first[:], in_=d_rows[:, 1:WINDOWS, cols(0)])
+        nc.sync.dma_start(out=d_lead[1][:], in_=d_rows[:, 1, cols(0)])
         load_dy(1, 1)
+        nc.sync.dma_start(out=d_first[:], in_=d_rows[:, LEAD:WINDOWS, cols(0)])
         load_dy(2, 0)
         load_dy(2, 1)
         nc.sync.dma_start(out=d_second[:], in_=d_rows[:, 0:LAST, cols(1)])
@@ -122,10 +136,16 @@ def tile_list_embg_dl_mulP_kernel(tc, dy, w4_words, w4_scales, wd, d, wgo, offs,
         nc.sync.dma_start(out=d_last[:], in_=d_rows[:, LAST, cols(1, count=3)])
 
         def prepare_wd(a):
-            split = WD_ON_SCALAR[a]
-            interleave(on_scalar, wd_grouped[a][:, :split, :], wd_raw[a][:, :, :split])
-            interleave(on_vector, wd_grouped[a][:, split:, :], wd_raw[a][:, :, split:])
-            nc.vector.quantize_mx(out=wd_codes[a][:].bitcast(E4M3), scales=wd_plane[a][:], in_=flat(wd_grouped[a][:]))
+            for h, copy in enumerate((on_vector, on_scalar)):
+                deal(copy, wd_grouped[a][h][:], wd_raw[a][:], cols(h, LEAD))
+
+        def quantize_wd(a, h):
+            part = cols(h, LEAD * P)
+            nc.vector.quantize_mx(
+                out=wd_codes[a][:, part].bitcast(E4M3),
+                scales=wd_plane[a][:, part],
+                in_=wd_grouped[a][h][:].rearrange("p s m i -> p (s m i)"),
+            )
 
         def group_dy(c, a, behind=None, part=slice(0, CHUNK), copy=on_scalar):
             name = f"dy_grouped{c}_{a}_{part.start}"
@@ -154,40 +174,78 @@ def tile_list_embg_dl_mulP_kernel(tc, dy, w4_words, w4_scales, wd, d, wgo, offs,
                     out=banks[b][:],
                     lhsT=dy_codes[c, a][:, tokens].bitcast(E5M2),
                     lhsT_scale=dy_plane[c][a][:, tokens],
-                    rhs=codes,
-                    rhs_scale=plane,
+                    rhs=codes(0, WINDOWS),
+                    rhs_scale=plane[:, :],
                     start=(step == 0),
                     stop=(step == len(order) - 1),
                 )
             return banks
 
-        w4_pass = [(w4_codes[:, a, :].bitcast(E2M1), w4_plane[:, a, :], a) for a in range(PASSES)]
-        wd_pass = [(wd_codes[a][:].bitcast(E4M3), wd_plane[a][:], a) for a in range(PASSES)]
+        def w4_columns(a):
+            return lambda s, count: w4_codes[:, a, 2 * P * s : 2 * P * (s + count)].bitcast(E2M1)
+
+        def wd_columns(a):
+            return lambda s, count: wd_codes[a][:, P * s : P * (s + count)].bitcast(E4M3)
+
+        w4_pass = [(w4_columns(a), w4_plane[:, a, :], a) for a in range(PASSES)]
+        wd_pass = [(wd_columns(a), wd_plane[a][:], a) for a in range(PASSES)]
         wd_first = [wd_pass[0], w4_pass[0], wd_pass[1], w4_pass[1]]
         w4_first = [w4_pass[0], wd_pass[0], w4_pass[1], wd_pass[1]]
 
         by_token = {}
 
-        def weigh(c, banks, first_window, count, vector_blocks=()):
-            for b in range(BLOCKS):
+        def multiply_first(order, lead_banks, bank_numbers):
+            leads = [psum.tile([P, CHUNK], F32, name=f"lead{s}", tag=f"bank{lead_banks[s]}") for s in range(LEAD)]
+            rest = WINDOWS - LEAD
+            banks = [psum.tile([P, rest * P], F32, name=f"sums0_{b}", tag=f"bank{bank_numbers[b]}") for b in range(BLOCKS)]
+            half = len(order) // 2
+            for steps in (range(half), range(half, len(order))):
+                for s in range(LEAD):
+                    for step in steps:
+                        codes, plane, a = order[step]
+                        nc.tensor.matmul_mx(
+                            out=leads[s][:],
+                            lhsT=codes(s, 1),
+                            lhsT_scale=plane[:, cols(s, P)],
+                            rhs=dy_codes[0, a][:].bitcast(E5M2),
+                            rhs_scale=dy_plane[0][a][:],
+                            start=(step == 0),
+                            stop=(step == len(order) - 1),
+                        )
+                for b in range(BLOCKS):
+                    for step in steps:
+                        codes, plane, a = order[step]
+                        nc.tensor.matmul_mx(
+                            out=banks[b][:],
+                            lhsT=dy_codes[0, a][:, cols(b, P)].bitcast(E5M2),
+                            lhsT_scale=dy_plane[0][a][:, cols(b, P)],
+                            rhs=codes(LEAD, rest),
+                            rhs_scale=plane[:, cols(LEAD, P, rest)],
+                            start=(step == 0),
+                            stop=(step == len(order) - 1),
+                        )
+            return leads, banks
+
+        def weigh(c, banks, first_window, count, origin=0, blocks=range(BLOCKS)):
+            for b in blocks:
                 block = BLOCKS * c + b
                 weight = wgo_cols[:, block : block + 1]
                 name = f"by_token{block}_{first_window}"
                 weighed = keep.tile([P, count, P], F32, name=name, tag=name, align_bytes=64)
-                sums = banks[b][:].rearrange("j (m s) -> j s m", s=WINDOWS)[:, first_window : first_window + count, :]
-                if b in vector_blocks:
-                    nc.vector.tensor_scalar(out=weighed[:], in0=sums, scalar1=weight, scalar2=None, op0=MULT)
-                else:
-                    nc.scalar.activation(out=weighed[:], in_=sums, func=COPY, scale=weight)
+                sums = banks[b][:, cols(first_window - origin, P, count)]
+                nc.scalar.activation(out=weighed[:].rearrange("j s m -> j (s m)"), in_=sums, func=COPY, scale=weight)
                 for s in range(count):
                     by_token[block, first_window + s] = weighed[:, s, :]
 
-        def turn(pieces, bank_number, rows, copy=on_scalar):
+        def transpose(pieces, bank_number):
             bank = psum.tile([P, len(pieces) * CHUNK], F32, name=f"turned{pieces[0][0]}_{pieces[0][1]}", tag=f"bank{bank_number}")
-            for k, (s, c) in enumerate(pieces):
-                for b in range(BLOCKS):
-                    nc.tensor.transpose(bank[:, cols(BLOCKS * k + b, P)], by_token[BLOCKS * c + b, s], ident[:])
-            copy(out=rows, in_=bank[:])
+            steps = sorted((BLOCKS * c + b, k, b, s) for k, (s, c) in enumerate(pieces) for b in range(BLOCKS))
+            for block, k, b, s in steps:
+                nc.tensor.transpose(bank[:, cols(BLOCKS * k + b, P)], by_token[block, s], ident[:])
+            return bank
+
+        def turn(pieces, bank_number, rows, copy=on_scalar):
+            copy(out=rows, in_=transpose(pieces, bank_number)[:])
 
         def scatter(s, first_chunk, count, rows, d_part):
             entries = offsets[:, cols(first_chunk, CHUNK // LIST_ROWS, count)]
@@ -205,29 +263,53 @@ def tile_list_embg_dl_mulP_kernel(tc, dy, w4_words, w4_scales, wd, d, wgo, offs,
 
         wgo_bank = psum.tile([P, P], F32, name="wgo_bank", tag="bank7")
 
+        on_scalar(
+            out=w4_codes[:].bitcast(U16).rearrange("p a (s m) -> p a s m", s=WINDOWS),
+            in_=w4_codes_raw[:].bitcast(U16).rearrange("p a (m s) -> p a s m", s=WINDOWS),
+        )
         prepare_wd(0)
+        on_vector(
+            out=w4_plane[:].rearrange("p a (s m) -> p a s m", s=WINDOWS),
+            in_=w4_plane_raw[:].rearrange("p a (m s) -> p a s m", s=WINDOWS),
+        )
+        quantize_wd(0, 0)
+        quantize_wd(0, 1)
         prepare_dy(0, 0)
         prepare_wd(1)
+        quantize_wd(1, 0)
         halves_of_chunk = [group_dy(0, 1, part=cols(b, P), copy=copy) for b, copy in enumerate((on_scalar, on_vector))]
+        quantize_wd(1, 1)
         for b in range(BLOCKS):
             quantize_dy(0, 1, halves_of_chunk[b], part=cols(b, P))
+        early = group_dy(1, 0)
         nc.tensor.transpose(wgo_bank[:], wgo_rows[:], ident[:])
+        wgo_cols = keep.tile([P, J // P], F32, name="wgo_cols", tag="dy_raw1_0", align_bytes=64)
         nc.scalar.copy(out=wgo_cols[:], in_=wgo_bank[:, 0 : J // P])
 
-        early = group_dy(1, 0)
+        leads, banks = multiply_first(wd_first, (4, 5), (0, 1))
+        def weigh_lead(s, behind=None):
+            name = f"lead_rows{s}"
+            rows = keep.tile([P, CHUNK], F32, name=name, tag=behind or name, align_bytes=64)
+            nc.vector.tensor_tensor(rows[:], leads[s][:], wgo_lead[:], MULT)
+            return rows
 
-        banks = multiply(0, wd_first, (0, 1))
-        weigh(0, banks, 0, 1, vector_blocks=(0, 1))
-        place(0, 1, 0, 4, d_lead, copy=on_vector)
-        quantize_dy(1, 0, early, behind="by_token1_0")
-        weigh(0, banks, 1, LAST, vector_blocks=(1,))
-        place(1, 1, 0, 5, d_first, origin=1)
-        prepare_dy(1, 1, behind="by_token0_1")
-        place(2, 2, 0, 6, d_first, behind="dy_raw1_1", origin=1)
+        scatter(0, 0, 1, weigh_lead(0)[:], d_lead[0][:])
+        weigh(0, banks, 2, 1, origin=LEAD, blocks=(0,))
+        weigh(0, banks, 3, 1, origin=LEAD, blocks=(0,))
+        weigh(0, banks, 2, 2, origin=LEAD, blocks=(1,))
+        first_bank = transpose([(2, 0), (3, 0)], 6)
+        second_rows = weigh_lead(1, behind="by_token0_2")
+        quantize_dy(1, 0, early, behind="by_token0_3")
+        scatter(1, 0, 1, second_rows[:], d_lead[1][:])
+        prepare_dy(1, 1, behind="by_token1_2")
+        first_rows = keep.tile([P, 2 * CHUNK], F32, name="first_rows", tag="dy_raw1_1", align_bytes=64)
+        on_scalar(out=first_rows[:], in_=first_bank[:])
+        for k in range(2):
+            scatter(2 + k, 0, 1, first_rows[:, cols(k)], d_first[:, k, :])
 
         banks = multiply(1, w4_first, (4, 5))
         weigh(1, banks, 0, 1)
-        prepare_dy(2, 0, behind="by_token0_1")
+        prepare_dy(2, 0, behind="by_token1_2")
         prepare_dy(2, 1, behind="dy_raw2_0")
         place(0, 1, 1, 7, d_second, behind="dy_raw2_1")
         weigh(1, banks, 1, LAST)

@@ -33,6 +33,7 @@ SCALE_ROWS = 4
 QUARTERS = 4
 QUARTER = T // QUARTERS
 RUN = 4
+WHOLE = 16
 LEAD = 2
 
 
@@ -162,24 +163,22 @@ def tile_list_embg_dl_mulP_kernel(tc, dy, w4_words, w4_scales, wd, d, wgo, offs,
         def prepare_dy(c, a, behind=None):
             quantize_dy(c, a, group_dy(c, a, behind))
 
-        def multiply(c, order, bank_numbers):
-            banks = [psum.tile([P, N], F32, name=f"sums{c}_{b}", tag=f"bank{bank_numbers[b]}") for b in range(BLOCKS)]
-            half = len(order) // 2
-            steps = [(step, b) for step in range(half) for b in range(BLOCKS)]
-            steps = steps + [(step, b) for b in range(BLOCKS) for step in range(half, len(order))]
-            for step, b in steps:
+        def sums(c, first_window, count, bank_number):
+            return psum.tile([P, BLOCKS, count * P], F32, name=f"sums{c}_{first_window}", tag=f"bank{bank_number}")
+
+        def multiply(c, first_window, count, bank, order, steps):
+            for step in steps:
                 codes, plane, a = order[step]
-                tokens = cols(b, P)
-                nc.tensor.matmul_mx(
-                    out=banks[b][:],
-                    lhsT=dy_codes[c, a][:, tokens].bitcast(E5M2),
-                    lhsT_scale=dy_plane[c][a][:, tokens],
-                    rhs=codes(0, WINDOWS),
-                    rhs_scale=plane[:, :],
-                    start=(step == 0),
-                    stop=(step == len(order) - 1),
-                )
-            return banks
+                for b in range(BLOCKS):
+                    nc.tensor.matmul_mx(
+                        out=bank[:, b, :],
+                        lhsT=dy_codes[c, a][:, cols(b, P)].bitcast(E5M2),
+                        lhsT_scale=dy_plane[c][a][:, cols(b, P)],
+                        rhs=codes(first_window, count),
+                        rhs_scale=plane[:, cols(first_window, P, count)],
+                        start=(step == 0 and b == 0),
+                        stop=(step == len(order) - 1 and b == BLOCKS - 1),
+                    )
 
         def w4_columns(a):
             return lambda s, count: w4_codes[:, a, 2 * P * s : 2 * P * (s + count)].bitcast(E2M1)
@@ -277,10 +276,11 @@ def tile_list_embg_dl_mulP_kernel(tc, dy, w4_words, w4_scales, wd, d, wgo, offs,
         prepare_dy(0, 0)
         prepare_wd(1)
         quantize_wd(1, 0)
-        halves_of_chunk = [group_dy(0, 1, part=cols(b, P), copy=copy) for b, copy in enumerate((on_scalar, on_vector))]
+        last_landing = keep.tile([P, CHUNK, PACK], BF16, name="last_landing", align_bytes=64)
+        for b, copy in enumerate((on_scalar, on_vector)):
+            interleave(copy, last_landing[:, cols(b, P), :], dy_raw[0][1][:, :, cols(b, P)])
         quantize_wd(1, 1)
-        for b in range(BLOCKS):
-            quantize_dy(0, 1, halves_of_chunk[b], part=cols(b, P))
+        quantize_dy(0, 1, last_landing)
         early = group_dy(1, 0)
         nc.tensor.transpose(wgo_bank[:], wgo_rows[:], ident[:])
         wgo_cols = keep.tile([P, J // P], F32, name="wgo_cols", tag="dy_raw1_0", align_bytes=64)
@@ -296,54 +296,77 @@ def tile_list_embg_dl_mulP_kernel(tc, dy, w4_words, w4_scales, wd, d, wgo, offs,
         scatter(0, 0, 1, weigh_lead(0)[:], d_lead[0][:])
         weigh(0, banks, 2, 1, origin=LEAD, blocks=(0,))
         weigh(0, banks, 3, 1, origin=LEAD, blocks=(0,))
-        weigh(0, banks, 2, 2, origin=LEAD, blocks=(1,))
+        weigh(0, banks, 2, 1, origin=LEAD, blocks=(1,))
+        weigh(0, banks, 3, 1, origin=LEAD, blocks=(1,))
         first_bank = transpose([(2, 0), (3, 0)], 6)
         second_rows = weigh_lead(1, behind="by_token0_2")
         quantize_dy(1, 0, early, behind="by_token0_3")
         scatter(1, 0, 1, second_rows[:], d_lead[1][:])
         prepare_dy(1, 1, behind="by_token1_2")
-        first_rows = keep.tile([P, 2 * CHUNK], F32, name="first_rows", tag="dy_raw1_1", align_bytes=64)
+        first_rows = keep.tile([P, 2 * CHUNK], F32, name="first_rows", align_bytes=64)
         on_scalar(out=first_rows[:], in_=first_bank[:])
         for k in range(2):
             scatter(2 + k, 0, 1, first_rows[:, cols(k)], d_first[:, k, :])
 
-        banks = multiply(1, w4_first, (4, 5))
-        weigh(1, banks, 0, 1)
-        prepare_dy(2, 0, behind="by_token1_2")
+        groups = ((0, 1), (1, 1), (2, 2))
+        early_steps, late_steps, all_steps = range(2), range(2, 4), range(4)
+
+        def weigh_group(c, g, bank):
+            first_window, count = groups[g]
+            weigh(c, [bank[:, b, :] for b in range(BLOCKS)], first_window, count, origin=first_window)
+
+        one = [sums(1, *groups[g], number) for g, number in enumerate((2, 4, 5))]
+        for g in range(3):
+            multiply(1, *groups[g], one[g], w4_first, early_steps)
+        multiply(1, *groups[0], one[0], w4_first, late_steps)
+        weigh_group(1, 0, one[0])
+        prepare_dy(2, 0, behind="by_token1_3")
         prepare_dy(2, 1, behind="dy_raw2_0")
         place(0, 1, 1, 7, d_second, behind="dy_raw2_1")
-        weigh(1, banks, 1, LAST)
+        multiply(1, *groups[1], one[1], w4_first, late_steps)
+        weigh_group(1, 1, one[1])
         place(1, 1, 1, 0, d_second)
+        multiply(1, *groups[2], one[2], w4_first, late_steps)
+        weigh_group(1, 2, one[2])
+
+        two = [sums(2, *groups[g], number) for g, number in enumerate((7, 4, 5))]
         prepare_dy(3, 0, behind="dy_codes1_1")
+        multiply(2, *groups[0], two[0], w4_first, all_steps)
+        weigh_group(2, 0, two[0])
         prepare_dy(3, 1, behind="dy_raw3_0")
-        place(2, 1, 1, 1, d_second, behind="dy_raw3_1")
+        place(0, 1, 2, 2, d_third[:, :, cols(0)], behind="dy_raw3_1")
+        place(2, 1, 1, 2, d_second)
+        for g in (1, 2):
+            multiply(2, *groups[g], two[g], w4_first, all_steps)
 
-        banks = multiply(2, w4_first, (7, 0))
-        weigh(2, banks, 0, 1)
-        place(0, 1, 2, 2, d_third[:, :, cols(0)])
-        weigh(2, banks, 1, LAST)
-        place(1, 1, 2, 3, d_third[:, :, cols(0)])
-
-        banks = multiply(3, w4_first, (2, 1))
-        weigh(3, banks, 0, 1)
-        place(0, 1, 3, 4, d_third[:, :, cols(1)])
+        three = [sums(3, *groups[g], number) for g, number in enumerate((4, 2, 5))]
+        weigh_group(2, 1, two[1])
+        multiply(3, *groups[0], three[0], w4_first, all_steps)
+        weigh_group(2, 2, two[2])
+        weigh_group(3, 0, three[0])
+        place(0, 1, 3, 3, d_third[:, :, cols(1)])
         store_window(0)
-        weigh(3, banks, 1, LAST)
-        place(1, 1, 3, 6, d_third[:, :, cols(1)])
+        multiply(3, *groups[1], three[1], w4_first, all_steps)
+        weigh_group(3, 1, three[1])
+        middle_rows = keep.tile([P, 2 * CHUNK], F32, name="middle_rows")
+        turn([(1, 2), (1, 3)], 6, middle_rows[:])
+        scatter(1, 2, 2, middle_rows[:], d_third[:, 1, :])
         store_window(1)
+        multiply(3, *groups[2], three[2], w4_first, all_steps)
+        weigh_group(3, 2, three[2])
         late_rows = keep.tile([P, 2 * CHUNK], F32, name="late_rows", tag="late_rows")
-        turn([(2, 2), (2, 3)], 5, late_rows[:])
+        turn([(2, 2), (2, 3)], 0, late_rows[:])
         scatter(2, 2, 2, late_rows[:], d_third[:, 2, :])
         store_window(2)
         last_rows = keep.tile([P, 3 * CHUNK], F32, name="last_rows")
-        turn([(LAST, 1), (LAST, 2)], 0, last_rows[:, cols(0, count=2)])
+        turn([(LAST, 1), (LAST, 2)], 1, last_rows[:, cols(0, count=2)])
         turn([(LAST, 3)], 7, last_rows[:, cols(2)])
         scatter(LAST, 1, 3, last_rows[:], d_last[:])
         store_window(LAST)
 
         shares = [
             keep.tile([P, 2, 2, QUARTER, 2], BF16, name=f"pairs{k}", tag=tag, align_bytes=64)
-            for k, tag in enumerate(("by_token7_1", "by_token6_1"))
+            for k, tag in enumerate(("by_token7_2", "by_token6_2"))
         ]
         out_grouped = [keep.tile([P, QUARTER, PACK], BF16, name=f"out_grouped{c}", align_bytes=64) for c in range(QUARTERS)]
         out_codes = [keep.tile([P, QUARTER], U32, name=f"out_codes{c}", align_bytes=64) for c in range(QUARTERS)]
@@ -361,10 +384,12 @@ def tile_list_embg_dl_mulP_kernel(tc, dy, w4_words, w4_scales, wd, d, wgo, offs,
             pairs = shares[c // 2][:, c % 2].rearrange("p h c e -> p (h c e)").bitcast(F32).rearrange("p (h c) -> p c h", h=2)
             copy(out=flat(out_grouped[c][:]).bitcast(F32).rearrange("p (c h) -> p c h", h=2)[:, part, :], in_=pairs[:, part, :])
 
-        def quantize_out(c, part=slice(0, QUARTER)):
+        def quantize_out(c, part):
             nc.vector.quantize_mx(
                 out=out_codes[c][:, part].bitcast(E4M3), scales=out_plane[SCALE_ROWS * c :, part], in_=flat(out_grouped[c][:, part, :])
             )
+
+        def store_codes(c, part=slice(0, QUARTER)):
             nc.sync.dma_start(
                 out=out_1[0][:, cols(c, QUARTER), :][:, part, :].rearrange("p c i -> p (c i)").bitcast(I32),
                 in_=out_codes[c][:, part].bitcast(I32),
@@ -373,8 +398,9 @@ def tile_list_embg_dl_mulP_kernel(tc, dy, w4_words, w4_scales, wd, d, wgo, offs,
         for s in (0, 1):
             for k in range(len(shares)):
                 round_share(s, k)
-        on_scalar(out=shares[0][:, :, 1, :, :], in_=share_of(2, 0).unsqueeze(3).to_broadcast([P, 2, QUARTER, 2]))
         round_share(2, 1)
+        on_scalar(out=shares[0][:, :, 1, WHOLE:, 0], in_=share_of(2, 0)[:, :, WHOLE:])
+        on_scalar(out=shares[0][:, :, 1, :WHOLE, :], in_=share_of(2, 0)[:, :, :WHOLE].unsqueeze(3).to_broadcast([P, 2, WHOLE, 2]))
         halves = [cols(h, QUARTER // 2) for h in range(2)]
         for c in (0, 1):
             round_quarter(on_vector, LAST, c)
@@ -386,9 +412,12 @@ def tile_list_embg_dl_mulP_kernel(tc, dy, w4_words, w4_scales, wd, d, wgo, offs,
         for part in halves:
             join(on_scalar, 3, part)
         for c in (0, 1, 2):
-            quantize_out(c)
+            for part in halves:
+                quantize_out(c, part)
+            store_codes(c)
         for part in halves:
             quantize_out(3, part)
+            store_codes(3, part)
         for q in range(QUADRANTS):
             queue = nc.scalar if q % 2 == 0 else nc.sync
             queue.dma_start(

@@ -93,7 +93,7 @@ def tile_list_embg_dl_mulP_kernel(tc, dy, w4_words, w4_scales, wd, d, wgo, offs,
         d_second = keep.tile([P, LAST, CHUNK], F32, name="d_second")
         d_third = keep.tile([P, LAST, 2 * CHUNK], F32, name="d_third")
         d_last = keep.tile([P, 3 * CHUNK], F32, name="d_last")
-        window = [keep.tile([P, T], F32, name=f"window{s}") for s in range(WINDOWS)]
+        window = [keep.tile([P, T], F32, name=f"window{s}") for s in range(LAST)]
         out_plane = keep.tile([P, QUARTER], U8, name="out_plane", align_bytes=64)
 
         dy_rows = dy.rearrange("(a p i) j -> a p i j", a=PASSES, i=PACK)
@@ -107,7 +107,7 @@ def tile_list_embg_dl_mulP_kernel(tc, dy, w4_words, w4_scales, wd, d, wgo, offs,
         nc.gpsimd.memset(w4_plane_raw[:].rearrange("p a n -> p (a n)").bitcast(I32), 0)
         nc.gpsimd.memset(wgo_rows[:], 0.0)
         make_identity(nc, ident[:])
-        for s in range(WINDOWS):
+        for s in range(LAST):
             nc.vector.memset(window[s][:], 0.0)
 
         nc.sync.dma_start(out=w4_codes_raw[:].bitcast(I32), in_=w4_words.rearrange("a p c -> p a c").bitcast(I32))
@@ -276,11 +276,13 @@ def tile_list_embg_dl_mulP_kernel(tc, dy, w4_words, w4_scales, wd, d, wgo, offs,
         prepare_dy(0, 0)
         prepare_wd(1)
         quantize_wd(1, 0)
-        last_landing = keep.tile([P, CHUNK, PACK], BF16, name="last_landing", align_bytes=64)
+        last_landing = keep.tile([P, CHUNK, PACK], BF16, name="last_landing", tag="last_landing", align_bytes=64)
         for b, copy in enumerate((on_scalar, on_vector)):
             interleave(copy, last_landing[:, cols(b, P), :], dy_raw[0][1][:, :, cols(b, P)])
         quantize_wd(1, 1)
         quantize_dy(0, 1, last_landing)
+        window.append(keep.tile([P, T], F32, name="window_last", tag="last_landing", align_bytes=64))
+        nc.gpsimd.memset(window[LAST][:], 0.0)
         early = group_dy(1, 0)
         nc.tensor.transpose(wgo_bank[:], wgo_rows[:], ident[:])
         wgo_cols = keep.tile([P, J // P], F32, name="wgo_cols", tag="dy_raw1_0", align_bytes=64)

@@ -68,9 +68,9 @@ def tile_list_embg_dl_mulP_kernel(tc, dy, w4_words, w4_scales, wd, d, wgo, offs,
         psum = ctx.enter_context(tc.psum_pool(name="psum", bufs=1))
 
         offsets = keep.tile([P, J // LIST_ROWS], U16, name="offsets")
-        w4_codes = keep.tile([P, PASSES, 2 * N], U8, name="w4_codes", align_bytes=64)
+        w4_codes = [keep.tile([P, 2 * N], U8, name=f"w4_codes{a}", align_bytes=64) for a in range(PASSES)]
         w4_plane = keep.tile([P, PASSES, N], U8, name="w4_plane", align_bytes=64)
-        w4_codes_raw = keep.tile([P, PASSES, 2 * N], U8, name="w4_codes_raw", align_bytes=64)
+        w4_codes_raw = [keep.tile([P, 2 * N], U8, name=f"w4_codes_raw{a}", align_bytes=64) for a in range(PASSES)]
         w4_plane_raw = keep.tile([P, PASSES, N], U8, name="w4_plane_raw", align_bytes=64)
         wgo_lead = keep.tile([P, CHUNK], F32, name="wgo_lead")
         wgo_rows = keep.tile([P, P], F32, name="wgo_rows")
@@ -108,9 +108,9 @@ def tile_list_embg_dl_mulP_kernel(tc, dy, w4_words, w4_scales, wd, d, wgo, offs,
         nc.gpsimd.memset(wgo_rows[:], 0.0)
         make_identity(nc, ident[:])
         for s in range(LAST):
-            nc.vector.memset(window[s][:], 0.0)
+            (nc.vector if s < 2 else nc.gpsimd).memset(window[s][:], 0.0)
 
-        nc.sync.dma_start(out=w4_codes_raw[:].bitcast(I32), in_=w4_words.rearrange("a p c -> p a c").bitcast(I32))
+        nc.sync.dma_start(out=w4_codes_raw[0][:].bitcast(I32), in_=w4_words[0].bitcast(I32))
         nc.sync.dma_start(out=wd_raw[0][:], in_=wd_rows[0])
         for q in range(QUADRANTS):
             nc.sync.dma_start(
@@ -121,6 +121,7 @@ def tile_list_embg_dl_mulP_kernel(tc, dy, w4_words, w4_scales, wd, d, wgo, offs,
         nc.sync.dma_start(out=wgo_rows[0 : J // P, :], in_=wgo[0:1, :].rearrange("o (b m) -> (o b) m", m=P))
         nc.sync.dma_start(out=wd_raw[1][:], in_=wd_rows[1])
         load_dy(0, 1)
+        nc.sync.dma_start(out=w4_codes_raw[1][:].bitcast(I32), in_=w4_words[1].bitcast(I32))
         nc.sync.dma_start(out=wgo_lead[:], in_=wgo[:, cols(0)])
         nc.sync.dma_start(offsets[:], offs)
         nc.sync.dma_start(out=d_lead[0][:], in_=d_rows[:, 0, cols(0)])
@@ -181,7 +182,7 @@ def tile_list_embg_dl_mulP_kernel(tc, dy, w4_words, w4_scales, wd, d, wgo, offs,
                     )
 
         def w4_columns(a):
-            return lambda s, count: w4_codes[:, a, 2 * P * s : 2 * P * (s + count)].bitcast(E2M1)
+            return lambda s, count: w4_codes[a][:, 2 * P * s : 2 * P * (s + count)].bitcast(E2M1)
 
         def wd_columns(a):
             return lambda s, count: wd_codes[a][:, P * s : P * (s + count)].bitcast(E4M3)
@@ -262,10 +263,13 @@ def tile_list_embg_dl_mulP_kernel(tc, dy, w4_words, w4_scales, wd, d, wgo, offs,
 
         wgo_bank = psum.tile([P, P], F32, name="wgo_bank", tag="bank7")
 
-        on_scalar(
-            out=w4_codes[:].bitcast(U16).rearrange("p a (s m) -> p a s m", s=WINDOWS),
-            in_=w4_codes_raw[:].bitcast(U16).rearrange("p a (m s) -> p a s m", s=WINDOWS),
-        )
+        def deal_w4(a, part):
+            on_scalar(
+                out=w4_codes[a][:].bitcast(U16).rearrange("p (s m) -> p s m", s=WINDOWS)[:, part],
+                in_=w4_codes_raw[a][:].bitcast(U16).rearrange("p (m s) -> p s m", s=WINDOWS)[:, part],
+            )
+
+        deal_w4(0, slice(0, WINDOWS))
         prepare_wd(0)
         on_vector(
             out=w4_plane[:].rearrange("p a (s m) -> p a s m", s=WINDOWS),
@@ -279,6 +283,8 @@ def tile_list_embg_dl_mulP_kernel(tc, dy, w4_words, w4_scales, wd, d, wgo, offs,
         last_landing = keep.tile([P, CHUNK, PACK], BF16, name="last_landing", tag="last_landing", align_bytes=64)
         for b, copy in enumerate((on_scalar, on_vector)):
             interleave(copy, last_landing[:, cols(b, P), :], dy_raw[0][1][:, :, cols(b, P)])
+        deal_w4(1, slice(0, LEAD))
+        deal_w4(1, slice(LEAD, WINDOWS))
         quantize_wd(1, 1)
         quantize_dy(0, 1, last_landing)
         window.append(keep.tile([P, T], F32, name="window_last", tag="last_landing", align_bytes=64))
@@ -295,16 +301,14 @@ def tile_list_embg_dl_mulP_kernel(tc, dy, w4_words, w4_scales, wd, d, wgo, offs,
             nc.vector.tensor_tensor(rows[:], leads[s][:], wgo_lead[:], MULT)
             return rows
 
-        scatter(0, 0, 1, weigh_lead(0)[:], d_lead[0][:])
-        weigh(0, banks, 2, 1, origin=LEAD, blocks=(0,))
-        weigh(0, banks, 3, 1, origin=LEAD, blocks=(0,))
-        weigh(0, banks, 2, 1, origin=LEAD, blocks=(1,))
-        weigh(0, banks, 3, 1, origin=LEAD, blocks=(1,))
+        lead_rows = [weigh_lead(s) for s in range(LEAD)]
+        for s in range(LEAD):
+            scatter(s, 0, 1, lead_rows[s][:], d_lead[s][:])
+        weigh(0, banks, 2, 2, origin=LEAD, blocks=(0,))
+        weigh(0, banks, 2, 2, origin=LEAD, blocks=(1,))
         first_bank = transpose([(2, 0), (3, 0)], 6)
-        second_rows = weigh_lead(1, behind="by_token0_2")
-        quantize_dy(1, 0, early, behind="by_token0_3")
-        scatter(1, 0, 1, second_rows[:], d_lead[1][:])
-        prepare_dy(1, 1, behind="by_token1_2")
+        quantize_dy(1, 0, early, behind="by_token0_2")
+        prepare_dy(1, 1)
         first_rows = keep.tile([P, 2 * CHUNK], F32, name="first_rows", align_bytes=64)
         on_scalar(out=first_rows[:], in_=first_bank[:])
         for k in range(2):
@@ -318,17 +322,15 @@ def tile_list_embg_dl_mulP_kernel(tc, dy, w4_words, w4_scales, wd, d, wgo, offs,
             weigh(c, [bank[:, b, :] for b in range(BLOCKS)], first_window, count, origin=first_window)
 
         one = [sums(1, *groups[g], number) for g, number in enumerate((2, 4, 5))]
-        for g in range(3):
-            multiply(1, *groups[g], one[g], w4_first, early_steps)
-        multiply(1, *groups[0], one[0], w4_first, late_steps)
+        multiply(1, *groups[0], one[0], w4_first, all_steps)
         weigh_group(1, 0, one[0])
-        prepare_dy(2, 0, behind="by_token1_3")
+        prepare_dy(2, 0, behind="by_token1_2")
         prepare_dy(2, 1, behind="dy_raw2_0")
         place(0, 1, 1, 7, d_second, behind="dy_raw2_1")
-        multiply(1, *groups[1], one[1], w4_first, late_steps)
+        multiply(1, *groups[1], one[1], w4_first, all_steps)
         weigh_group(1, 1, one[1])
         place(1, 1, 1, 0, d_second)
-        multiply(1, *groups[2], one[2], w4_first, late_steps)
+        multiply(1, *groups[2], one[2], w4_first, all_steps)
         weigh_group(1, 2, one[2])
 
         two = [sums(2, *groups[g], number) for g, number in enumerate((7, 4, 5))]

@@ -70,14 +70,15 @@ def tile_list_embg_dl_mulP_kernel(tc, dy, w4_words, w4_scales, wd, d, wgo, offs,
         offsets = keep.tile([P, J // LIST_ROWS], U16, name="offsets")
         w4_codes = [keep.tile([P, 2 * N], U8, name=f"w4_codes{a}", align_bytes=64) for a in range(PASSES)]
         w4_plane = keep.tile([P, PASSES, N], U8, name="w4_plane", align_bytes=64)
-        w4_codes_raw = [keep.tile([P, 2 * N], U8, name=f"w4_codes_raw{a}", align_bytes=64) for a in range(PASSES)]
+        w4_codes_raw = keep.tile([P, PASSES, 2 * N], U8, name="w4_codes_raw", align_bytes=64)
         w4_plane_raw = keep.tile([P, PASSES, N], U8, name="w4_plane_raw", align_bytes=64)
         wgo_lead = keep.tile([P, CHUNK], F32, name="wgo_lead")
         wgo_rows = keep.tile([P, P], F32, name="wgo_rows")
         ident = keep.tile([P, P], F32, name="ident")
-        wd_raw = [keep.tile([P, PACK, N], F32, name=f"wd_raw{a}") for a in range(PASSES)]
+        wd_raw = keep.tile([P, PACK, N], F32, name="wd_raw")
+        wd_late = [keep.tile([P, PACK // 2, N], F32, name=f"wd_late{h}") for h in range(2)]
         wd_grouped = [
-            [keep.tile([P, LEAD, P, PACK], BF16, name=f"wd_grouped{a}_{h}", align_bytes=64) for h in range(WINDOWS // LEAD)]
+            [keep.tile([P, LEAD, P, PACK], BF16, name=f"wd_grouped{a}_{h}", tag=f"wd_grouped{a}_{h}", align_bytes=64) for h in range(WINDOWS // LEAD)]
             for a in range(PASSES)
         ]
         wd_codes = [keep.tile([P, N], U32, name=f"wd_codes{a}", align_bytes=64) for a in range(PASSES)]
@@ -110,20 +111,20 @@ def tile_list_embg_dl_mulP_kernel(tc, dy, w4_words, w4_scales, wd, d, wgo, offs,
         for s in range(LAST):
             (nc.vector if s < 2 else nc.gpsimd).memset(window[s][:], 0.0)
 
-        nc.sync.dma_start(out=w4_codes_raw[0][:].bitcast(I32), in_=w4_words[0].bitcast(I32))
-        nc.sync.dma_start(out=wd_raw[0][:], in_=wd_rows[0])
+        nc.sync.dma_start(out=w4_codes_raw[:].bitcast(I32), in_=w4_words.rearrange("a p c -> p a c").bitcast(I32))
+        nc.sync.dma_start(out=wd_raw[:], in_=wd_rows[0])
         for q in range(QUADRANTS):
             nc.sync.dma_start(
                 out=w4_plane_raw[QUADRANT * q : QUADRANT * q + SCALE_ROWS].bitcast(I32),
                 in_=w4_scales[:, cols(q, SCALE_ROWS), :].rearrange("a r n -> r a n").bitcast(I32),
             )
         load_dy(0, 0)
-        nc.sync.dma_start(out=wgo_rows[0 : J // P, :], in_=wgo[0:1, :].rearrange("o (b m) -> (o b) m", m=P))
-        nc.sync.dma_start(out=wd_raw[1][:], in_=wd_rows[1])
         load_dy(0, 1)
-        nc.sync.dma_start(out=w4_codes_raw[1][:].bitcast(I32), in_=w4_words[1].bitcast(I32))
+        for h in range(2):
+            nc.sync.dma_start(out=wd_late[h][:], in_=wd_rows[1][:, cols(h, 2), :])
         nc.sync.dma_start(out=wgo_lead[:], in_=wgo[:, cols(0)])
         nc.sync.dma_start(offsets[:], offs)
+        nc.sync.dma_start(out=wgo_rows[0 : J // P, :], in_=wgo[0:1, :].rearrange("o (b m) -> (o b) m", m=P))
         nc.sync.dma_start(out=d_lead[0][:], in_=d_rows[:, 0, cols(0)])
         load_dy(1, 0)
         nc.sync.dma_start(out=d_lead[1][:], in_=d_rows[:, 1, cols(0)])
@@ -137,16 +138,12 @@ def tile_list_embg_dl_mulP_kernel(tc, dy, w4_words, w4_scales, wd, d, wgo, offs,
         nc.sync.dma_start(out=d_third[:], in_=d_rows[:, 0:LAST, cols(2, count=2)])
         nc.sync.dma_start(out=d_last[:], in_=d_rows[:, LAST, cols(1, count=3)])
 
-        def prepare_wd(a):
-            for h, copy in enumerate((on_vector, on_scalar)):
-                deal(copy, wd_grouped[a][h][:], wd_raw[a][:], cols(h, LEAD))
-
-        def quantize_wd(a, h):
-            part = cols(h, LEAD * P)
+        def quantize_wd(a, first, count):
+            part = cols(first, P, count)
             nc.vector.quantize_mx(
                 out=wd_codes[a][:, part].bitcast(E4M3),
                 scales=wd_plane[a][:, part],
-                in_=wd_grouped[a][h][:].rearrange("p s m i -> p (s m i)"),
+                in_=wd_grouped[a][first // LEAD][:, cols(first % LEAD, 1, count)].rearrange("p s m i -> p (s m i)"),
             )
 
         def group_dy(c, a, behind=None, part=slice(0, CHUNK), copy=on_scalar):
@@ -189,7 +186,8 @@ def tile_list_embg_dl_mulP_kernel(tc, dy, w4_words, w4_scales, wd, d, wgo, offs,
 
         w4_pass = [(w4_columns(a), w4_plane[:, a, :], a) for a in range(PASSES)]
         wd_pass = [(wd_columns(a), wd_plane[a][:], a) for a in range(PASSES)]
-        wd_first = [wd_pass[0], w4_pass[0], wd_pass[1], w4_pass[1]]
+        wd_first = [wd_pass[0], w4_pass[0], w4_pass[1], wd_pass[1]]
+        wd_both = [wd_pass[0], wd_pass[1], w4_pass[0], w4_pass[1]]
         w4_first = [w4_pass[0], wd_pass[0], w4_pass[1], wd_pass[1]]
 
         by_token = {}
@@ -198,8 +196,7 @@ def tile_list_embg_dl_mulP_kernel(tc, dy, w4_words, w4_scales, wd, d, wgo, offs,
             leads = [psum.tile([P, CHUNK], F32, name=f"lead{s}", tag=f"bank{lead_banks[s]}") for s in range(LEAD)]
             rest = WINDOWS - LEAD
             banks = [psum.tile([P, rest * P], F32, name=f"sums0_{b}", tag=f"bank{bank_numbers[b]}") for b in range(BLOCKS)]
-            half = len(order) // 2
-            for steps in (range(half), range(half, len(order))):
+            for steps in (range(2), range(2, 3), range(3, 4)):
                 for s in range(LEAD):
                     for step in steps:
                         codes, plane, a = order[step]
@@ -212,9 +209,10 @@ def tile_list_embg_dl_mulP_kernel(tc, dy, w4_words, w4_scales, wd, d, wgo, offs,
                             start=(step == 0),
                             stop=(step == len(order) - 1),
                         )
+            for steps in (range(1), range(1, 4)):
                 for b in range(BLOCKS):
                     for step in steps:
-                        codes, plane, a = order[step]
+                        codes, plane, a = wd_both[step]
                         nc.tensor.matmul_mx(
                             out=banks[b][:],
                             lhsT=dy_codes[0, a][:, cols(b, P)].bitcast(E5M2),
@@ -266,28 +264,33 @@ def tile_list_embg_dl_mulP_kernel(tc, dy, w4_words, w4_scales, wd, d, wgo, offs,
         def deal_w4(a, part):
             on_scalar(
                 out=w4_codes[a][:].bitcast(U16).rearrange("p (s m) -> p s m", s=WINDOWS)[:, part],
-                in_=w4_codes_raw[a][:].bitcast(U16).rearrange("p (m s) -> p s m", s=WINDOWS)[:, part],
+                in_=w4_codes_raw[:, a, :].bitcast(U16).rearrange("p (m s) -> p s m", s=WINDOWS)[:, part],
             )
 
         deal_w4(0, slice(0, WINDOWS))
-        prepare_wd(0)
+        deal_w4(1, slice(0, WINDOWS))
+        for h, copy in enumerate((on_vector, on_scalar)):
+            deal(copy, wd_grouped[0][h][:], wd_raw[:], cols(h, LEAD))
         on_vector(
             out=w4_plane[:].rearrange("p a (s m) -> p a s m", s=WINDOWS),
             in_=w4_plane_raw[:].rearrange("p a (m s) -> p a s m", s=WINDOWS),
         )
-        quantize_wd(0, 0)
-        quantize_wd(0, 1)
+        quantize_wd(0, 0, LEAD)
+        quantize_wd(0, LEAD, LEAD)
         prepare_dy(0, 0)
-        prepare_wd(1)
-        quantize_wd(1, 0)
-        last_landing = keep.tile([P, CHUNK, PACK], BF16, name="last_landing", tag="last_landing", align_bytes=64)
-        for b, copy in enumerate((on_scalar, on_vector)):
-            interleave(copy, last_landing[:, cols(b, P), :], dy_raw[0][1][:, :, cols(b, P)])
-        deal_w4(1, slice(0, LEAD))
-        deal_w4(1, slice(LEAD, WINDOWS))
-        quantize_wd(1, 1)
-        quantize_dy(0, 1, last_landing)
-        window.append(keep.tile([P, T], F32, name="window_last", tag="last_landing", align_bytes=64))
+        prepare_dy(0, 1)
+        for h, copy in enumerate((on_vector, on_scalar)):
+            deal(copy, wd_grouped[1][h][:, :, :, cols(0, 2)], wd_late[0][:], cols(h, LEAD))
+        for s in range(LEAD):
+            on_vector(
+                out=wd_grouped[1][0][:, s, :, cols(1, 2)],
+                in_=wd_late[1][:].rearrange("p i (m s) -> p s m i", s=WINDOWS)[:, s],
+            )
+        deal(on_scalar, wd_grouped[1][1][:, :, :, cols(1, 2)], wd_late[1][:], cols(1, LEAD))
+        quantize_wd(1, 0, 1)
+        quantize_wd(1, 1, 1)
+        quantize_wd(1, LEAD, LEAD)
+        window.append(keep.tile([P, T], F32, name="window_last", tag="wd_grouped1_1", align_bytes=64))
         nc.gpsimd.memset(window[LAST][:], 0.0)
         early = group_dy(1, 0)
         nc.tensor.transpose(wgo_bank[:], wgo_rows[:], ident[:])
@@ -385,8 +388,12 @@ def tile_list_embg_dl_mulP_kernel(tc, dy, w4_words, w4_scales, wd, d, wgo, offs,
             copy(out=shares[c // 2][:, c % 2][:, s // 2, :, s % 2], in_=window[s][:, cols(c, QUARTER)])
 
         def join(copy, c, part=slice(0, QUARTER)):
-            pairs = shares[c // 2][:, c % 2].rearrange("p h c e -> p (h c e)").bitcast(F32).rearrange("p (h c) -> p c h", h=2)
-            copy(out=flat(out_grouped[c][:]).bitcast(F32).rearrange("p (c h) -> p c h", h=2)[:, part, :], in_=pairs[:, part, :])
+            pairs = shares[c // 2][:, c % 2].rearrange("p h c e -> p (h c e)").bitcast(F32).rearrange("p (h c) -> p h c", h=2)
+            words = flat(out_grouped[c][:, part, :]).bitcast(F32)
+            copy(
+                out=words.rearrange("p (c f h) -> p c h f", h=2, f=RUN),
+                in_=pairs[:, :, part].rearrange("p h (c f) -> p c h f", f=RUN),
+            )
 
         def quantize_out(c, part):
             nc.vector.quantize_mx(

@@ -67,43 +67,54 @@ def tile_list_embg_dl_mulP_kernel(tc, dy, w4_words, w4_scales, wd, d, wgo, offs,
         keep = ctx.enter_context(tc.tile_pool(name="keep", bufs=1))
         psum = ctx.enter_context(tc.psum_pool(name="psum", bufs=1))
 
+        reuse = ctx.enter_context(tc.tile_pool(name="reuse", bufs=1))
+        row = CHUNK * 4
+        place_of = {"dy_raw2_1": 0, "by_token2_1": 0, "by_token3_1": 2 * row, "dy_grouped3_0": 0, "rows0_1": 3 * row,
+                    "dy_raw3_1": 4 * row, "rows0_2": 4 * row, "rows2_1": 5 * row, "by_token4_1": 6 * row, "by_token5_1": 7 * row,
+                    "by_token4_0": 8 * row, "by_token5_0": 8 * row + row // 2, "by_token2_3": 8 * row, "by_token3_3": 8 * row + row // 2}
+
+        def tile(name, shape, dtype, behind=None):
+            if name in place_of:
+                return reuse.tile(shape, dtype, name=name, align_bytes=64, offset=place_of[name])
+            return keep.tile(shape, dtype, name=name, tag=behind or name, align_bytes=64)
+
+        def bank(name, shape, number):
+            return psum.tile(shape, F32, name=name, tag=f"bank{number}")
+
         offsets = keep.tile([P, J // LIST_ROWS], U16, name="offsets")
-        w4_codes = [keep.tile([P, 2 * N], U8, name=f"w4_codes{a}", align_bytes=64) for a in range(PASSES)]
-        w4_plane = keep.tile([P, PASSES, N], U8, name="w4_plane", align_bytes=64)
-        w4_codes_raw = keep.tile([P, PASSES, 2 * N], U8, name="w4_codes_raw", align_bytes=64)
-        w4_plane_raw = keep.tile([P, PASSES, N], U8, name="w4_plane_raw", align_bytes=64)
-        wgo_lead = keep.tile([P, CHUNK], F32, name="wgo_lead")
-        wgo_rows = keep.tile([P, P], F32, name="wgo_rows")
-        ident = keep.tile([P, P], F32, name="ident")
-        wd_raw = keep.tile([P, PACK, N], F32, name="wd_raw")
-        wd_late = [keep.tile([P, PACK // 2, N], F32, name=f"wd_late{h}") for h in range(2)]
-        wd_grouped = [
-            [keep.tile([P, LEAD, P, PACK], BF16, name=f"wd_grouped{a}_{h}", tag=f"wd_grouped{a}_{h}", align_bytes=64) for h in range(WINDOWS // LEAD)]
-            for a in range(PASSES)
-        ]
-        wd_codes = [keep.tile([P, N], U32, name=f"wd_codes{a}", align_bytes=64) for a in range(PASSES)]
-        wd_plane = [keep.tile([P, N], U8, name=f"wd_plane{a}", align_bytes=64) for a in range(PASSES)]
-        dy_raw = [
-            [keep.tile([P, PACK, CHUNK], F32, name=f"dy_raw{c}_{a}", tag=f"dy_raw{c}_{a}", align_bytes=64) for a in range(PASSES)]
-            for c in range(CHUNKS)
-        ]
+        w4_codes_raw = tile("w4_codes_raw", [P, PASSES, 2 * N], U8)
+        w4_plane_raw = tile("w4_plane_raw", [P, PASSES, N], U8)
+        w4_codes = [tile(f"w4_codes{a}", [P, 2 * N], U8) for a in range(PASSES)]
+        w4_plane = tile("w4_plane", [P, PASSES, N], U8)
+        wgo_rows = tile("wgo_rows", [P, P], F32)
+        wgo_wide = [tile(f"wgo_wide{c}", [P, CHUNK], F32) for c in range(2)]
+        ident = tile("ident", [P, P], F32)
+        wd_raw = tile("wd_raw", [P, PACK, N], F32)
+        wd_late = [tile(f"wd_late{h}", [P, PACK // 2, N], F32) for h in range(2)]
+        wd_grouped = [[tile(f"wd_grouped{a}_{h}", [P, LEAD, P, PACK], BF16) for h in range(WINDOWS // LEAD)] for a in range(PASSES)]
+        wd_codes = [tile(f"wd_codes{a}", [P, N], U32) for a in range(PASSES)]
+        wd_plane = [tile(f"wd_plane{a}", [P, N], U8) for a in range(PASSES)]
+        dy_raw = [[tile(f"dy_raw{c}_{a}", [P, PACK, CHUNK], F32) for a in range(PASSES)] for c in range(CHUNKS)]
+        dy_plane = [[tile(f"dy_plane{c}_{a}", [P, CHUNK], U8) for a in range(PASSES)] for c in range(CHUNKS)]
         dy_codes = {}
-        dy_plane = [[keep.tile([P, CHUNK], U8, name=f"dy_plane{c}_{a}", align_bytes=64) for a in range(PASSES)] for c in range(CHUNKS)]
-        d_lead = [keep.tile([P, CHUNK], F32, name=f"d_lead{s}") for s in range(LEAD)]
-        d_first = keep.tile([P, WINDOWS - LEAD, CHUNK], F32, name="d_first")
-        d_second = keep.tile([P, LAST, CHUNK], F32, name="d_second")
-        d_third = keep.tile([P, LAST, 2 * CHUNK], F32, name="d_third")
-        d_last = keep.tile([P, 3 * CHUNK], F32, name="d_last")
-        window = [keep.tile([P, T], F32, name=f"window{s}") for s in range(LAST)]
-        out_plane = keep.tile([P, QUARTER], U8, name="out_plane", align_bytes=64)
+        window = [tile(f"window{s}", [P, T], F32) for s in range(LAST)]
 
         dy_rows = dy.rearrange("(a p i) j -> a p i j", a=PASSES, i=PACK)
         wd_rows = wd.rearrange("(a p i) n -> a p i n", a=PASSES, i=PACK)
         d_rows = d.rearrange("(p s) j -> p s j", s=WINDOWS)
         out_rows = out_0.rearrange("(p s) c -> p s c", s=WINDOWS)
 
+        d_part = {}
+
         def load_dy(c, a):
             nc.sync.dma_start(out=dy_raw[c][a][:], in_=dy_rows[a][:, :, cols(c)])
+
+        def load_d(first_window, windows, first_chunk, chunks):
+            piece = tile(f"d{first_window}_{first_chunk}", [P, windows, chunks * CHUNK], F32)
+            nc.sync.dma_start(out=piece[:], in_=d_rows[:, cols(first_window, 1, windows), cols(first_chunk, count=chunks)])
+            for s in range(windows):
+                for c in range(chunks):
+                    d_part[first_window + s, first_chunk + c] = (piece[:, s, :], first_chunk)
 
         nc.gpsimd.memset(w4_plane_raw[:].rearrange("p a n -> p (a n)").bitcast(I32), 0)
         nc.gpsimd.memset(wgo_rows[:], 0.0)
@@ -118,25 +129,27 @@ def tile_list_embg_dl_mulP_kernel(tc, dy, w4_words, w4_scales, wd, d, wgo, offs,
                 out=w4_plane_raw[QUADRANT * q : QUADRANT * q + SCALE_ROWS].bitcast(I32),
                 in_=w4_scales[:, cols(q, SCALE_ROWS), :].rearrange("a r n -> r a n").bitcast(I32),
             )
+        nc.sync.dma_start(out=wgo_rows[0 : J // P, :], in_=wgo[0:1, :].rearrange("o (b m) -> (o b) m", m=P))
         load_dy(0, 0)
         load_dy(0, 1)
         for h in range(2):
             nc.sync.dma_start(out=wd_late[h][:], in_=wd_rows[1][:, cols(h, 2), :])
-        nc.sync.dma_start(out=wgo_lead[:], in_=wgo[:, cols(0)])
+        nc.sync.dma_start(out=wgo_wide[0][:], in_=wgo[:, cols(0)])
         nc.sync.dma_start(offsets[:], offs)
-        nc.sync.dma_start(out=wgo_rows[0 : J // P, :], in_=wgo[0:1, :].rearrange("o (b m) -> (o b) m", m=P))
-        nc.sync.dma_start(out=d_lead[0][:], in_=d_rows[:, 0, cols(0)])
+        load_d(0, 1, 0, 1)
         load_dy(1, 0)
-        nc.sync.dma_start(out=d_lead[1][:], in_=d_rows[:, 1, cols(0)])
+        load_d(1, 1, 0, 1)
         load_dy(1, 1)
-        nc.sync.dma_start(out=d_first[:], in_=d_rows[:, LEAD:WINDOWS, cols(0)])
+        load_d(2, 2, 0, 1)
         load_dy(2, 0)
         load_dy(2, 1)
-        nc.sync.dma_start(out=d_second[:], in_=d_rows[:, 0:LAST, cols(1)])
+        nc.sync.dma_start(out=wgo_wide[1][:], in_=wgo[:, cols(1)])
+        load_d(0, 1, 1, 1)
         load_dy(3, 0)
+        load_d(1, 2, 1, 1)
         load_dy(3, 1)
-        nc.sync.dma_start(out=d_third[:], in_=d_rows[:, 0:LAST, cols(2, count=2)])
-        nc.sync.dma_start(out=d_last[:], in_=d_rows[:, LAST, cols(1, count=3)])
+        load_d(0, LAST, 2, 2)
+        load_d(LAST, 1, 1, 3)
 
         def quantize_wd(a, first, count):
             part = cols(first, P, count)
@@ -146,37 +159,14 @@ def tile_list_embg_dl_mulP_kernel(tc, dy, w4_words, w4_scales, wd, d, wgo, offs,
                 in_=wd_grouped[a][first // LEAD][:, cols(first % LEAD, 1, count)].rearrange("p s m i -> p (s m i)"),
             )
 
-        def group_dy(c, a, behind=None, part=slice(0, CHUNK), copy=on_scalar):
-            name = f"dy_grouped{c}_{a}_{part.start}"
-            grouped = keep.tile([P, part.stop - part.start, PACK], BF16, name=name, tag=behind or name, align_bytes=64)
-            interleave(copy, grouped[:], dy_raw[c][a][:, :, part])
+        def group_dy(c, a, behind=None):
+            grouped = tile(f"dy_grouped{c}_{a}", [P, CHUNK, PACK], BF16, behind)
+            interleave(on_scalar, grouped[:], dy_raw[c][a][:])
             return grouped
 
-        def quantize_dy(c, a, grouped, behind=None, part=slice(0, CHUNK)):
-            if (c, a) not in dy_codes:
-                name = f"dy_codes{c}_{a}"
-                dy_codes[c, a] = keep.tile([P, CHUNK], U32, name=name, tag=behind or name, align_bytes=64)
-            nc.vector.quantize_mx(out=dy_codes[c, a][:, part].bitcast(E5M2), scales=dy_plane[c][a][:, part], in_=flat(grouped[:]))
-
-        def prepare_dy(c, a, behind=None):
-            quantize_dy(c, a, group_dy(c, a, behind))
-
-        def sums(c, first_window, count, bank_number):
-            return psum.tile([P, BLOCKS, count * P], F32, name=f"sums{c}_{first_window}", tag=f"bank{bank_number}")
-
-        def multiply(c, first_window, count, bank, order, steps):
-            for step in steps:
-                codes, plane, a = order[step]
-                for b in range(BLOCKS):
-                    nc.tensor.matmul_mx(
-                        out=bank[:, b, :],
-                        lhsT=dy_codes[c, a][:, cols(b, P)].bitcast(E5M2),
-                        lhsT_scale=dy_plane[c][a][:, cols(b, P)],
-                        rhs=codes(first_window, count),
-                        rhs_scale=plane[:, cols(first_window, P, count)],
-                        start=(step == 0 and b == 0),
-                        stop=(step == len(order) - 1 and b == BLOCKS - 1),
-                    )
+        def quantize_dy(c, a, grouped, behind=None):
+            dy_codes[c, a] = tile(f"dy_codes{c}_{a}", [P, CHUNK], U32, behind)
+            nc.vector.quantize_mx(out=dy_codes[c, a][:].bitcast(E5M2), scales=dy_plane[c][a][:], in_=flat(grouped[:]))
 
         def w4_columns(a):
             return lambda s, count: w4_codes[a][:, 2 * P * s : 2 * P * (s + count)].bitcast(E2M1)
@@ -186,89 +176,91 @@ def tile_list_embg_dl_mulP_kernel(tc, dy, w4_words, w4_scales, wd, d, wgo, offs,
 
         w4_pass = [(w4_columns(a), w4_plane[:, a, :], a) for a in range(PASSES)]
         wd_pass = [(wd_columns(a), wd_plane[a][:], a) for a in range(PASSES)]
-        wd_first = [wd_pass[0], w4_pass[0], w4_pass[1], wd_pass[1]]
-        wd_both = [wd_pass[0], wd_pass[1], w4_pass[0], w4_pass[1]]
-        w4_first = [w4_pass[0], wd_pass[0], w4_pass[1], wd_pass[1]]
+        by_pass = [w4_pass[0], wd_pass[0], w4_pass[1], wd_pass[1]]
+        one_early = [wd_pass[0], wd_pass[1], w4_pass[0], w4_pass[1]]
+        early, late, every = range(2), range(2, 4), range(4)
+
+        def multiply_rows(sums, s, c, steps):
+            for step in steps:
+                codes, plane, a = by_pass[step]
+                nc.tensor.matmul_mx(
+                    out=sums[:],
+                    lhsT=codes(s, 1),
+                    lhsT_scale=plane[:, cols(s, P)],
+                    rhs=dy_codes[c, a][:].bitcast(E5M2),
+                    rhs_scale=dy_plane[c][a][:],
+                    start=(step == 0),
+                    stop=(step == len(by_pass) - 1),
+                )
+
+        def multiply_tokens(sums, first_window, count, c, steps, order=by_pass):
+            for step in steps:
+                codes, plane, a = order[step]
+                for b in range(BLOCKS):
+                    nc.tensor.matmul_mx(
+                        out=sums[:, b, :],
+                        lhsT=dy_codes[c, a][:, cols(b, P)].bitcast(E5M2),
+                        lhsT_scale=dy_plane[c][a][:, cols(b, P)],
+                        rhs=codes(first_window, count),
+                        rhs_scale=plane[:, cols(first_window, P, count)],
+                        start=(step == 0 and b == 0),
+                        stop=(step == len(order) - 1 and b == BLOCKS - 1),
+                    )
+
+        def token_sums(first_window, count, c, number):
+            return bank(f"sums{c}_{first_window}", [P, BLOCKS, count * P], number)
 
         by_token = {}
 
-        def multiply_first(order, lead_banks, bank_numbers):
-            leads = [psum.tile([P, CHUNK], F32, name=f"lead{s}", tag=f"bank{lead_banks[s]}") for s in range(LEAD)]
-            rest = WINDOWS - LEAD
-            banks = [psum.tile([P, rest * P], F32, name=f"sums0_{b}", tag=f"bank{bank_numbers[b]}") for b in range(BLOCKS)]
-            for steps in (range(2), range(2, 3), range(3, 4)):
-                for s in range(LEAD):
-                    for step in steps:
-                        codes, plane, a = order[step]
-                        nc.tensor.matmul_mx(
-                            out=leads[s][:],
-                            lhsT=codes(s, 1),
-                            lhsT_scale=plane[:, cols(s, P)],
-                            rhs=dy_codes[0, a][:].bitcast(E5M2),
-                            rhs_scale=dy_plane[0][a][:],
-                            start=(step == 0),
-                            stop=(step == len(order) - 1),
-                        )
-            for steps in (range(1), range(1, 4)):
-                for b in range(BLOCKS):
-                    for step in steps:
-                        codes, plane, a = wd_both[step]
-                        nc.tensor.matmul_mx(
-                            out=banks[b][:],
-                            lhsT=dy_codes[0, a][:, cols(b, P)].bitcast(E5M2),
-                            lhsT_scale=dy_plane[0][a][:, cols(b, P)],
-                            rhs=codes(LEAD, rest),
-                            rhs_scale=plane[:, cols(LEAD, P, rest)],
-                            start=(step == 0),
-                            stop=(step == len(order) - 1),
-                        )
-            return leads, banks
-
-        def weigh(c, banks, first_window, count, origin=0, blocks=range(BLOCKS)):
-            for b in blocks:
+        def weigh_tokens(sums, first_window, count, c, behind=(None, None)):
+            for b in range(BLOCKS):
                 block = BLOCKS * c + b
-                weight = wgo_cols[:, block : block + 1]
-                name = f"by_token{block}_{first_window}"
-                weighed = keep.tile([P, count, P], F32, name=name, tag=name, align_bytes=64)
-                sums = banks[b][:, cols(first_window - origin, P, count)]
-                nc.scalar.activation(out=weighed[:].rearrange("j s m -> j (s m)"), in_=sums, func=COPY, scale=weight)
+                weighed = tile(f"by_token{block}_{first_window}", [P, count, P], F32, behind[b])
+                nc.scalar.activation(
+                    out=weighed[:].rearrange("j s m -> j (s m)"), in_=sums[:, b, :], func=COPY, scale=wgo_cols[:, block : block + 1]
+                )
                 for s in range(count):
                     by_token[block, first_window + s] = weighed[:, s, :]
 
-        def transpose(pieces, bank_number):
-            bank = psum.tile([P, len(pieces) * CHUNK], F32, name=f"turned{pieces[0][0]}_{pieces[0][1]}", tag=f"bank{bank_number}")
-            steps = sorted((BLOCKS * c + b, k, b, s) for k, (s, c) in enumerate(pieces) for b in range(BLOCKS))
-            for block, k, b, s in steps:
-                nc.tensor.transpose(bank[:, cols(BLOCKS * k + b, P)], by_token[block, s], ident[:])
-            return bank
+        def weigh_rows(sums, s, c):
+            rows = tile(f"rows{s}_{c}", [P, CHUNK], F32)
+            nc.vector.tensor_tensor(rows[:], sums[:], wgo_wide[c][:], MULT)
+            return rows
 
-        def turn(pieces, bank_number, rows, copy=on_scalar):
-            copy(out=rows, in_=transpose(pieces, bank_number)[:])
+        def turn(s, first_chunk, chunks, number):
+            turned = bank(f"turned{s}_{first_chunk}", [P, chunks * CHUNK], number)
+            for b in range(chunks * BLOCKS):
+                nc.tensor.transpose(turned[:, cols(b, P)], by_token[BLOCKS * first_chunk + b, s], ident[:])
+            return turned
 
-        def scatter(s, first_chunk, count, rows, d_part):
-            entries = offsets[:, cols(first_chunk, CHUNK // LIST_ROWS, count)]
-            nc.vector.tensor_tensor(window[s][:].indirect(entries), rows, d_part, MULT)
+        def turn_pair(first_window, c, numbers):
+            turned = [bank(f"turned{first_window + k}_{c}", [P, CHUNK], numbers[k]) for k in range(2)]
+            for b in range(BLOCKS):
+                for k in range(2):
+                    nc.tensor.transpose(turned[k][:, cols(b, P)], by_token[BLOCKS * c + b, first_window + k], ident[:])
+            return turned
 
-        def place(first_window, count, c, bank_number, d_part, behind=None, copy=on_scalar, origin=0):
-            name = f"by_row{first_window}_{c}"
-            rows = keep.tile([P, count * CHUNK], F32, name=name, tag=behind or name, align_bytes=64)
-            turn([(first_window + k, c) for k in range(count)], bank_number, rows[:], copy)
-            for k in range(count):
-                scatter(first_window + k, c, 1, rows[:, cols(k)], d_part[:, first_window + k - origin, :])
+        def scatter(s, first_chunk, chunks, rows):
+            entries = offsets[:, cols(first_chunk, CHUNK // LIST_ROWS, chunks)]
+            row, origin = d_part[s, first_chunk]
+            nc.vector.tensor_tensor(window[s][:].indirect(entries), rows, row[:, cols(first_chunk - origin, count=chunks)], MULT)
+
+        def place(s, first_chunk, chunks, turned, behind=None):
+            rows = tile(f"rows{s}_{first_chunk}", [P, chunks * CHUNK], F32, behind)
+            on_scalar(out=rows[:], in_=turned[:])
+            scatter(s, first_chunk, chunks, rows[:])
 
         def store_window(s):
             nc.sync.dma_start(out=out_rows[:, s, :], in_=window[s][:])
 
-        wgo_bank = psum.tile([P, P], F32, name="wgo_bank", tag="bank7")
-
-        def deal_w4(a, part):
+        def deal_w4(a):
             on_scalar(
-                out=w4_codes[a][:].bitcast(U16).rearrange("p (s m) -> p s m", s=WINDOWS)[:, part],
-                in_=w4_codes_raw[:, a, :].bitcast(U16).rearrange("p (m s) -> p s m", s=WINDOWS)[:, part],
+                out=w4_codes[a][:].bitcast(U16).rearrange("p (s m) -> p s m", s=WINDOWS),
+                in_=w4_codes_raw[:, a, :].bitcast(U16).rearrange("p (m s) -> p s m", s=WINDOWS),
             )
 
-        deal_w4(0, slice(0, WINDOWS))
-        deal_w4(1, slice(0, WINDOWS))
+        for a in range(PASSES):
+            deal_w4(a)
         for h, copy in enumerate((on_vector, on_scalar)):
             deal(copy, wd_grouped[0][h][:], wd_raw[:], cols(h, LEAD))
         on_vector(
@@ -277,8 +269,8 @@ def tile_list_embg_dl_mulP_kernel(tc, dy, w4_words, w4_scales, wd, d, wgo, offs,
         )
         quantize_wd(0, 0, LEAD)
         quantize_wd(0, LEAD, LEAD)
-        prepare_dy(0, 0)
-        prepare_dy(0, 1)
+        for a in range(PASSES):
+            quantize_dy(0, a, group_dy(0, a))
         for h, copy in enumerate((on_vector, on_scalar)):
             deal(copy, wd_grouped[1][h][:, :, :, cols(0, 2)], wd_late[0][:], cols(h, LEAD))
         for s in range(LEAD):
@@ -287,93 +279,87 @@ def tile_list_embg_dl_mulP_kernel(tc, dy, w4_words, w4_scales, wd, d, wgo, offs,
                 in_=wd_late[1][:].rearrange("p i (m s) -> p s m i", s=WINDOWS)[:, s],
             )
         deal(on_scalar, wd_grouped[1][1][:, :, :, cols(1, 2)], wd_late[1][:], cols(1, LEAD))
+        wgo_bank = bank("wgo_bank", [P, P], 7)
+        nc.tensor.transpose(wgo_bank[:], wgo_rows[:], ident[:])
+        wgo_cols = tile("wgo_cols", [P, J // P], F32, behind="wd_late1")
+        on_scalar(out=wgo_cols[:], in_=wgo_bank[:, 0 : J // P])
         quantize_wd(1, 0, 1)
         quantize_wd(1, 1, 1)
         quantize_wd(1, LEAD, LEAD)
-        window.append(keep.tile([P, T], F32, name="window_last", tag="wd_grouped1_1", align_bytes=64))
+        window.append(tile("window_last", [P, T], F32, behind="wd_grouped1_1"))
         nc.gpsimd.memset(window[LAST][:], 0.0)
-        early = group_dy(1, 0)
-        nc.tensor.transpose(wgo_bank[:], wgo_rows[:], ident[:])
-        wgo_cols = keep.tile([P, J // P], F32, name="wgo_cols", tag="dy_raw1_0", align_bytes=64)
-        nc.scalar.copy(out=wgo_cols[:], in_=wgo_bank[:, 0 : J // P])
 
-        leads, banks = multiply_first(wd_first, (4, 5), (0, 1))
-        def weigh_lead(s, behind=None):
-            name = f"lead_rows{s}"
-            rows = keep.tile([P, CHUNK], F32, name=name, tag=behind or name, align_bytes=64)
-            nc.vector.tensor_tensor(rows[:], leads[s][:], wgo_lead[:], MULT)
-            return rows
-
-        lead_rows = [weigh_lead(s) for s in range(LEAD)]
+        leads = [bank(f"lead{s}", [P, CHUNK], s) for s in range(LEAD)]
+        for steps in (range(2), range(2, 3), range(3, 4)):
+            for s in range(LEAD):
+                multiply_rows(leads[s], s, 0, steps)
+        sums = token_sums(2, 2, 0, 2)
+        multiply_tokens(sums, 2, 2, 0, every, order=one_early)
+        lead_rows = [weigh_rows(leads[s], s, 0) for s in range(LEAD)]
         for s in range(LEAD):
-            scatter(s, 0, 1, lead_rows[s][:], d_lead[s][:])
-        weigh(0, banks, 2, 2, origin=LEAD, blocks=(0,))
-        weigh(0, banks, 2, 2, origin=LEAD, blocks=(1,))
-        first_bank = transpose([(2, 0), (3, 0)], 6)
-        quantize_dy(1, 0, early, behind="by_token0_2")
-        prepare_dy(1, 1)
-        first_rows = keep.tile([P, 2 * CHUNK], F32, name="first_rows", align_bytes=64)
-        on_scalar(out=first_rows[:], in_=first_bank[:])
-        for k in range(2):
-            scatter(2 + k, 0, 1, first_rows[:, cols(k)], d_first[:, k, :])
+            scatter(s, 0, 1, lead_rows[s][:])
+        weigh_tokens(sums, 2, 2, 0)
+        turned = [turn(2, 0, 1, 4), turn(3, 0, 1, 5)]
+        quantize_dy(1, 0, group_dy(1, 0, behind="dy_codes0_1"))
+        place(2, 0, 1, turned[0])
+        quantize_dy(1, 1, group_dy(1, 1))
+        place(3, 0, 1, turned[1], behind="dy_raw1_1")
 
-        groups = ((0, 1), (1, 1), (2, 2))
-        early_steps, late_steps, all_steps = range(2), range(2, 4), range(4)
+        lead = bank("lead_second", [P, CHUNK], 3)
+        middle, last = token_sums(1, 2, 1, 0), token_sums(LAST, 1, 1, 1)
+        for steps in (early, late):
+            multiply_rows(lead, 0, 1, steps)
+            multiply_tokens(middle, 1, 2, 1, steps)
+        multiply_tokens(last, LAST, 1, 1, every)
+        quantize_dy(2, 0, group_dy(2, 0))
+        grouped = group_dy(2, 1)
+        rows = weigh_rows(lead, 0, 1)
+        quantize_dy(2, 1, grouped)
+        scatter(0, 1, 1, rows[:])
+        weigh_tokens(middle, 1, 2, 1)
+        waiting = turn_pair(1, 1, (2, 4))
+        quantize_dy(3, 0, group_dy(3, 0))
+        place(1, 1, 1, waiting[0])
 
-        def weigh_group(c, g, bank):
-            first_window, count = groups[g]
-            weigh(c, [bank[:, b, :] for b in range(BLOCKS)], first_window, count, origin=first_window)
-
-        one = [sums(1, *groups[g], number) for g, number in enumerate((2, 4, 5))]
-        multiply(1, *groups[0], one[0], w4_first, all_steps)
-        weigh_group(1, 0, one[0])
-        prepare_dy(2, 0, behind="by_token1_2")
-        prepare_dy(2, 1, behind="dy_raw2_0")
-        place(0, 1, 1, 7, d_second, behind="dy_raw2_1")
-        multiply(1, *groups[1], one[1], w4_first, all_steps)
-        weigh_group(1, 1, one[1])
-        place(1, 1, 1, 0, d_second)
-        multiply(1, *groups[2], one[2], w4_first, all_steps)
-        weigh_group(1, 2, one[2])
-
-        two = [sums(2, *groups[g], number) for g, number in enumerate((7, 4, 5))]
-        prepare_dy(3, 0, behind="dy_codes1_1")
-        multiply(2, *groups[0], two[0], w4_first, all_steps)
-        weigh_group(2, 0, two[0])
-        prepare_dy(3, 1, behind="dy_raw3_0")
-        place(0, 1, 2, 2, d_third[:, :, cols(0)], behind="dy_raw3_1")
-        place(2, 1, 1, 2, d_second)
-        for g in (1, 2):
-            multiply(2, *groups[g], two[g], w4_first, all_steps)
-
-        three = [sums(3, *groups[g], number) for g, number in enumerate((4, 2, 5))]
-        weigh_group(2, 1, two[1])
-        multiply(3, *groups[0], three[0], w4_first, all_steps)
-        weigh_group(2, 2, two[2])
-        weigh_group(3, 0, three[0])
-        place(0, 1, 3, 3, d_third[:, :, cols(1)])
+        first, middle = token_sums(0, 1, 2, 0), token_sums(1, 2, 2, 2)
+        multiply_tokens(first, 0, 1, 2, every)
+        multiply_tokens(middle, 1, 2, 2, every)
+        weigh_tokens(first, 0, 1, 2)
+        turned = turn(0, 2, 1, 3)
+        quantize_dy(3, 1, group_dy(3, 1, behind="dy_raw3_0"))
+        place(0, 2, 1, turned)
+        weigh_tokens(middle, 1, 2, 2)
+        place(2, 1, 1, waiting[1])
+        first = token_sums(0, 1, 3, 0)
+        multiply_tokens(first, 0, 1, 3, every)
+        second = token_sums(1, 1, 3, 3)
+        multiply_tokens(second, 1, 1, 3, every)
+        weigh_tokens(first, 0, 1, 3)
+        turned = turn(0, 3, 1, 2)
+        weigh_tokens(last, LAST, 1, 1)
+        place(0, 3, 1, turned)
         store_window(0)
-        multiply(3, *groups[1], three[1], w4_first, all_steps)
-        weigh_group(3, 1, three[1])
-        middle_rows = keep.tile([P, 2 * CHUNK], F32, name="middle_rows")
-        turn([(1, 2), (1, 3)], 6, middle_rows[:])
-        scatter(1, 2, 2, middle_rows[:], d_third[:, 1, :])
+        weigh_tokens(second, 1, 1, 3)
+        place(1, 2, 2, turn(1, 2, 2, 1))
         store_window(1)
-        multiply(3, *groups[2], three[2], w4_first, all_steps)
-        weigh_group(3, 2, three[2])
-        late_rows = keep.tile([P, 2 * CHUNK], F32, name="late_rows", tag="late_rows")
-        turn([(2, 2), (2, 3)], 0, late_rows[:])
-        scatter(2, 2, 2, late_rows[:], d_third[:, 2, :])
+        rest = token_sums(2, 2, 3, 0)
+        multiply_tokens(rest, 2, 2, 3, every)
+        last = token_sums(LAST, 1, 2, 3)
+        multiply_tokens(last, LAST, 1, 2, every)
+        weigh_tokens(rest, 2, 2, 3)
+        place(2, 2, 2, turn(2, 2, 2, 4))
         store_window(2)
-        last_rows = keep.tile([P, 3 * CHUNK], F32, name="last_rows")
-        turn([(LAST, 1), (LAST, 2)], 1, last_rows[:, cols(0, count=2)])
-        turn([(LAST, 3)], 7, last_rows[:, cols(2)])
-        scatter(LAST, 1, 3, last_rows[:], d_last[:])
+        weigh_tokens(last, LAST, 1, 2)
+        last_rows = tile("last_rows", [P, 3 * CHUNK], F32)
+        on_scalar(out=last_rows[:, cols(2)], in_=turn(LAST, 3, 1, 6)[:])
+        on_scalar(out=last_rows[:, cols(0, count=2)], in_=turn(LAST, 1, 2, 5)[:])
+        scatter(LAST, 1, 3, last_rows[:])
         store_window(LAST)
 
+        out_plane = tile("out_plane", [P, QUARTER], U8)
         shares = [
             keep.tile([P, 2, 2, QUARTER, 2], BF16, name=f"pairs{k}", tag=tag, align_bytes=64)
-            for k, tag in enumerate(("by_token7_2", "by_token6_2"))
+            for k, tag in enumerate(("by_token5_3", "by_token4_3"))
         ]
         out_grouped = [keep.tile([P, QUARTER, PACK], BF16, name=f"out_grouped{c}", align_bytes=64) for c in range(QUARTERS)]
         out_codes = [keep.tile([P, QUARTER], U32, name=f"out_codes{c}", align_bytes=64) for c in range(QUARTERS)]

@@ -69,9 +69,11 @@ def tile_list_embg_dl_mulP_kernel(tc, dy, w4_words, w4_scales, wd, d, wgo, offs,
 
         reuse = ctx.enter_context(tc.tile_pool(name="reuse", bufs=1))
         row = CHUNK * 4
-        place_of = {"dy_raw2_1": 0, "by_token2_1": 0, "by_token3_1": 2 * row, "dy_grouped3_0": 0, "rows0_1": 3 * row,
-                    "dy_raw3_1": 4 * row, "rows0_2": 4 * row, "rows2_1": 5 * row, "by_token4_1": 6 * row, "by_token5_1": 7 * row,
-                    "by_token4_0": 8 * row, "by_token5_0": 8 * row + row // 2, "by_token2_3": 8 * row, "by_token3_3": 8 * row + row // 2}
+        place_of = {
+            "dy_raw2_1": row // 2, "rows0_1": 0, "dy_grouped3_0": row, "by_token1_1": 3 * row,
+            "dy_raw3_1": 5 * row + row // 2, "by_token1_3": 5 * row, "rows0_2": 6 * row, "by_token2_1": 8 * row,
+            "pairs0": 10 * row, "by_token3_2": 17 * row, "pairs1": 18 * row,
+        }
 
         def tile(name, shape, dtype, behind=None):
             if name in place_of:
@@ -212,32 +214,26 @@ def tile_list_embg_dl_mulP_kernel(tc, dy, w4_words, w4_scales, wd, d, wgo, offs,
 
         by_token = {}
 
-        def weigh_tokens(sums, first_window, count, c, behind=(None, None)):
+        def weigh_tokens(sums, first_window, count, c):
+            weighed = tile(f"by_token{c}_{first_window}", [P, BLOCKS, count, P], F32)
             for b in range(BLOCKS):
                 block = BLOCKS * c + b
-                weighed = tile(f"by_token{block}_{first_window}", [P, count, P], F32, behind[b])
                 nc.scalar.activation(
-                    out=weighed[:].rearrange("j s m -> j (s m)"), in_=sums[:, b, :], func=COPY, scale=wgo_cols[:, block : block + 1]
+                    out=weighed[:, b].rearrange("j s m -> j (s m)"), in_=sums[:, b, :], func=COPY, scale=wgo_cols[:, block : block + 1]
                 )
                 for s in range(count):
-                    by_token[block, first_window + s] = weighed[:, s, :]
+                    by_token[block, first_window + s] = weighed[:, b, s, :]
 
         def weigh_rows(sums, s, c):
             rows = tile(f"rows{s}_{c}", [P, CHUNK], F32)
             nc.vector.tensor_tensor(rows[:], sums[:], wgo_wide[c][:], MULT)
             return rows
 
-        def turn(s, first_chunk, chunks, number):
-            turned = bank(f"turned{s}_{first_chunk}", [P, chunks * CHUNK], number)
-            for b in range(chunks * BLOCKS):
-                nc.tensor.transpose(turned[:, cols(b, P)], by_token[BLOCKS * first_chunk + b, s], ident[:])
-            return turned
-
-        def turn_pair(first_window, c, numbers):
-            turned = [bank(f"turned{first_window + k}_{c}", [P, CHUNK], numbers[k]) for k in range(2)]
-            for b in range(BLOCKS):
-                for k in range(2):
-                    nc.tensor.transpose(turned[k][:, cols(b, P)], by_token[BLOCKS * c + b, first_window + k], ident[:])
+        def turn(pieces, number):
+            turned = bank(f"turned{pieces[0][0]}_{pieces[0][1]}", [P, len(pieces) * CHUNK], number)
+            for k, (s, c) in enumerate(pieces):
+                for b in range(BLOCKS):
+                    nc.tensor.transpose(turned[:, cols(BLOCKS * k + b, P)], by_token[BLOCKS * c + b, s], ident[:])
             return turned
 
         def scatter(s, first_chunk, chunks, rows):
@@ -299,7 +295,7 @@ def tile_list_embg_dl_mulP_kernel(tc, dy, w4_words, w4_scales, wd, d, wgo, offs,
         for s in range(LEAD):
             scatter(s, 0, 1, lead_rows[s][:])
         weigh_tokens(sums, 2, 2, 0)
-        turned = [turn(2, 0, 1, 4), turn(3, 0, 1, 5)]
+        turned = [turn([(2, 0)], 4), turn([(3, 0)], 5)]
         quantize_dy(1, 0, group_dy(1, 0, behind="dy_codes0_1"))
         place(2, 0, 1, turned[0])
         quantize_dy(1, 1, group_dy(1, 1))
@@ -317,50 +313,48 @@ def tile_list_embg_dl_mulP_kernel(tc, dy, w4_words, w4_scales, wd, d, wgo, offs,
         quantize_dy(2, 1, grouped)
         scatter(0, 1, 1, rows[:])
         weigh_tokens(middle, 1, 2, 1)
-        waiting = turn_pair(1, 1, (2, 4))
+        turned = turn([(1, 1)], 2)
         quantize_dy(3, 0, group_dy(3, 0))
-        place(1, 1, 1, waiting[0])
+        place(1, 1, 1, turned)
 
         first, middle = token_sums(0, 1, 2, 0), token_sums(1, 2, 2, 2)
         multiply_tokens(first, 0, 1, 2, every)
         multiply_tokens(middle, 1, 2, 2, every)
         weigh_tokens(first, 0, 1, 2)
-        turned = turn(0, 2, 1, 3)
+        turned = turn([(2, 1), (0, 2)], 3)
         quantize_dy(3, 1, group_dy(3, 1, behind="dy_raw3_0"))
-        place(0, 2, 1, turned)
+        rows = tile("rows0_2", [P, 2 * CHUNK], F32)
+        on_scalar(out=rows[:], in_=turned[:])
+        scatter(0, 2, 1, rows[:, cols(1)])
+        scatter(2, 1, 1, rows[:, cols(0)])
         weigh_tokens(middle, 1, 2, 2)
-        place(2, 1, 1, waiting[1])
+        weigh_tokens(last, LAST, 1, 1)
         first = token_sums(0, 1, 3, 0)
         multiply_tokens(first, 0, 1, 3, every)
         second = token_sums(1, 1, 3, 3)
         multiply_tokens(second, 1, 1, 3, every)
         weigh_tokens(first, 0, 1, 3)
-        turned = turn(0, 3, 1, 2)
-        weigh_tokens(last, LAST, 1, 1)
-        place(0, 3, 1, turned)
+        place(0, 3, 1, turn([(0, 3)], 5))
         store_window(0)
+        last = token_sums(LAST, 1, 2, 2)
+        multiply_tokens(last, LAST, 1, 2, every)
         weigh_tokens(second, 1, 1, 3)
-        place(1, 2, 2, turn(1, 2, 2, 1))
+        place(1, 2, 2, turn([(1, 2), (1, 3)], 1))
         store_window(1)
         rest = token_sums(2, 2, 3, 0)
         multiply_tokens(rest, 2, 2, 3, every)
-        last = token_sums(LAST, 1, 2, 3)
-        multiply_tokens(last, LAST, 1, 2, every)
-        weigh_tokens(rest, 2, 2, 3)
-        place(2, 2, 2, turn(2, 2, 2, 4))
-        store_window(2)
         weigh_tokens(last, LAST, 1, 2)
         last_rows = tile("last_rows", [P, 3 * CHUNK], F32)
-        on_scalar(out=last_rows[:, cols(2)], in_=turn(LAST, 3, 1, 6)[:])
-        on_scalar(out=last_rows[:, cols(0, count=2)], in_=turn(LAST, 1, 2, 5)[:])
+        on_scalar(out=last_rows[:, cols(0, count=2)], in_=turn([(LAST, 1), (LAST, 2)], 4)[:])
+        weigh_tokens(rest, 2, 2, 3)
+        place(2, 2, 2, turn([(2, 2), (2, 3)], 7))
+        store_window(2)
+        on_scalar(out=last_rows[:, cols(2)], in_=turn([(LAST, 3)], 6)[:])
         scatter(LAST, 1, 3, last_rows[:])
         store_window(LAST)
 
         out_plane = tile("out_plane", [P, QUARTER], U8)
-        shares = [
-            keep.tile([P, 2, 2, QUARTER, 2], BF16, name=f"pairs{k}", tag=tag, align_bytes=64)
-            for k, tag in enumerate(("by_token5_3", "by_token4_3"))
-        ]
+        shares = [tile(f"pairs{k}", [P, 2, 2, QUARTER, 2], BF16) for k in range(2)]
         out_grouped = [keep.tile([P, QUARTER, PACK], BF16, name=f"out_grouped{c}", align_bytes=64) for c in range(QUARTERS)]
         out_codes = [keep.tile([P, QUARTER], U32, name=f"out_codes{c}", align_bytes=64) for c in range(QUARTERS)]
 
@@ -395,8 +389,8 @@ def tile_list_embg_dl_mulP_kernel(tc, dy, w4_words, w4_scales, wd, d, wgo, offs,
         for s in (0, 1):
             for k in range(len(shares)):
                 round_share(s, k)
-        round_share(2, 1)
         on_scalar(out=shares[0][:, :, 1, WHOLE:, 0], in_=share_of(2, 0)[:, :, WHOLE:])
+        round_share(2, 1)
         on_scalar(out=shares[0][:, :, 1, :WHOLE, :], in_=share_of(2, 0)[:, :, :WHOLE].unsqueeze(3).to_broadcast([P, 2, WHOLE, 2]))
         halves = [cols(h, QUARTER // 2) for h in range(2)]
         for c in (0, 1):

@@ -71,8 +71,8 @@ def tile_list_embg_dl_mulP_kernel(tc, dy, w4_words, w4_scales, wd, d, wgo, offs,
         row = CHUNK * 4
         place_of = {
             "dy_raw2_1": row // 2, "rows0_1": 0, "dy_grouped3_0": row, "by_token1_1": 3 * row,
-            "dy_raw3_1": 5 * row + row // 2, "by_token1_3": 5 * row, "rows0_2": 6 * row, "by_token2_1": 8 * row,
-            "pairs0": 10 * row, "by_token3_2": 17 * row, "pairs1": 18 * row,
+            "dy_raw3_1": 6 * row, "by_token2_1": 5 * row, "by_token1_3": 7 * row, "by_token2_3": 8 * row, "rows0_2": 9 * row,
+            "pairs0": 11 * row, "by_token3_2": 18 * row, "pairs1": 19 * row,
         }
 
         def tile(name, shape, dtype, behind=None):
@@ -322,34 +322,33 @@ def tile_list_embg_dl_mulP_kernel(tc, dy, w4_words, w4_scales, wd, d, wgo, offs,
         multiply_tokens(middle, 1, 2, 2, every)
         weigh_tokens(first, 0, 1, 2)
         turned = turn([(2, 1), (0, 2)], 3)
+        last_second = token_sums(LAST, 1, 2, 0)
+        multiply_tokens(last_second, LAST, 1, 2, every)
         quantize_dy(3, 1, group_dy(3, 1, behind="dy_raw3_0"))
+        groups = ((0, 1), (1, 1), (2, 2))
+        sums = [token_sums(*group, 3, 4 + g) for g, group in enumerate(groups)]
+        for steps in (early, late):
+            for g, group in enumerate(groups):
+                multiply_tokens(sums[g], *group, 3, steps)
         rows = tile("rows0_2", [P, 2 * CHUNK], F32)
         on_scalar(out=rows[:], in_=turned[:])
         scatter(0, 2, 1, rows[:, cols(1)])
         scatter(2, 1, 1, rows[:, cols(0)])
         weigh_tokens(middle, 1, 2, 2)
         weigh_tokens(last, LAST, 1, 1)
-        first = token_sums(0, 1, 3, 0)
-        multiply_tokens(first, 0, 1, 3, every)
-        second = token_sums(1, 1, 3, 3)
-        multiply_tokens(second, 1, 1, 3, every)
-        weigh_tokens(first, 0, 1, 3)
-        place(0, 3, 1, turn([(0, 3)], 5))
+        weigh_tokens(last_second, LAST, 1, 2)
+        weigh_tokens(sums[0], 0, 1, 3)
+        place(0, 3, 1, turn([(0, 3)], 7))
         store_window(0)
-        last = token_sums(LAST, 1, 2, 2)
-        multiply_tokens(last, LAST, 1, 2, every)
-        weigh_tokens(second, 1, 1, 3)
+        weigh_tokens(sums[1], 1, 1, 3)
         place(1, 2, 2, turn([(1, 2), (1, 3)], 1))
         store_window(1)
-        rest = token_sums(2, 2, 3, 0)
-        multiply_tokens(rest, 2, 2, 3, every)
-        weigh_tokens(last, LAST, 1, 2)
         last_rows = tile("last_rows", [P, 3 * CHUNK], F32)
-        on_scalar(out=last_rows[:, cols(0, count=2)], in_=turn([(LAST, 1), (LAST, 2)], 4)[:])
-        weigh_tokens(rest, 2, 2, 3)
-        place(2, 2, 2, turn([(2, 2), (2, 3)], 7))
+        on_scalar(out=last_rows[:, cols(0, count=2)], in_=turn([(LAST, 1), (LAST, 2)], 0)[:])
+        weigh_tokens(sums[2], 2, 2, 3)
+        place(2, 2, 2, turn([(2, 2), (2, 3)], 2))
         store_window(2)
-        on_scalar(out=last_rows[:, cols(2)], in_=turn([(LAST, 3)], 6)[:])
+        on_scalar(out=last_rows[:, cols(2)], in_=turn([(LAST, 3)], 3)[:])
         scatter(LAST, 1, 3, last_rows[:])
         store_window(LAST)
 
@@ -395,14 +394,18 @@ def tile_list_embg_dl_mulP_kernel(tc, dy, w4_words, w4_scales, wd, d, wgo, offs,
         halves = [cols(h, QUARTER // 2) for h in range(2)]
         for c in (0, 1):
             round_quarter(on_vector, LAST, c)
-        for c in (0, 1):
-            join(on_vector, c)
         for c in (2, 3):
             round_quarter(on_scalar, LAST, c)
         join(on_scalar, 2)
         for part in halves:
             join(on_scalar, 3, part)
-        for c in (0, 1, 2):
+        for part in halves:
+            join(on_vector, 0, part)
+        for part in halves:
+            quantize_out(0, part)
+            join(on_vector, 1, part)
+        store_codes(0)
+        for c in (1, 2):
             for part in halves:
                 quantize_out(c, part)
             store_codes(c)

@@ -126,10 +126,10 @@ def tile_list_embg_dl_mulP_kernel(tc, dy, w4_words, w4_scales, wd, d, wgo, offs,
 
         nc.sync.dma_start(out=w4_codes_raw[:].bitcast(I32), in_=w4_words.rearrange("a p c -> p a c").bitcast(I32))
         nc.sync.dma_start(out=wd_raw[:], in_=wd_rows[0])
-        for q in range(QUADRANTS):
+        for r in range(SCALE_ROWS):
             nc.sync.dma_start(
-                out=w4_plane_raw[QUADRANT * q : QUADRANT * q + SCALE_ROWS].bitcast(I32),
-                in_=w4_scales[:, cols(q, SCALE_ROWS), :].rearrange("a r n -> r a n").bitcast(I32),
+                out=w4_plane_raw[r:P:QUADRANT].bitcast(I32),
+                in_=w4_scales.rearrange("a (q r) n -> r q a n", r=SCALE_ROWS)[r].bitcast(I32),
             )
         nc.sync.dma_start(out=wgo_rows[0 : J // P, :], in_=wgo[0:1, :].rearrange("o (b m) -> (o b) m", m=P))
         load_dy(0, 0)
@@ -388,30 +388,46 @@ def tile_list_embg_dl_mulP_kernel(tc, dy, w4_words, w4_scales, wd, d, wgo, offs,
         for s in (0, 1):
             for k in range(len(shares)):
                 round_share(s, k)
-        on_scalar(out=shares[0][:, :, 1, WHOLE:, 0], in_=share_of(2, 0)[:, :, WHOLE:])
-        round_share(2, 1)
-        on_scalar(out=shares[0][:, :, 1, :WHOLE, :], in_=share_of(2, 0)[:, :, :WHOLE].unsqueeze(3).to_broadcast([P, 2, WHOLE, 2]))
         halves = [cols(h, QUARTER // 2) for h in range(2)]
-        for c in (0, 1):
-            round_quarter(on_vector, LAST, c)
+        ahead, behind = halves
+
+        def both_halves(c, part):
+            width = part.stop - part.start
+            on_scalar(out=shares[0][:, c, 1, part, :], in_=share_of(2, 0)[:, c, part].unsqueeze(2).to_broadcast([P, width, 2]))
+
+        both_halves(0, ahead)
+        for c, start in enumerate((behind.start, 0)):
+            part = slice(start, QUARTER - WHOLE)
+            on_scalar(out=shares[0][:, c, 1, part, 0], in_=share_of(2, 0)[:, c, part])
+        round_share(2, 1)
+        on_scalar(
+            out=shares[0][:, :, 1, QUARTER - WHOLE :, :],
+            in_=share_of(2, 0)[:, :, QUARTER - WHOLE :].unsqueeze(3).to_broadcast([P, 2, WHOLE, 2]),
+        )
+        join(on_scalar, 0, ahead)
+        on_vector(out=shares[0][:, 0, 1, behind, 1], in_=window[LAST][:, behind])
+        round_quarter(on_vector, LAST, 1)
+        on_vector(out=out_grouped[0][:, ahead, LAST], in_=window[LAST][:, ahead])
         for c in (2, 3):
             round_quarter(on_scalar, LAST, c)
         join(on_scalar, 2)
-        for part in halves:
+        ends = [ahead, cols(2, QUARTER // 4), cols(3, QUARTER // 4)]
+        for part in ends:
             join(on_scalar, 3, part)
-        for part in halves:
-            join(on_vector, 0, part)
-        for part in halves:
-            quantize_out(0, part)
-            join(on_vector, 1, part)
+        join(on_vector, 0, behind)
+        quantize_out(0, ahead)
+        join(on_vector, 1, ahead)
+        quantize_out(0, behind)
+        join(on_vector, 1, behind)
         store_codes(0)
         for c in (1, 2):
             for part in halves:
                 quantize_out(c, part)
             store_codes(c)
-        for part in halves:
+        for part in ends:
             quantize_out(3, part)
-            store_codes(3, part)
+        store_codes(3, cols(0, QUARTER // 4, 3))
+        store_codes(3, ends[2])
         for q in range(QUADRANTS):
             queue = nc.scalar if q % 2 == 0 else nc.sync
             queue.dma_start(

@@ -72,6 +72,7 @@ def tile_list_embg_dl_mulP_kernel(tc, dy, w4_words, w4_scales, wd, d, wgo, offs,
         place_of = {
             "dy_raw2_1": row // 2, "rows0_1": 0, "dy_grouped3_0": row, "by_token1_1": 3 * row,
             "dy_raw3_1": 6 * row, "by_token2_1": 5 * row, "by_token1_3": 7 * row, "by_token2_3": 8 * row, "rows0_2": 9 * row,
+            "dy_raw1_0": 27 * row, "by_token0_2": 27 * row, "dy_codes1_0": 27 * row, "dy_grouped1_1": 28 * row,
             "pairs0": 11 * row, "by_token3_2": 18 * row, "pairs1": 19 * row,
         }
 
@@ -137,10 +138,10 @@ def tile_list_embg_dl_mulP_kernel(tc, dy, w4_words, w4_scales, wd, d, wgo, offs,
         for h in range(2):
             nc.sync.dma_start(out=wd_late[h][:], in_=wd_rows[1][:, cols(h, 2), :])
         nc.sync.dma_start(out=wgo_wide[0][:], in_=wgo[:, cols(0)])
-        nc.sync.dma_start(offsets[:], offs)
         load_d(0, 1, 0, 1)
-        load_dy(1, 0)
         load_d(1, 1, 0, 1)
+        nc.sync.dma_start(offsets[:], offs)
+        load_dy(1, 0)
         load_dy(1, 1)
         load_d(2, 2, 0, 1)
         load_dy(2, 0)
@@ -214,15 +215,15 @@ def tile_list_embg_dl_mulP_kernel(tc, dy, w4_words, w4_scales, wd, d, wgo, offs,
 
         by_token = {}
 
-        def weigh_tokens(sums, first_window, count, c):
-            weighed = tile(f"by_token{c}_{first_window}", [P, BLOCKS, count, P], F32)
+        def weigh_tokens(sums, first_window, count, c, into=None):
+            if into is None:
+                weighed = tile(f"by_token{c}_{first_window}", [P, BLOCKS, count * P], F32)
+                into = [weighed[:, b, :] for b in range(BLOCKS)]
             for b in range(BLOCKS):
                 block = BLOCKS * c + b
-                nc.scalar.activation(
-                    out=weighed[:, b].rearrange("j s m -> j (s m)"), in_=sums[:, b, :], func=COPY, scale=wgo_cols[:, block : block + 1]
-                )
+                nc.scalar.activation(out=into[b], in_=sums[:, b, :], func=COPY, scale=wgo_cols[:, block : block + 1])
                 for s in range(count):
-                    by_token[block, first_window + s] = weighed[:, b, s, :]
+                    by_token[block, first_window + s] = into[b][:, cols(s, P)]
 
         def weigh_rows(sums, s, c):
             rows = tile(f"rows{s}_{c}", [P, CHUNK], F32)
@@ -235,6 +236,11 @@ def tile_list_embg_dl_mulP_kernel(tc, dy, w4_words, w4_scales, wd, d, wgo, offs,
                 for b in range(BLOCKS):
                     nc.tensor.transpose(turned[:, cols(BLOCKS * k + b, P)], by_token[BLOCKS * c + b, s], ident[:])
             return turned
+
+        def weigh_d(s):
+            weighed = tile(f"d_weighed{s}", [P, CHUNK], F32)
+            nc.vector.tensor_tensor(weighed[:], d_part[s, 0][0], wgo_wide[0][:], MULT)
+            d_part[s, 0] = (weighed[:], 0)
 
         def scatter(s, first_chunk, chunks, rows):
             entries = offsets[:, cols(first_chunk, CHUNK // LIST_ROWS, chunks)]
@@ -291,14 +297,20 @@ def tile_list_embg_dl_mulP_kernel(tc, dy, w4_words, w4_scales, wd, d, wgo, offs,
                 multiply_rows(leads[s], s, 0, steps)
         sums = token_sums(2, 2, 0, 2)
         multiply_tokens(sums, 2, 2, 0, every, order=one_early)
-        lead_rows = [weigh_rows(leads[s], s, 0) for s in range(LEAD)]
         for s in range(LEAD):
-            scatter(s, 0, 1, lead_rows[s][:])
-        weigh_tokens(sums, 2, 2, 0)
+            weigh_d(s)
+        for s in range(LEAD):
+            place(s, 0, 1, leads[s])
+        grouped = group_dy(1, 0)
+        second = tile("dy_grouped1_1", [P, CHUNK, PACK], BF16)
+        own = tile("by_token0_2", [P, 2 * P], F32)
+        weigh_tokens(sums, 2, 2, 0, into=[flat(second[:, cols(1, P), :]).bitcast(F32), own[:]])
         turned = [turn([(2, 0)], 4), turn([(3, 0)], 5)]
-        quantize_dy(1, 0, group_dy(1, 0, behind="dy_codes0_1"))
+        quantize_dy(1, 0, grouped)
+        interleave(on_scalar, second[:, cols(0, P), :], dy_raw[1][1][:, :, cols(0, P)])
         place(2, 0, 1, turned[0])
-        quantize_dy(1, 1, group_dy(1, 1))
+        interleave(on_scalar, second[:, cols(1, P), :], dy_raw[1][1][:, :, cols(1, P)])
+        quantize_dy(1, 1, second)
         place(3, 0, 1, turned[1], behind="dy_raw1_1")
 
         lead = bank("lead_second", [P, CHUNK], 3)

@@ -147,12 +147,12 @@ def tile_list_embg_dl_mulP_kernel(tc, dy, w4_words, w4_scales, wd, d, wgo, offs,
         load_dy(2, 0)
         load_dy(2, 1)
         nc.sync.dma_start(out=wgo_wide[1][:], in_=wgo[:, cols(1)])
-        load_d(0, 1, 1, 1)
+        load_d(0, 2, 1, 1)
         load_dy(3, 0)
-        load_d(1, 2, 1, 1)
         load_dy(3, 1)
-        load_d(0, LAST, 2, 2)
-        load_d(LAST, 1, 1, 3)
+        load_d(0, 1, 2, 2)
+        load_d(2, 2, 1, 3)
+        load_d(1, 1, 2, 2)
 
         def quantize_wd(a, first, count):
             part = cols(first, P, count)

@@ -441,8 +441,7 @@ def tile_list_embg_dl_mulP_kernel(tc, dy, w4_words, w4_scales, wd, d, wgo, offs,
         store_codes(3, cols(0, QUARTER // 4, 3))
         store_codes(3, ends[2])
         for q in range(QUADRANTS):
-            queue = nc.scalar if q % 2 == 0 else nc.sync
-            queue.dma_start(
+            nc.sync.dma_start(
                 out=out_2[0][cols(q, SCALE_ROWS), :].rearrange("r (c n) -> c r n", c=QUARTERS).bitcast(I32),
                 in_=out_plane[QUADRANT * q : QUADRANT * q + SCALE_ROWS * QUARTERS, :].bitcast(I32),
             )

@@ -438,8 +438,7 @@ def tile_list_embg_dl_mulP_kernel(tc, dy, w4_words, w4_scales, wd, d, wgo, offs,
             store_codes(c)
         for part in ends:
             quantize_out(3, part)
-        store_codes(3, cols(0, QUARTER // 4, 3))
-        store_codes(3, ends[2])
+        store_codes(3)
         for q in range(QUADRANTS):
             nc.sync.dma_start(
                 out=out_2[0][cols(q, SCALE_ROWS), :].rearrange("r (c n) -> c r n", c=QUARTERS).bitcast(I32),

from contextlib import ExitStack

import concourse.mybir as mybir
from concourse.masks import make_identity

K, N, T, J = 1024, 512, 2048, 1024
FLOPS = 2 * 2 * K * N * J

F32 = mybir.dt.float32
BF16 = mybir.dt.bfloat16
I32 = mybir.dt.int32
U32 = mybir.dt.uint32
U16 = mybir.dt.uint16
U8 = mybir.dt.uint8
E4M3 = mybir.dt.float8_e4m3fn_x4
E5M2 = mybir.dt.float8_e5m2_x4
E2M1 = mybir.dt.float4_e2m1fn_x4
MULT = mybir.AluOpType.mult
COPY = mybir.ActivationFunctionType.Copy

P = 128
PACK = 4
PASSES = K // (P * PACK)
CHUNK = 256
CHUNKS = J // CHUNK
BLOCKS = CHUNK // P
WINDOWS = N // P
LAST = WINDOWS - 1
LIST_ROWS = 16
QUADRANTS = 4
QUADRANT = P // QUADRANTS
SCALE_ROWS = 4
QUARTERS = 4
QUARTER = T // QUARTERS
RUN = 4
WHOLE = 16
LEAD = 2


def interleave(copy, grouped, rows):
    copy(
        out=grouped.rearrange("p (c f) i -> p c i f", f=RUN),
        in_=rows.rearrange("p i (c f) -> p c i f", f=RUN),
    )


def deal(copy, grouped, rows, part):
    copy(
        out=grouped.rearrange("p s m i -> p m i s"),
        in_=rows.rearrange("p i (m s) -> p m i s", s=WINDOWS)[:, :, :, part],
    )


def flat(grouped):
    return grouped.rearrange("p c i -> p (c i)")


def cols(index, width=CHUNK, count=1):
    return slice(index * width, (index + count) * width)


def tile_list_embg_dl_mulP_kernel(tc, dy, w4_words, w4_scales, wd, d, wgo, offs, out_0, out_1, out_2):
    nc = tc.nc
    on_vector = nc.vector.tensor_copy
    on_scalar = nc.scalar.copy
    with ExitStack() as ctx:
        keep = ctx.enter_context(tc.tile_pool(name="keep", bufs=1))
        psum = ctx.enter_context(tc.psum_pool(name="psum", bufs=1))

        reuse = ctx.enter_context(tc.tile_pool(name="reuse", bufs=1))
        row = CHUNK * 4
        place_of = {
            "dy_raw2_1": row // 2, "rows0_1": 0, "dy_grouped3_0": row, "by_token1_1": 3 * row,
            "dy_raw3_1": 6 * row, "by_token2_1": 5 * row, "by_token1_3": 7 * row, "by_token2_3": 8 * row, "rows0_2": 9 * row,
            "dy_raw1_0": 27 * row, "by_token0_2": 27 * row, "dy_codes1_0": 27 * row, "dy_grouped1_1": 28 * row,
            "pairs0": 11 * row, "by_token3_2": 18 * row, "pairs1": 19 * row,
        }

        def tile(name, shape, dtype, behind=None):
            if name in place_of:
                return reuse.tile(shape, dtype, name=name, align_bytes=64, offset=place_of[name])
            return keep.tile(shape, dtype, name=name, tag=behind or name, align_bytes=64)

        def bank(name, shape, number):
            return psum.tile(shape, F32, name=name, tag=f"bank{number}")

        offsets = keep.tile([P, J // LIST_ROWS], U16, name="offsets")
        w4_codes_raw = tile("w4_codes_raw", [P, PASSES, 2 * N], U8)
        w4_plane_raw = tile("w4_plane_raw", [P, PASSES, N], U8)
        w4_codes = [tile(f"w4_codes{a}", [P, 2 * N], U8) for a in range(PASSES)]
        w4_plane = tile("w4_plane", [P, PASSES, N], U8)
        wgo_rows = tile("wgo_rows", [P, P], F32)
        wgo_wide = [tile(f"wgo_wide{c}", [P, CHUNK], F32) for c in range(2)]
        ident = tile("ident", [P, P], F32)
        wd_raw = tile("wd_raw", [P, PACK, N], F32)
        wd_late = [tile(f"wd_late{h}", [P, PACK // 2, N], F32) for h in range(2)]
        wd_grouped = [[tile(f"wd_grouped{a}_{h}", [P, LEAD, P, PACK], BF16) for h in range(WINDOWS // LEAD)] for a in range(PASSES)]
        wd_codes = [tile(f"wd_codes{a}", [P, N], U32) for a in range(PASSES)]
        wd_plane = [tile(f"wd_plane{a}", [P, N], U8) for a in range(PASSES)]
        dy_raw = [[tile(f"dy_raw{c}_{a}", [P, PACK, CHUNK], F32) for a in range(PASSES)] for c in range(CHUNKS)]
        dy_plane = [[tile(f"dy_plane{c}_{a}", [P, CHUNK], U8) for a in range(PASSES)] for c in range(CHUNKS)]
        dy_codes = {}
        window = [tile(f"window{s}", [P, T], F32) for s in range(LAST)]

        dy_rows = dy.rearrange("(a p i) j -> a p i j", a=PASSES, i=PACK)
        wd_rows = wd.rearrange("(a p i) n -> a p i n", a=PASSES, i=PACK)
        d_rows = d.rearrange("(p s) j -> p s j", s=WINDOWS)
        out_rows = out_0.rearrange("(p s) c -> p s c", s=WINDOWS)

        d_part = {}

        def load_dy(c, a):
            nc.sync.dma_start(out=dy_raw[c][a][:], in_=dy_rows[a][:, :, cols(c)])

        def load_d(first_window, windows, first_chunk, chunks):
            piece = tile(f"d{first_window}_{first_chunk}", [P, windows, chunks * CHUNK], F32)
            nc.sync.dma_start(out=piece[:], in_=d_rows[:, cols(first_window, 1, windows), cols(first_chunk, count=chunks)])
            for s in range(windows):
                for c in range(chunks):
                    d_part[first_window + s, first_chunk + c] = (piece[:, s, :], first_chunk)

        nc.gpsimd.memset(w4_plane_raw[:].rearrange("p a n -> p (a n)").bitcast(I32), 0)
        nc.gpsimd.memset(wgo_rows[:], 0.0)
        make_identity(nc, ident[:])
        for s in range(LAST):
            (nc.vector if s < 2 else nc.gpsimd).memset(window[s][:], 0.0)

        nc.sync.dma_start(out=w4_codes_raw[:].bitcast(I32), in_=w4_words.rearrange("a p c -> p a c").bitcast(I32))
        nc.sync.dma_start(out=wd_raw[:], in_=wd_rows[0])
        for r in range(SCALE_ROWS):
            nc.sync.dma_start(
                out=w4_plane_raw[r:P:QUADRANT].bitcast(I32),
                in_=w4_scales.rearrange("a (q r) n -> r q a n", r=SCALE_ROWS)[r].bitcast(I32),
            )
        nc.sync.dma_start(out=wgo_rows[0 : J // P, :], in_=wgo[0:1, :].rearrange("o (b m) -> (o b) m", m=P))
        load_dy(0, 0)
        load_dy(0, 1)
        for h in range(2):
            nc.sync.dma_start(out=wd_late[h][:], in_=wd_rows[1][:, cols(h, 2), :])
        nc.sync.dma_start(out=wgo_wide[0][:], in_=wgo[:, cols(0)])
        load_d(0, 1, 0, 1)
        load_d(1, 1, 0, 1)
        nc.sync.dma_start(offsets[:], offs)
        load_dy(1, 0)
        load_dy(1, 1)
        load_d(2, 2, 0, 1)
        load_dy(2, 0)
        load_dy(2, 1)
        nc.sync.dma_start(out=wgo_wide[1][:], in_=wgo[:, cols(1)])
        load_d(0, 2, 1, 1)
        load_dy(3, 0)
        load_dy(3, 1)
        load_d(0, 1, 2, 2)
        load_d(2, 2, 1, 3)
        load_d(1, 1, 2, 2)

        def quantize_wd(a, first, count):
            part = cols(first, P, count)
            nc.vector.quantize_mx(
                out=wd_codes[a][:, part].bitcast(E4M3),
                scales=wd_plane[a][:, part],
                in_=wd_grouped[a][first // LEAD][:, cols(first % LEAD, 1, count)].rearrange("p s m i -> p (s m i)"),
            )

        def group_dy(c, a, behind=None):
            grouped = tile(f"dy_grouped{c}_{a}", [P, CHUNK, PACK], BF16, behind)
            interleave(on_scalar, grouped[:], dy_raw[c][a][:])
            return grouped

        def quantize_dy(c, a, grouped, behind=None):
            dy_codes[c, a] = tile(f"dy_codes{c}_{a}", [P, CHUNK], U32, behind)
            nc.vector.quantize_mx(out=dy_codes[c, a][:].bitcast(E5M2), scales=dy_plane[c][a][:], in_=flat(grouped[:]))

        def w4_columns(a):
            return lambda s, count: w4_codes[a][:, 2 * P * s : 2 * P * (s + count)].bitcast(E2M1)

        def wd_columns(a):
            return lambda s, count: wd_codes[a][:, P * s : P * (s + count)].bitcast(E4M3)

        w4_pass = [(w4_columns(a), w4_plane[:, a, :], a) for a in range(PASSES)]
        wd_pass = [(wd_columns(a), wd_plane[a][:], a) for a in range(PASSES)]
        by_pass = [w4_pass[0], wd_pass[0], w4_pass[1], wd_pass[1]]
        one_early = [wd_pass[0], wd_pass[1], w4_pass[0], w4_pass[1]]
        early, late, every = range(2), range(2, 4), range(4)

        def multiply_rows(sums, s, c, steps):
            for step in steps:
                codes, plane, a = by_pass[step]
                nc.tensor.matmul_mx(
                    out=sums[:],
                    lhsT=codes(s, 1),
                    lhsT_scale=plane[:, cols(s, P)],
                    rhs=dy_codes[c, a][:].bitcast(E5M2),
                    rhs_scale=dy_plane[c][a][:],
                    start=(step == 0),
                    stop=(step == len(by_pass) - 1),
                )

        def multiply_tokens(sums, first_window, count, c, steps, order=by_pass):
            for step in steps:
                codes, plane, a = order[step]
                for b in range(BLOCKS):
                    nc.tensor.matmul_mx(
                        out=sums[:, b, :],
                        lhsT=dy_codes[c, a][:, cols(b, P)].bitcast(E5M2),
                        lhsT_scale=dy_plane[c][a][:, cols(b, P)],
                        rhs=codes(first_window, count),
                        rhs_scale=plane[:, cols(first_window, P, count)],
                        start=(step == 0 and b == 0),
                        stop=(step == len(order) - 1 and b == BLOCKS - 1),
                    )

        def token_sums(first_window, count, c, number):
            return bank(f"sums{c}_{first_window}", [P, BLOCKS, count * P], number)

        by_token = {}

        def weigh_tokens(sums, first_window, count, c, into=None):
            if into is None:
                weighed = tile(f"by_token{c}_{first_window}", [P, BLOCKS, count * P], F32)
                into = [weighed[:, b, :] for b in range(BLOCKS)]
            for b in range(BLOCKS):
                block = BLOCKS * c + b
                nc.scalar.activation(out=into[b], in_=sums[:, b, :], func=COPY, scale=wgo_cols[:, block : block + 1])
                for s in range(count):
                    by_token[block, first_window + s] = into[b][:, cols(s, P)]

        def weigh_rows(sums, s, c):
            rows = tile(f"rows{s}_{c}", [P, CHUNK], F32)
            nc.vector.tensor_tensor(rows[:], sums[:], wgo_wide[c][:], MULT)
            return rows

        def turn(pieces, number):
            turned = bank(f"turned{pieces[0][0]}_{pieces[0][1]}", [P, len(pieces) * CHUNK], number)
            for k, (s, c) in enumerate(pieces):
                for b in range(BLOCKS):
                    nc.tensor.transpose(turned[:, cols(BLOCKS * k + b, P)], by_token[BLOCKS * c + b, s], ident[:])
            return turned

        def weigh_d(s):
            weighed = tile(f"d_weighed{s}", [P, CHUNK], F32)
            nc.vector.tensor_tensor(weighed[:], d_part[s, 0][0], wgo_wide[0][:], MULT)
            d_part[s, 0] = (weighed[:], 0)

        def scatter(s, first_chunk, chunks, rows):
            entries = offsets[:, cols(first_chunk, CHUNK // LIST_ROWS, chunks)]
            row, origin = d_part[s, first_chunk]
            nc.vector.tensor_tensor(window[s][:].indirect(entries), rows, row[:, cols(first_chunk - origin, count=chunks)], MULT)

        def place(s, first_chunk, chunks, turned, behind=None):
            rows = tile(f"rows{s}_{first_chunk}", [P, chunks * CHUNK], F32, behind)
            on_scalar(out=rows[:], in_=turned[:])
            scatter(s, first_chunk, chunks, rows[:])

        def store_window(s):
            nc.sync.dma_start(out=out_rows[:, s, :], in_=window[s][:])

        def deal_w4(a):
            on_scalar(
                out=w4_codes[a][:].bitcast(U16).rearrange("p (s m) -> p s m", s=WINDOWS),
                in_=w4_codes_raw[:, a, :].bitcast(U16).rearrange("p (m s) -> p s m", s=WINDOWS),
            )

        for a in range(PASSES):
            deal_w4(a)
        for h, copy in enumerate((on_vector, on_scalar)):
            deal(copy, wd_grouped[0][h][:], wd_raw[:], cols(h, LEAD))
        on_vector(
            out=w4_plane[:].rearrange("p a (s m) -> p a s m", s=WINDOWS),
            in_=w4_plane_raw[:].rearrange("p a (m s) -> p a s m", s=WINDOWS),
        )
        quantize_wd(0, 0, LEAD)
        quantize_wd(0, LEAD, LEAD)
        for a in range(PASSES):
            quantize_dy(0, a, group_dy(0, a))
        for h, copy in enumerate((on_vector, on_scalar)):
            deal(copy, wd_grouped[1][h][:, :, :, cols(0, 2)], wd_late[0][:], cols(h, LEAD))
        for s in range(LEAD):
            on_vector(
                out=wd_grouped[1][0][:, s, :, cols(1, 2)],
                in_=wd_late[1][:].rearrange("p i (m s) -> p s m i", s=WINDOWS)[:, s],
            )
        deal(on_scalar, wd_grouped[1][1][:, :, :, cols(1, 2)], wd_late[1][:], cols(1, LEAD))
        wgo_bank = bank("wgo_bank", [P, P], 7)
        nc.tensor.transpose(wgo_bank[:], wgo_rows[:], ident[:])
        wgo_cols = tile("wgo_cols", [P, J // P], F32, behind="wd_late1")
        on_scalar(out=wgo_cols[:], in_=wgo_bank[:, 0 : J // P])
        quantize_wd(1, 0, 1)
        quantize_wd(1, 1, 1)
        quantize_wd(1, LEAD, LEAD)
        window.append(tile("window_last", [P, T], F32, behind="wd_grouped1_1"))
        nc.gpsimd.memset(window[LAST][:], 0.0)

        leads = [bank(f"lead{s}", [P, CHUNK], s) for s in range(LEAD)]
        for steps in (range(2), range(2, 3), range(3, 4)):
            for s in range(LEAD):
                multiply_rows(leads[s], s, 0, steps)
        sums = token_sums(2, 2, 0, 2)
        multiply_tokens(sums, 2, 2, 0, every, order=one_early)
        for s in range(LEAD):
            weigh_d(s)
        for s in range(LEAD):
            place(s, 0, 1, leads[s])
        grouped = group_dy(1, 0)
        second = tile("dy_grouped1_1", [P, CHUNK, PACK], BF16)
        own = tile("by_token0_2", [P, 2 * P], F32)
        weigh_tokens(sums, 2, 2, 0, into=[flat(second[:, cols(1, P), :]).bitcast(F32), own[:]])
        turned = [turn([(2, 0)], 4), turn([(3, 0)], 5)]
        quantize_dy(1, 0, grouped)
        interleave(on_scalar, second[:, cols(0, P), :], dy_raw[1][1][:, :, cols(0, P)])
        place(2, 0, 1, turned[0])
        interleave(on_scalar, second[:, cols(1, P), :], dy_raw[1][1][:, :, cols(1, P)])
        quantize_dy(1, 1, second)
        place(3, 0, 1, turned[1], behind="dy_raw1_1")

        lead = bank("lead_second", [P, CHUNK], 3)
        middle, last = token_sums(1, 2, 1, 0), token_sums(LAST, 1, 1, 1)
        for steps in (early, late):
            multiply_rows(lead, 0, 1, steps)
            multiply_tokens(middle, 1, 2, 1, steps)
        multiply_tokens(last, LAST, 1, 1, every)
        quantize_dy(2, 0, group_dy(2, 0))
        grouped = group_dy(2, 1)
        rows = weigh_rows(lead, 0, 1)
        quantize_dy(2, 1, grouped)
        scatter(0, 1, 1, rows[:])
        weigh_tokens(middle, 1, 2, 1)
        turned = turn([(1, 1)], 2)
        quantize_dy(3, 0, group_dy(3, 0))
        place(1, 1, 1, turned)

        first, middle = token_sums(0, 1, 2, 0), token_sums(1, 2, 2, 2)
        multiply_tokens(first, 0, 1, 2, every)
        multiply_tokens(middle, 1, 2, 2, every)
        weigh_tokens(first, 0, 1, 2)
        turned = turn([(2, 1), (0, 2)], 3)
        last_second = token_sums(LAST, 1, 2, 0)
        multiply_tokens(last_second, LAST, 1, 2, every)
        quantize_dy(3, 1, group_dy(3, 1, behind="dy_raw3_0"))
        groups = ((0, 1), (1, 1), (2, 2))
        sums = [token_sums(*group, 3, 4 + g) for g, group in enumerate(groups)]
        for steps in (early, late):
            for g, group in enumerate(groups):
                multiply_tokens(sums[g], *group, 3, steps)
        rows = tile("rows0_2", [P, 2 * CHUNK], F32)
        on_scalar(out=rows[:], in_=turned[:])
        scatter(0, 2, 1, rows[:, cols(1)])
        scatter(2, 1, 1, rows[:, cols(0)])
        weigh_tokens(middle, 1, 2, 2)
        weigh_tokens(last, LAST, 1, 1)
        weigh_tokens(last_second, LAST, 1, 2)
        weigh_tokens(sums[0], 0, 1, 3)
        place(0, 3, 1, turn([(0, 3)], 7))
        store_window(0)
        weigh_tokens(sums[1], 1, 1, 3)
        place(1, 2, 2, turn([(1, 2), (1, 3)], 1))
        store_window(1)
        last_rows = tile("last_rows", [P, 3 * CHUNK], F32)
        on_scalar(out=last_rows[:, cols(0, count=2)], in_=turn([(LAST, 1), (LAST, 2)], 0)[:])
        weigh_tokens(sums[2], 2, 2, 3)
        place(2, 2, 2, turn([(2, 2), (2, 3)], 2))
        store_window(2)
        on_scalar(out=last_rows[:, cols(2)], in_=turn([(LAST, 3)], 3)[:])
        scatter(LAST, 1, 3, last_rows[:])
        store_window(LAST)

        out_plane = tile("out_plane", [P, QUARTER], U8)
        shares = [tile(f"pairs{k}", [P, 2, 2, QUARTER, 2], BF16) for k in range(2)]
        out_grouped = [keep.tile([P, QUARTER, PACK], BF16, name=f"out_grouped{c}", align_bytes=64) for c in range(QUARTERS)]
        out_codes = [keep.tile([P, QUARTER], U32, name=f"out_codes{c}", align_bytes=64) for c in range(QUARTERS)]

        def share_of(s, k):
            return window[s][:, cols(k, T // 2)].rearrange("p (g c) -> p g c", g=2)

        def round_share(s, k):
            on_scalar(out=shares[k][:, :, s // 2, :, s % 2], in_=share_of(s, k))

        def round_quarter(copy, s, c):
            copy(out=shares[c // 2][:, c % 2][:, s // 2, :, s % 2], in_=window[s][:, cols(c, QUARTER)])

        def join(copy, c, part=slice(0, QUARTER)):
            pairs = shares[c // 2][:, c % 2].rearrange("p h c e -> p (h c e)").bitcast(F32).rearrange("p (h c) -> p h c", h=2)
            words = flat(out_grouped[c][:, part, :]).bitcast(F32)
            copy(
                out=words.rearrange("p (c f h) -> p c h f", h=2, f=RUN),
                in_=pairs[:, :, part].rearrange("p h (c f) -> p c h f", f=RUN),
            )

        def quantize_out(c, part):
            nc.vector.quantize_mx(
                out=out_codes[c][:, part].bitcast(E4M3), scales=out_plane[SCALE_ROWS * c :, part], in_=flat(out_grouped[c][:, part, :])
            )

        def store_codes(c, part=slice(0, QUARTER)):
            nc.sync.dma_start(
                out=out_1[0][:, cols(c, QUARTER), :][:, part, :].rearrange("p c i -> p (c i)").bitcast(I32),
                in_=out_codes[c][:, part].bitcast(I32),
            )

        for s in (0, 1):
            for k in range(len(shares)):
                round_share(s, k)
        halves = [cols(h, QUARTER // 2) for h in range(2)]
        ahead, behind = halves

        def both_halves(c, part):
            width = part.stop - part.start
            on_scalar(out=shares[0][:, c, 1, part, :], in_=share_of(2, 0)[:, c, part].unsqueeze(2).to_broadcast([P, width, 2]))

        both_halves(0, ahead)
        for c, start in enumerate((behind.start, 0)):
            part = slice(start, QUARTER - WHOLE)
            on_scalar(out=shares[0][:, c, 1, part, 0], in_=share_of(2, 0)[:, c, part])
        round_share(2, 1)
        on_scalar(
            out=shares[0][:, :, 1, QUARTER - WHOLE :, :],
            in_=share_of(2, 0)[:, :, QUARTER - WHOLE :].unsqueeze(3).to_broadcast([P, 2, WHOLE, 2]),
        )
        join(on_scalar, 0, ahead)
        on_vector(out=shares[0][:, 0, 1, behind, 1], in_=window[LAST][:, behind])
        round_quarter(on_vector, LAST, 1)
        on_vector(out=out_grouped[0][:, ahead, LAST], in_=window[LAST][:, ahead])
        for c in (2, 3):
            round_quarter(on_scalar, LAST, c)
        join(on_scalar, 2)
        ends = [ahead, cols(2, QUARTER // 4), cols(3, QUARTER // 4)]
        for part in ends:
            join(on_scalar, 3, part)
        join(on_vector, 0, behind)
        quantize_out(0, ahead)
        join(on_vector, 1, ahead)
        quantize_out(0, behind)
        join(on_vector, 1, behind)
        store_codes(0)
        for c in (1, 2):
            for part in halves:
                quantize_out(c, part)
            store_codes(c)
        for part in ends:
            quantize_out(3, part)
        store_codes(3)
        for q in range(QUADRANTS):
            nc.sync.dma_start(
                out=out_2[0][cols(q, SCALE_ROWS), :].rearrange("r (c n) -> c r n", c=QUARTERS).bitcast(I32),
                in_=out_plane[QUADRANT * q : QUADRANT * q + SCALE_ROWS * QUARTERS, :].bitcast(I32),
            )
